import numpy as np
import ml_dtypes


def mxq(x, axis, fmt="e4m3"):
    dtype, down = {"e4m3": (ml_dtypes.float8_e4m3fn, 7), "e5m2": (ml_dtypes.float8_e5m2, 14)}[fmt]
    v = np.moveaxis(np.asarray(x, np.float32).astype(ml_dtypes.bfloat16).astype(np.float64), axis, -1)
    blocks = v.reshape(v.shape[:-1] + (-1, 32))
    amax = np.abs(blocks).max(-1, keepdims=True)
    byte = np.maximum(np.where(amax > 0, np.frexp(amax)[1] - 1 + 127, 0) - down, 1)
    scale = np.exp2(byte - 127.0)
    codes = (blocks / scale).astype(np.float32).astype(dtype).astype(np.float64)
    return np.moveaxis((codes * scale).reshape(v.shape), -1, axis)


WIDE = False


def mx_kscale(k):
    if not WIDE:
        return np.ones(k)
    levels = np.array([10, -10, 5, -5, 0])
    if k % 512:
        return np.exp2(np.random.permutation(np.resize(levels, k // 32))).repeat(32)
    a = np.empty((k // 512, 16))
    for p in range(k // 512):
        a[p, :8] = np.random.permutation(np.resize(levels, 8))
        for g in range(8):
            far = levels[np.abs(levels - a[p, g]) >= 10]
            a[p, g + 8] = far[np.random.randint(len(far))]
    return np.exp2(a.ravel()).repeat(32)


def f64(x):
    return np.asarray(x).astype(np.float64)


def striped(idx):
    return np.tile(np.asarray(idx).reshape(-1, 16).T, (8, 1)).astype(np.uint16)


def unstriped(offs):
    return offs[:16].T.reshape(-1).astype(np.int64)


E2M1 = np.array([0.0, 0.5, 1.0, 1.5, 2.0, 3.0, 4.0, 6.0, -0.0, -0.5, -1.0, -1.5, -2.0, -3.0, -4.0, -6.0])


def pack_weight(w, fmt):
    k, n = w.shape
    w = f64(np.asarray(w, np.float32).astype(ml_dtypes.bfloat16)).reshape(k // 32, 32, n)
    amax = np.abs(w).max(1)
    if fmt == "e4m3":
        byte = np.frexp(amax)[1] - 1 + 127 - 7
    else:
        mant, ex = np.frexp(amax / 6.0)
        byte = np.where(mant > 0.5, ex, ex - 1) + 127
    byte = np.clip(np.where(amax > 0, byte, 1), 1, 254)
    scaled = (w * np.exp2(127.0 - byte)[:, None, :]).reshape(k, n).astype(np.float32)
    by_word = np.ascontiguousarray(scaled.reshape(k // 512, 128, 4, n).transpose(0, 1, 3, 2))
    if fmt == "e4m3":
        words = by_word.astype(ml_dtypes.float8_e4m3fn).view(np.uint8)
    else:
        c = by_word.astype(ml_dtypes.float4_e2m1fn).view(np.uint8) & 0xF
        words = (c[..., 0::2] | (c[..., 1::2] << 4)).reshape(k // 512, 128, 2 * n)
    return np.ascontiguousarray(words), np.ascontiguousarray(byte.astype(np.uint8).reshape(k // 512, 16, n))


def unpack_weight(words, scales, fmt):
    g, _, n = scales.shape
    words = np.ascontiguousarray(words).reshape(g, 128, n, -1)
    if fmt == "e4m3":
        vals = words.view(ml_dtypes.float8_e4m3fn).astype(np.float64)
    else:
        nib = np.empty((g, 128, n, 4), np.uint8)
        nib[..., 0::2] = words & 0xF
        nib[..., 1::2] = words >> 4
        vals = E2M1[nib]
    vals = vals * np.repeat(np.exp2(scales.astype(np.float64) - 127.0), 8, axis=1)[..., None]
    return vals.transpose(0, 1, 3, 2).reshape(g * 512, n)


B, N, T, D, DV, NQ = 1, 1536, 4096, 1024, 256, 128
PAGE = 512


def setup_inputs():
    n = np.random.standard_normal
    pages = np.random.permutation(T // PAGE)[:B * N // PAGE]
    idx = (pages[:, None] * PAGE + np.arange(PAGE)[None, :]).reshape(-1)
    s = mx_kscale(D)[:, None]
    u = np.ones(T)
    u[idx] = mx_kscale(B * N)
    r = np.random.uniform(0.5, 2.0, T)
    k = n((D, T)) / s
    v = n((DV, T)) / (u * r)
    kp = pack_weight(k, "e2m1")
    vp = pack_weight(v.T, "e4m3")
    return {
        "qT": (n((B, D, NQ)) * s * (1.00 / np.sqrt(D))).astype(np.float32),
        "k_words": np.ascontiguousarray(kp[0].reshape(D // 1024, 2, 128, T, 2).transpose(0, 2, 3, 1, 4)).reshape(D // 1024, 128, T, 4),
        "k_scales": kp[1],
        "v_words": vp[0],
        "v_scales": vp[1],
        "vs": np.tile(u * r, (128, 1)).astype(np.float32),
        "sink": (2.0 + 3.0 * n((B, NQ, 1))).astype(np.float32),
        "offs": striped(idx),
        "voffs": striped((pages[:, None] * DV + np.arange(DV)[None, :]).reshape(-1)),
    }


def reference(qT, k_words, k_scales, v_words, v_scales, vs, sink, offs, voffs):
    idx = unstriped(offs)
    k = unpack_weight(k_words.reshape(D // 1024, 128, T, 2, 2).transpose(0, 3, 1, 2, 4).reshape(D // 512, 128, 2 * T), k_scales, "e2m1")
    v = unpack_weight(v_words, v_scales, "e4m3")
    v = v.reshape(T // 512, 512, DV)[unstriped(voffs)[::DV] // DV].reshape(B, N, DV)
    pick = lambda x: x[:, idx].reshape(x.shape[0], B, N).transpose(1, 0, 2)
    q = f64(qT)
    score = mxq(q, 1, "e4m3").transpose(0, 2, 1) @ pick(k)
    m = np.maximum(score.max(-1, keepdims=True), f64(sink))
    p = np.exp(score - m)
    total = p.sum(-1, keepdims=True) + np.exp(f64(sink) - m)
    w = p * pick(f64(vs))[:, :1, :]
    y = mxq(w, 2, "e4m3") @ v
    y = y / total
    return y

@@ -1,0 +1,170 @@
+from contextlib import ExitStack
+
+import concourse.mybir as mybir
+from concourse.masks import make_identity
+
+F32 = mybir.dt.float32
+BF16 = mybir.dt.bfloat16
+I32 = mybir.dt.int32
+U32 = mybir.dt.uint32
+U16 = mybir.dt.uint16
+U8 = mybir.dt.uint8
+FP8X4 = mybir.dt.float8_e4m3fn_x4
+FP4X4 = mybir.dt.float4_e2m1fn_x4
+ALU = mybir.AluOpType
+ACT = mybir.ActivationFunctionType
+AXIS = mybir.AxisListType
+
+P = 128
+PACK = 4
+PAGE = 512
+SLOTS, POOL, D, DV, NQ = 1536, 4096, 1024, 256, 128
+PAGES = SLOTS // PAGE
+POOL_PAGES = POOL // PAGE
+PASSES = D // PAGE
+FLOPS = 2 * NQ * SLOTS * (D + DV)
+
+
+def tile_attend_pkv4_sink_kernel(tc, qT, k_words, k_scales, v_words, v_scales, vs, sink, offs, voffs, out):
+    nc = tc.nc
+    with ExitStack() as ctx:
+        lists = ctx.enter_context(tc.tile_pool(name="lists", bufs=1))
+        keep = ctx.enter_context(tc.tile_pool(name="keep", bufs=1))
+        psum = ctx.enter_context(tc.psum_pool(name="psum", bufs=1))
+
+        slot_list = lists.tile([P, SLOTS // 16], U16, name="slot_list")
+        nc.sync.dma_start(slot_list[:], offs)
+        q_raw = keep.tile([P, PASSES, PACK, NQ], F32, name="q_raw")
+        nc.sync.dma_start(q_raw[:], qT[0].rearrange("(g p j) w -> p g j w", g=PASSES, j=PACK))
+        key_pool = keep.tile([P, POOL], I32, name="key_pool")
+        nc.sync.dma_start(key_pool[:], k_words[0].rearrange("p t b -> p (t b)").bitcast(I32))
+        column_list = lists.tile([P, PAGES * DV // 16], U16, name="column_list")
+        nc.sync.dma_start(column_list[:], voffs)
+
+        key_scale_pool = keep.tile([P, POOL], U8, name="key_scale_pool", tag="late_values", align_bytes=64)
+        nc.vector.memset(key_scale_pool[:].bitcast(I32), 0)
+        nc.scalar.dma_start(key_scale_pool[:].bitcast(I32)[0:P:4, :], k_scales.rearrange("o f t -> (o f) t").bitcast(I32))
+        value_scale_pool = keep.tile([P, POOL_PAGES * DV], U8, name="value_scale_pool")
+        token_scale_pool = keep.tile([P, POOL], F32, name="token_scale_pool")
+        nc.vector.memset(token_scale_pool[:], 0.0)
+        nc.vector.memset(value_scale_pool[:].bitcast(I32), 0)
+        key_planes = keep.tile([P, PASSES, SLOTS], U8, name="key_planes", align_bytes=64)
+        nc.vector.memset(key_planes[:].rearrange("p o n -> p (o n)").bitcast(I32), 0)
+
+        zero_col = keep.tile([P, 1], F32, name="zero_col")
+        nc.gpsimd.memset(zero_col[:], 0.0)
+        sink_col = keep.tile([P, 1], F32, name="sink_col")
+        nc.gpsimd.dma_start(sink_col[:], sink[0])
+        ident = keep.tile([P, P], F32, name="ident")
+        make_identity(nc, ident[:])
+        for quad in range(4):
+            nc.gpsimd.dma_start(
+                value_scale_pool[32 * quad : 32 * quad + 4, :].bitcast(I32).rearrange("f (u e) -> f u e", u=POOL_PAGES),
+                v_scales[:, 4 * quad : 4 * quad + 4, :].bitcast(I32).rearrange("u f e -> f u e"),
+            )
+
+        warm = keep.tile([P, 1], F32, name="warm")
+        nc.scalar.activation(warm[:], zero_col[:], ACT.Exp)
+
+        q_grouped = keep.tile([P, PASSES, NQ, PACK], BF16, name="q_grouped", align_bytes=64)
+        nc.scalar.copy(q_grouped[:], q_raw[:].rearrange("p g j w -> p g w j"))
+        nc.scalar.dma_start(token_scale_pool[0:1, :], vs[0:1, :])
+        neg_sink = keep.tile([P, 1], F32, name="neg_sink")
+        nc.scalar.activation(neg_sink[:], sink_col[:], ACT.Copy, scale=-1.0)
+
+        key_scales = keep.tile([P, SLOTS], U8, name="key_scales")
+        nc.vector.tensor_copy(key_scales[:], key_scale_pool[:].indirect(slot_list[:]))
+        for o in range(PASSES):
+            for r in range(4):
+                nc.sync.dma_start(
+                    key_planes[r:P:32, o, :].bitcast(I32),
+                    key_scales[64 * o + 4 * r : 64 * o + 64 : 16, :].bitcast(I32),
+                )
+        value_pool = keep.tile([P, POOL_PAGES * DV], I32, name="value_pool", tag="late_values", align_bytes=64)
+        nc.sync.dma_start(
+            value_pool[:].rearrange("p (u e) -> p u e", u=POOL_PAGES),
+            v_words.rearrange("u p e r -> p u (e r)").bitcast(I32),
+        )
+
+        q_codes = keep.tile([P, PASSES * NQ], U32, name="q_codes", align_bytes=64)
+        q_scales = keep.tile([P, PASSES * NQ], U8, name="q_scales", align_bytes=64)
+        nc.vector.quantize_mx(q_codes[:].bitcast(FP8X4), q_scales[:], q_grouped[:].rearrange("p g w j -> p (g w j)"))
+
+        token_scales = keep.tile([P, SLOTS], F32, name="token_scales")
+        nc.vector.tensor_copy(token_scales[:], token_scale_pool[:].indirect(slot_list[:]))
+        slot_scales = keep.tile([P, PAGES, PACK], F32, name="slot_scales")
+        for u in range(PAGES):
+            turned = psum.tile([P, PACK, NQ], F32, name="turned_scales%d" % u, tag="turned%d" % u)
+            for t in range(PACK):
+                nc.tensor.transpose(turned[:, t, :], token_scales[:, PAGE * u + t : PAGE * (u + 1) : PACK], ident[:])
+            nc.scalar.copy(slot_scales[:, u, :], turned[:, :, 0])
+
+        neg_scores = []
+        neg_max = neg_sink
+        for u in range(PAGES):
+            key_pairs = keep.tile([P, PAGE], U32, name="key_pairs%d" % u)
+            nc.vector.tensor_copy(key_pairs[:], key_pool[:].bitcast(U32).indirect(slot_list[:, 32 * u : 32 * (u + 1)]))
+            keys = keep.tile([P, PASSES, PAGE], U16, name="keys%d" % u, align_bytes=64)
+            nc.vector.tensor_copy(keys[:], key_pairs[:].bitcast(U16).rearrange("p (n o) -> p o n", o=PASSES))
+            scores = psum.tile([NQ, PAGE], F32, name="scores%d" % u)
+            for o in range(PASSES):
+                nc.tensor.matmul_mx(
+                    scores[:],
+                    lhsT=q_codes[:, NQ * o : NQ * (o + 1)].bitcast(FP8X4),
+                    lhsT_scale=q_scales[:, NQ * o : NQ * (o + 1)],
+                    rhs=keys[:, o, :].bitcast(FP4X4),
+                    rhs_scale=key_planes[:, o, PAGE * u : PAGE * (u + 1)],
+                    start=(o == 0),
+                    stop=(o == PASSES - 1),
+                )
+            neg_scores.append((scores, keep.tile([NQ, PACK, P], F32, name="neg_scores%d" % u)))
+        for u in range(PAGES):
+            scores, negated = neg_scores[u]
+            running = keep.tile([NQ, 1], F32, name="neg_max%d" % u)
+            nc.vector.tensor_scalar(
+                negated[:], scores[:].rearrange("q (s t) -> q t s", t=PACK), -1.0, neg_max[:],
+                op0=ALU.mult, op1=ALU.min, accum_out=running[:],
+            )
+            neg_max = running
+
+        value_scales = keep.tile([P, PAGES * DV], U8, name="value_scales", align_bytes=64)
+        nc.vector.tensor_copy(value_scales[:], value_scale_pool[:].indirect(column_list[:]))
+        values = keep.tile([P, PAGES * DV], U32, name="values", align_bytes=64)
+        nc.vector.tensor_copy(values[:], value_pool[:].bitcast(U32).indirect(column_list[:]))
+
+        terms = keep.tile([NQ, PAGES + 1], F32, name="terms")
+        sums = psum.tile([NQ, DV], F32, name="sums")
+        weights = []
+        for u in range(PAGES):
+            probs = keep.tile([NQ, PACK, P], F32, name="probs%d" % u)
+            nc.scalar.activation(probs[:], neg_scores[u][1][:], ACT.Exp, bias=neg_max[:], scale=-1.0, accum_out=terms[:, u : u + 1])
+            turned = psum.tile([P, PACK, NQ], F32, name="turned_probs%d" % u, tag="turned%d" % u)
+            for t in range(PACK):
+                nc.tensor.transpose(turned[:, t, :], probs[:, t, :], ident[:])
+            w_grouped = keep.tile([P, NQ, PACK], BF16, name="w_grouped%d" % u, align_bytes=64)
+            nc.vector.tensor_tensor(
+                w_grouped[:], turned[:].rearrange("p t q -> p q t"),
+                slot_scales[:, u, :].unsqueeze(1).to_broadcast([P, NQ, PACK]), ALU.mult,
+            )
+            weights.append(w_grouped)
+        nc.scalar.activation(terms[:, PAGES : PAGES + 1], sink_col[:], ACT.Exp, bias=neg_max[:])
+        for u in range(PAGES):
+            w_codes = keep.tile([P, NQ], U32, name="w_codes%d" % u, align_bytes=64)
+            w_scales = keep.tile([P, NQ], U8, name="w_scales%d" % u, align_bytes=64)
+            nc.vector.quantize_mx(w_codes[:].bitcast(FP8X4), w_scales[:], weights[u][:].rearrange("p q t -> p (q t)"))
+            nc.tensor.matmul_mx(
+                sums[:],
+                lhsT=w_codes[:].bitcast(FP8X4),
+                lhsT_scale=w_scales[:],
+                rhs=values[:, DV * u : DV * (u + 1)].bitcast(FP8X4),
+                rhs_scale=value_scales[:, DV * u : DV * (u + 1)],
+                start=(u == 0),
+                stop=(u == PAGES - 1),
+            )
+        total = keep.tile([NQ, 1], F32, name="total")
+        nc.vector.tensor_reduce(total[:], terms[:], AXIS.X, ALU.add)
+        inverse = keep.tile([NQ, 1], F32, name="inverse")
+        nc.vector.reciprocal(inverse[:], total[:])
+        result = keep.tile([NQ, DV], F32, name="result")
+        nc.scalar.activation(result[:], sums[:], ACT.Copy, scale=inverse[:])
+        nc.sync.dma_start(out[0], result[:])

@@ -41,32 +41,25 @@ def tile_attend_pkv4_sink_kernel(tc, qT, k_words, k_scales, v_words, v_scales, v
         column_list = lists.tile([P, PAGES * DV // 16], U16, name="column_list")
         nc.sync.dma_start(column_list[:], voffs)
 
-        key_scale_pool = keep.tile([P, POOL], U8, name="key_scale_pool", tag="late_values", align_bytes=64)
+        sink_col = keep.tile([P, 1], F32, name="sink_col")
+        nc.scalar.dma_start(sink_col[:], sink[0])
+        key_scale_pool = keep.tile([P, POOL], U8, name="key_scale_pool", tag="scale_pool")
         nc.vector.memset(key_scale_pool[:].bitcast(I32), 0)
         nc.scalar.dma_start(key_scale_pool[:].bitcast(I32)[0:P:4, :], k_scales.rearrange("o f t -> (o f) t").bitcast(I32))
-        value_scale_pool = keep.tile([P, POOL_PAGES * DV], U8, name="value_scale_pool")
-        token_scale_pool = keep.tile([P, POOL], F32, name="token_scale_pool")
+        zero_col = keep.tile([P, 1], F32, name="zero_col")
+        nc.vector.memset(zero_col[:], 0.0)
+        token_scale_pool = keep.tile([P, POOL], F32, name="token_scale_pool", tag="pairs")
         nc.vector.memset(token_scale_pool[:], 0.0)
-        nc.vector.memset(value_scale_pool[:].bitcast(I32), 0)
         key_planes = keep.tile([P, PASSES, SLOTS], U8, name="key_planes", align_bytes=64)
         nc.vector.memset(key_planes[:].rearrange("p o n -> p (o n)").bitcast(I32), 0)
 
-        zero_col = keep.tile([P, 1], F32, name="zero_col")
-        nc.gpsimd.memset(zero_col[:], 0.0)
-        sink_col = keep.tile([P, 1], F32, name="sink_col")
-        nc.gpsimd.dma_start(sink_col[:], sink[0])
         ident = keep.tile([P, P], F32, name="ident")
         make_identity(nc, ident[:])
-        for quad in range(4):
-            nc.gpsimd.dma_start(
-                value_scale_pool[32 * quad : 32 * quad + 4, :].bitcast(I32).rearrange("f (u e) -> f u e", u=POOL_PAGES),
-                v_scales[:, 4 * quad : 4 * quad + 4, :].bitcast(I32).rearrange("u f e -> f u e"),
-            )
 
         warm = keep.tile([P, 1], F32, name="warm")
         nc.scalar.activation(warm[:], zero_col[:], ACT.Exp)
 
-        q_grouped = keep.tile([P, PASSES, NQ, PACK], BF16, name="q_grouped", align_bytes=64)
+        q_grouped = keep.tile([P, PASSES, NQ, PACK], BF16, name="q_grouped", tag="late_values", align_bytes=64)
         nc.scalar.copy(q_grouped[:], q_raw[:].rearrange("p g j w -> p g w j"))
         nc.scalar.dma_start(token_scale_pool[0:1, :], vs[0:1, :])
         neg_sink = keep.tile([P, 1], F32, name="neg_sink")
@@ -80,32 +73,39 @@ def tile_attend_pkv4_sink_kernel(tc, qT, k_words, k_scales, v_words, v_scales, v
                     key_planes[r:P:32, o, :].bitcast(I32),
                     key_scales[64 * o + 4 * r : 64 * o + 64 : 16, :].bitcast(I32),
                 )
+        q_codes = keep.tile([P, PASSES * NQ], U32, name="q_codes", tag="codes", align_bytes=64)
+        q_scales = keep.tile([P, PASSES * NQ], U8, name="q_scales", tag="scales", align_bytes=64)
+        nc.vector.quantize_mx(q_codes[:].bitcast(FP8X4), q_scales[:], q_grouped[:].rearrange("p g w j -> p (g w j)"))
+
         value_pool = keep.tile([P, POOL_PAGES * DV], I32, name="value_pool", tag="late_values", align_bytes=64)
         nc.sync.dma_start(
             value_pool[:].rearrange("p (u e) -> p u e", u=POOL_PAGES),
             v_words.rearrange("u p e r -> p u (e r)").bitcast(I32),
         )
 
-        q_codes = keep.tile([P, PASSES * NQ], U32, name="q_codes", align_bytes=64)
-        q_scales = keep.tile([P, PASSES * NQ], U8, name="q_scales", align_bytes=64)
-        nc.vector.quantize_mx(q_codes[:].bitcast(FP8X4), q_scales[:], q_grouped[:].rearrange("p g w j -> p (g w j)"))
-
+        value_scale_pool = keep.tile([P, POOL_PAGES * DV], U8, name="value_scale_pool", tag="scale_pool")
+        nc.vector.memset(value_scale_pool[:].bitcast(I32), 0)
+        for quad in range(4):
+            nc.sync.dma_start(
+                value_scale_pool[32 * quad : 32 * quad + 4, :].bitcast(I32).rearrange("f (u e) -> f u e", u=POOL_PAGES),
+                v_scales[:, 4 * quad : 4 * quad + 4, :].bitcast(I32).rearrange("u f e -> f u e"),
+            )
         token_scales = keep.tile([P, SLOTS], F32, name="token_scales")
         nc.vector.tensor_copy(token_scales[:], token_scale_pool[:].indirect(slot_list[:]))
-        slot_scales = keep.tile([P, PAGES, PACK], F32, name="slot_scales")
+        slot_scales = []
         for u in range(PAGES):
-            turned = psum.tile([P, PACK, NQ], F32, name="turned_scales%d" % u, tag="turned%d" % u)
-            for t in range(PACK):
-                nc.tensor.transpose(turned[:, t, :], token_scales[:, PAGE * u + t : PAGE * (u + 1) : PACK], ident[:])
-            nc.scalar.copy(slot_scales[:, u, :], turned[:, :, 0])
+            spread = keep.tile([P, PACK], F32, name="slot_scales%d" % u)
+            nc.sync.dma_start(spread[:], token_scales[0:1, PAGE * u : PAGE * (u + 1)])
+            slot_scales.append(spread)
 
         neg_scores = []
         neg_max = neg_sink
+        all_pairs = keep.tile([P, SLOTS], U32, name="key_pairs", tag="pairs")
         for u in range(PAGES):
-            key_pairs = keep.tile([P, PAGE], U32, name="key_pairs%d" % u)
-            nc.vector.tensor_copy(key_pairs[:], key_pool[:].bitcast(U32).indirect(slot_list[:, 32 * u : 32 * (u + 1)]))
+            key_pairs = all_pairs[:, PAGE * u : PAGE * (u + 1)]
+            nc.vector.tensor_copy(key_pairs, key_pool[:].bitcast(U32).indirect(slot_list[:, 32 * u : 32 * (u + 1)]))
             keys = keep.tile([P, PASSES, PAGE], U16, name="keys%d" % u, align_bytes=64)
-            nc.vector.tensor_copy(keys[:], key_pairs[:].bitcast(U16).rearrange("p (n o) -> p o n", o=PASSES))
+            nc.vector.tensor_copy(keys[:], key_pairs.bitcast(U16).rearrange("p (n o) -> p o n", o=PASSES))
             scores = psum.tile([NQ, PAGE], F32, name="scores%d" % u)
             for o in range(PASSES):
                 nc.tensor.matmul_mx(
@@ -127,9 +127,9 @@ def tile_attend_pkv4_sink_kernel(tc, qT, k_words, k_scales, v_words, v_scales, v
             )
             neg_max = running
 
-        value_scales = keep.tile([P, PAGES * DV], U8, name="value_scales", align_bytes=64)
+        value_scales = keep.tile([P, PAGES * DV], U8, name="value_scales", tag="scales", align_bytes=64)
         nc.vector.tensor_copy(value_scales[:], value_scale_pool[:].indirect(column_list[:]))
-        values = keep.tile([P, PAGES * DV], U32, name="values", align_bytes=64)
+        values = keep.tile([P, PAGES * DV], U32, name="values", tag="codes", align_bytes=64)
         nc.vector.tensor_copy(values[:], value_pool[:].bitcast(U32).indirect(column_list[:]))
 
         terms = keep.tile([NQ, PAGES + 1], F32, name="terms")
@@ -138,13 +138,13 @@ def tile_attend_pkv4_sink_kernel(tc, qT, k_words, k_scales, v_words, v_scales, v
         for u in range(PAGES):
             probs = keep.tile([NQ, PACK, P], F32, name="probs%d" % u)
             nc.scalar.activation(probs[:], neg_scores[u][1][:], ACT.Exp, bias=neg_max[:], scale=-1.0, accum_out=terms[:, u : u + 1])
-            turned = psum.tile([P, PACK, NQ], F32, name="turned_probs%d" % u, tag="turned%d" % u)
+            turned = psum.tile([P, PACK, NQ], F32, name="turned_probs%d" % u)
             for t in range(PACK):
                 nc.tensor.transpose(turned[:, t, :], probs[:, t, :], ident[:])
             w_grouped = keep.tile([P, NQ, PACK], BF16, name="w_grouped%d" % u, align_bytes=64)
             nc.vector.tensor_tensor(
                 w_grouped[:], turned[:].rearrange("p t q -> p q t"),
-                slot_scales[:, u, :].unsqueeze(1).to_broadcast([P, NQ, PACK]), ALU.mult,
+                slot_scales[u][:].unsqueeze(1).to_broadcast([P, NQ, PACK]), ALU.mult,
             )
             weights.append(w_grouped)
         nc.scalar.activation(terms[:, PAGES : PAGES + 1], sink_col[:], ACT.Exp, bias=neg_max[:])
@@ -162,7 +162,8 @@ def tile_attend_pkv4_sink_kernel(tc, qT, k_words, k_scales, v_words, v_scales, v
                 stop=(u == PAGES - 1),
             )
         total = keep.tile([NQ, 1], F32, name="total")
-        nc.vector.tensor_reduce(total[:], terms[:], AXIS.X, ALU.add)
+        summed = keep.tile([NQ, PAGES + 1], F32, name="summed")
+        nc.scalar.activation(summed[:], terms[:], ACT.Copy, accum_out=total[:])
         inverse = keep.tile([NQ, 1], F32, name="inverse")
         nc.vector.reciprocal(inverse[:], total[:])
         result = keep.tile([NQ, DV], F32, name="result")

@@ -22,6 +22,7 @@ SLOTS, POOL, D, DV, NQ = 1536, 4096, 1024, 256, 128
 PAGES = SLOTS // PAGE
 POOL_PAGES = POOL // PAGE
 PASSES = D // PAGE
+ROW0 = P - 16 * PASSES
 FLOPS = 2 * NQ * SLOTS * (D + DV)
 
 
@@ -34,78 +35,76 @@ def tile_attend_pkv4_sink_kernel(tc, qT, k_words, k_scales, v_words, v_scales, v
 
         slot_list = lists.tile([P, SLOTS // 16], U16, name="slot_list")
         nc.sync.dma_start(slot_list[:], offs)
+        key_scale_pool = keep.tile([P, POOL], U8, name="key_scale_pool")
+        nc.vector.memset(key_scale_pool[0:ROW0, :].bitcast(I32), 0)
+        nc.sync.dma_start(key_scale_pool[ROW0:P, :].bitcast(I32), k_scales.rearrange("o f t -> (o f) t").bitcast(I32))
+        token_scale_pool = keep.tile([P, POOL], F32, name="token_scale_pool")
+        nc.sync.dma_start(token_scale_pool[P - 1 : P, :], vs[0:1, :])
         q_raw = keep.tile([P, PASSES, PACK, NQ], F32, name="q_raw")
         nc.sync.dma_start(q_raw[:], qT[0].rearrange("(g p j) w -> p g j w", g=PASSES, j=PACK))
         key_pool = keep.tile([P, POOL], I32, name="key_pool")
         nc.sync.dma_start(key_pool[:], k_words[0].rearrange("p t b -> p (t b)").bitcast(I32))
         column_list = lists.tile([P, PAGES * DV // 16], U16, name="column_list")
         nc.sync.dma_start(column_list[:], voffs)
-
         sink_col = keep.tile([P, 1], F32, name="sink_col")
-        nc.scalar.dma_start(sink_col[:], sink[0])
-        key_scale_pool = keep.tile([P, POOL], U8, name="key_scale_pool", tag="scale_pool")
-        nc.vector.memset(key_scale_pool[:].bitcast(I32), 0)
-        nc.scalar.dma_start(key_scale_pool[:].bitcast(I32)[0:P:4, :], k_scales.rearrange("o f t -> (o f) t").bitcast(I32))
-        zero_col = keep.tile([P, 1], F32, name="zero_col")
-        nc.vector.memset(zero_col[:], 0.0)
-        token_scale_pool = keep.tile([P, POOL], F32, name="token_scale_pool", tag="pairs")
-        nc.vector.memset(token_scale_pool[:], 0.0)
-        key_planes = keep.tile([P, PASSES, SLOTS], U8, name="key_planes", align_bytes=64)
-        nc.vector.memset(key_planes[:].rearrange("p o n -> p (o n)").bitcast(I32), 0)
+        nc.sync.dma_start(sink_col[:], sink[0])
 
         ident = keep.tile([P, P], F32, name="ident")
         make_identity(nc, ident[:])
+        nc.gpsimd.memset(token_scale_pool[0 : P - 1, :], 0.0)
+        key_planes = keep.tile([P, PASSES, SLOTS], U8, name="key_planes", align_bytes=64)
+        nc.vector.memset(key_planes[:].rearrange("p o n -> p (o n)").bitcast(I32), 0)
+        value_scale_pool = keep.tile([P, POOL_PAGES * DV], U8, name="value_scale_pool")
+        nc.gpsimd.memset(value_scale_pool[:].bitcast(I32), 0)
 
+        zero_col = keep.tile([P, 1], F32, name="zero_col")
+        nc.vector.memset(zero_col[:], 0.0)
         warm = keep.tile([P, 1], F32, name="warm")
         nc.scalar.activation(warm[:], zero_col[:], ACT.Exp)
 
-        q_grouped = keep.tile([P, PASSES, NQ, PACK], BF16, name="q_grouped", tag="late_values", align_bytes=64)
+        q_grouped = keep.tile([P, PASSES, NQ, PACK], BF16, name="q_grouped", align_bytes=64)
         nc.scalar.copy(q_grouped[:], q_raw[:].rearrange("p g j w -> p g w j"))
-        nc.scalar.dma_start(token_scale_pool[0:1, :], vs[0:1, :])
         neg_sink = keep.tile([P, 1], F32, name="neg_sink")
         nc.scalar.activation(neg_sink[:], sink_col[:], ACT.Copy, scale=-1.0)
 
-        key_scales = keep.tile([P, SLOTS], U8, name="key_scales")
+        key_scales = keep.tile([P, SLOTS], U8, name="key_scales", tag="late_values")
         nc.vector.tensor_copy(key_scales[:], key_scale_pool[:].indirect(slot_list[:]))
         for o in range(PASSES):
-            for r in range(4):
-                nc.sync.dma_start(
-                    key_planes[r:P:32, o, :].bitcast(I32),
-                    key_scales[64 * o + 4 * r : 64 * o + 64 : 16, :].bitcast(I32),
+            for quad in range(4):
+                row = ROW0 + 16 * o + 4 * quad
+                nc.scalar.dma_start(
+                    key_planes[32 * quad : 32 * quad + 4, o, :].bitcast(I32),
+                    key_scales[row : row + 4, :].bitcast(I32),
                 )
-        q_codes = keep.tile([P, PASSES * NQ], U32, name="q_codes", tag="codes", align_bytes=64)
-        q_scales = keep.tile([P, PASSES * NQ], U8, name="q_scales", tag="scales", align_bytes=64)
+        q_codes = keep.tile([P, PASSES * NQ], U32, name="q_codes", align_bytes=64)
+        q_scales = keep.tile([P, PASSES * NQ], U8, name="q_scales", align_bytes=64)
         nc.vector.quantize_mx(q_codes[:].bitcast(FP8X4), q_scales[:], q_grouped[:].rearrange("p g w j -> p (g w j)"))
 
-        value_pool = keep.tile([P, POOL_PAGES * DV], I32, name="value_pool", tag="late_values", align_bytes=64)
-        nc.sync.dma_start(
-            value_pool[:].rearrange("p (u e) -> p u e", u=POOL_PAGES),
-            v_words.rearrange("u p e r -> p u (e r)").bitcast(I32),
-        )
-
-        value_scale_pool = keep.tile([P, POOL_PAGES * DV], U8, name="value_scale_pool", tag="scale_pool")
-        nc.vector.memset(value_scale_pool[:].bitcast(I32), 0)
         for quad in range(4):
             nc.sync.dma_start(
                 value_scale_pool[32 * quad : 32 * quad + 4, :].bitcast(I32).rearrange("f (u e) -> f u e", u=POOL_PAGES),
                 v_scales[:, 4 * quad : 4 * quad + 4, :].bitcast(I32).rearrange("u f e -> f u e"),
             )
+        value_pool = keep.tile([P, POOL_PAGES * DV], I32, name="value_pool", tag="late_values")
+        nc.sync.dma_start(
+            value_pool[:].rearrange("p (u e) -> p u e", u=POOL_PAGES),
+            v_words.rearrange("u p e r -> p u (e r)").bitcast(I32),
+        )
         token_scales = keep.tile([P, SLOTS], F32, name="token_scales")
         nc.vector.tensor_copy(token_scales[:], token_scale_pool[:].indirect(slot_list[:]))
         slot_scales = []
         for u in range(PAGES):
             spread = keep.tile([P, PACK], F32, name="slot_scales%d" % u)
-            nc.sync.dma_start(spread[:], token_scales[0:1, PAGE * u : PAGE * (u + 1)])
+            nc.sync.dma_start(spread[:], token_scales[P - 1 : P, PAGE * u : PAGE * (u + 1)])
             slot_scales.append(spread)
 
         neg_scores = []
         neg_max = neg_sink
-        all_pairs = keep.tile([P, SLOTS], U32, name="key_pairs", tag="pairs")
         for u in range(PAGES):
-            key_pairs = all_pairs[:, PAGE * u : PAGE * (u + 1)]
-            nc.vector.tensor_copy(key_pairs, key_pool[:].bitcast(U32).indirect(slot_list[:, 32 * u : 32 * (u + 1)]))
+            key_pairs = keep.tile([P, PAGE], U32, name="key_pairs%d" % u, tag="pairs%d" % u, align_bytes=64)
+            nc.vector.tensor_copy(key_pairs[:], key_pool[:].bitcast(U32).indirect(slot_list[:, 32 * u : 32 * (u + 1)]))
             keys = keep.tile([P, PASSES, PAGE], U16, name="keys%d" % u, align_bytes=64)
-            nc.vector.tensor_copy(keys[:], key_pairs.bitcast(U16).rearrange("p (n o) -> p o n", o=PASSES))
+            nc.vector.tensor_copy(keys[:], key_pairs[:].bitcast(U16).rearrange("p (n o) -> p o n", o=PASSES))
             scores = psum.tile([NQ, PAGE], F32, name="scores%d" % u)
             for o in range(PASSES):
                 nc.tensor.matmul_mx(
@@ -120,16 +119,16 @@ def tile_attend_pkv4_sink_kernel(tc, qT, k_words, k_scales, v_words, v_scales, v
             neg_scores.append((scores, keep.tile([NQ, PACK, P], F32, name="neg_scores%d" % u)))
         for u in range(PAGES):
             scores, negated = neg_scores[u]
-            running = keep.tile([NQ, 1], F32, name="neg_max%d" % u)
+            running = keep.tile([NQ, 1], F32, name="neg_max%d" % u, tag="max%d" % u, align_bytes=64)
             nc.vector.tensor_scalar(
                 negated[:], scores[:].rearrange("q (s t) -> q t s", t=PACK), -1.0, neg_max[:],
                 op0=ALU.mult, op1=ALU.min, accum_out=running[:],
             )
             neg_max = running
 
-        value_scales = keep.tile([P, PAGES * DV], U8, name="value_scales", tag="scales", align_bytes=64)
+        value_scales = keep.tile([P, PAGES * DV], U8, name="value_scales", tag="pairs%d" % (PAGES - 1), align_bytes=64)
         nc.vector.tensor_copy(value_scales[:], value_scale_pool[:].indirect(column_list[:]))
-        values = keep.tile([P, PAGES * DV], U32, name="values", tag="codes", align_bytes=64)
+        values = keep.tile([P, PAGES * DV], U32, name="values", tag="max%d" % (PAGES - 2), align_bytes=64)
         nc.vector.tensor_copy(values[:], value_pool[:].bitcast(U32).indirect(column_list[:]))
 
         terms = keep.tile([NQ, PAGES + 1], F32, name="terms")

@@ -35,39 +35,34 @@ def tile_attend_pkv4_sink_kernel(tc, qT, k_words, k_scales, v_words, v_scales, v
 
         slot_list = lists.tile([P, SLOTS // 16], U16, name="slot_list")
         nc.sync.dma_start(slot_list[:], offs)
-        key_scale_pool = keep.tile([P, POOL], U8, name="key_scale_pool")
+        key_scale_pool = keep.tile([P, POOL], U8, name="key_scale_pool", tag="scale_pool")
         nc.vector.memset(key_scale_pool[0:ROW0, :].bitcast(I32), 0)
         nc.sync.dma_start(key_scale_pool[ROW0:P, :].bitcast(I32), k_scales.rearrange("o f t -> (o f) t").bitcast(I32))
         token_scale_pool = keep.tile([P, POOL], F32, name="token_scale_pool")
         nc.sync.dma_start(token_scale_pool[P - 1 : P, :], vs[0:1, :])
+        sink_col = keep.tile([P, 1], F32, name="sink_col")
+        nc.sync.dma_start(sink_col[:], sink[0])
+        column_list = lists.tile([P, PAGES * DV // 16], U16, name="column_list")
+        nc.sync.dma_start(column_list[:], voffs)
         q_raw = keep.tile([P, PASSES, PACK, NQ], F32, name="q_raw")
         nc.sync.dma_start(q_raw[:], qT[0].rearrange("(g p j) w -> p g j w", g=PASSES, j=PACK))
         key_pool = keep.tile([P, POOL], I32, name="key_pool")
         nc.sync.dma_start(key_pool[:], k_words[0].rearrange("p t b -> p (t b)").bitcast(I32))
-        column_list = lists.tile([P, PAGES * DV // 16], U16, name="column_list")
-        nc.sync.dma_start(column_list[:], voffs)
-        sink_col = keep.tile([P, 1], F32, name="sink_col")
-        nc.sync.dma_start(sink_col[:], sink[0])
 
         ident = keep.tile([P, P], F32, name="ident")
         make_identity(nc, ident[:])
-        nc.gpsimd.memset(token_scale_pool[0 : P - 1, :], 0.0)
-        key_planes = keep.tile([P, PASSES, SLOTS], U8, name="key_planes", align_bytes=64)
-        nc.vector.memset(key_planes[:].rearrange("p o n -> p (o n)").bitcast(I32), 0)
-        value_scale_pool = keep.tile([P, POOL_PAGES * DV], U8, name="value_scale_pool")
-        nc.gpsimd.memset(value_scale_pool[:].bitcast(I32), 0)
-
         zero_col = keep.tile([P, 1], F32, name="zero_col")
         nc.vector.memset(zero_col[:], 0.0)
+        key_planes = keep.tile([P, PASSES, SLOTS], U8, name="key_planes", align_bytes=64)
+        nc.vector.memset(key_planes[:].rearrange("p o n -> p (o n)").bitcast(I32), 0)
+        nc.vector.memset(token_scale_pool[0 : P - 1, :], 0.0)
+
         warm = keep.tile([P, 1], F32, name="warm")
         nc.scalar.activation(warm[:], zero_col[:], ACT.Exp)
-
-        q_grouped = keep.tile([P, PASSES, NQ, PACK], BF16, name="q_grouped", align_bytes=64)
-        nc.scalar.copy(q_grouped[:], q_raw[:].rearrange("p g j w -> p g w j"))
         neg_sink = keep.tile([P, 1], F32, name="neg_sink")
         nc.scalar.activation(neg_sink[:], sink_col[:], ACT.Copy, scale=-1.0)
 
-        key_scales = keep.tile([P, SLOTS], U8, name="key_scales", tag="late_values")
+        key_scales = keep.tile([P, SLOTS], U8, name="key_scales")
         nc.vector.tensor_copy(key_scales[:], key_scale_pool[:].indirect(slot_list[:]))
         for o in range(PASSES):
             for quad in range(4):
@@ -76,27 +71,31 @@ def tile_attend_pkv4_sink_kernel(tc, qT, k_words, k_scales, v_words, v_scales, v
                     key_planes[32 * quad : 32 * quad + 4, o, :].bitcast(I32),
                     key_scales[row : row + 4, :].bitcast(I32),
                 )
+        q_grouped = keep.tile([P, PASSES, NQ, PACK], BF16, name="q_grouped", tag="late_values", align_bytes=64)
+        nc.vector.tensor_copy(q_grouped[:], q_raw[:].rearrange("p g j w -> p g w j"))
+        token_scales = keep.tile([P, SLOTS], F32, name="token_scales")
+        nc.vector.tensor_copy(token_scales[:], token_scale_pool[:].indirect(slot_list[:]))
         q_codes = keep.tile([P, PASSES * NQ], U32, name="q_codes", align_bytes=64)
         q_scales = keep.tile([P, PASSES * NQ], U8, name="q_scales", align_bytes=64)
         nc.vector.quantize_mx(q_codes[:].bitcast(FP8X4), q_scales[:], q_grouped[:].rearrange("p g w j -> p (g w j)"))
 
-        for quad in range(4):
-            nc.sync.dma_start(
-                value_scale_pool[32 * quad : 32 * quad + 4, :].bitcast(I32).rearrange("f (u e) -> f u e", u=POOL_PAGES),
-                v_scales[:, 4 * quad : 4 * quad + 4, :].bitcast(I32).rearrange("u f e -> f u e"),
-            )
-        value_pool = keep.tile([P, POOL_PAGES * DV], I32, name="value_pool", tag="late_values")
-        nc.sync.dma_start(
-            value_pool[:].rearrange("p (u e) -> p u e", u=POOL_PAGES),
-            v_words.rearrange("u p e r -> p u (e r)").bitcast(I32),
-        )
-        token_scales = keep.tile([P, SLOTS], F32, name="token_scales")
-        nc.vector.tensor_copy(token_scales[:], token_scale_pool[:].indirect(slot_list[:]))
         slot_scales = []
         for u in range(PAGES):
             spread = keep.tile([P, PACK], F32, name="slot_scales%d" % u)
             nc.sync.dma_start(spread[:], token_scales[P - 1 : P, PAGE * u : PAGE * (u + 1)])
             slot_scales.append(spread)
+        value_pool = keep.tile([P, POOL_PAGES * DV], I32, name="value_pool", tag="late_values", align_bytes=64)
+        nc.sync.dma_start(
+            value_pool[:].rearrange("p (u e) -> p u e", u=POOL_PAGES),
+            v_words.rearrange("u p e r -> p u (e r)").bitcast(I32),
+        )
+        value_scale_pool = keep.tile([P, POOL_PAGES * DV], U8, name="value_scale_pool", tag="scale_pool")
+        nc.vector.memset(value_scale_pool[:].bitcast(I32), 0)
+        for quad in range(4):
+            nc.sync.dma_start(
+                value_scale_pool[32 * quad : 32 * quad + 4, :].bitcast(I32).rearrange("f (u e) -> f u e", u=POOL_PAGES),
+                v_scales[:, 4 * quad : 4 * quad + 4, :].bitcast(I32).rearrange("u f e -> f u e"),
+            )
 
         neg_scores = []
         neg_max = neg_sink
@@ -126,10 +125,10 @@ def tile_attend_pkv4_sink_kernel(tc, qT, k_words, k_scales, v_words, v_scales, v
             )
             neg_max = running
 
-        value_scales = keep.tile([P, PAGES * DV], U8, name="value_scales", tag="pairs%d" % (PAGES - 1), align_bytes=64)
-        nc.vector.tensor_copy(value_scales[:], value_scale_pool[:].indirect(column_list[:]))
         values = keep.tile([P, PAGES * DV], U32, name="values", tag="max%d" % (PAGES - 2), align_bytes=64)
         nc.vector.tensor_copy(values[:], value_pool[:].bitcast(U32).indirect(column_list[:]))
+        value_scales = keep.tile([P, PAGES * DV], U8, name="value_scales", tag="late_values", align_bytes=64)
+        nc.vector.tensor_copy(value_scales[:], value_scale_pool[:].indirect(column_list[:]))
 
         terms = keep.tile([NQ, PAGES + 1], F32, name="terms")
         sums = psum.tile([NQ, DV], F32, name="sums")

@@ -23,6 +23,7 @@ PAGES = SLOTS // PAGE
 POOL_PAGES = POOL // PAGE
 PASSES = D // PAGE
 ROW0 = P - 16 * PASSES
+HALF = DV // 2
 FLOPS = 2 * NQ * SLOTS * (D + DV)
 
 
@@ -35,11 +36,16 @@ def tile_attend_pkv4_sink_kernel(tc, qT, k_words, k_scales, v_words, v_scales, v
 
         slot_list = lists.tile([P, SLOTS // 16], U16, name="slot_list")
         nc.sync.dma_start(slot_list[:], offs)
-        key_scale_pool = keep.tile([P, POOL], U8, name="key_scale_pool", tag="scale_pool")
+        key_scale_pool = keep.tile([P, POOL], U8, name="key_scale_pool")
         nc.vector.memset(key_scale_pool[0:ROW0, :].bitcast(I32), 0)
         nc.sync.dma_start(key_scale_pool[ROW0:P, :].bitcast(I32), k_scales.rearrange("o f t -> (o f) t").bitcast(I32))
         token_scale_pool = keep.tile([P, POOL], F32, name="token_scale_pool")
         nc.sync.dma_start(token_scale_pool[P - 1 : P, :], vs[0:1, :])
+        value_scale_pool = keep.tile([P, POOL_PAGES * DV], U8, name="value_scale_pool")
+        nc.sync.dma_start(
+            value_scale_pool[P - 16 : P, :].bitcast(I32).rearrange("f (u e) -> f u e", u=POOL_PAGES),
+            v_scales.bitcast(I32).rearrange("u f e -> f u e"),
+        )
         sink_col = keep.tile([P, 1], F32, name="sink_col")
         nc.sync.dma_start(sink_col[:], sink[0])
         column_list = lists.tile([P, PAGES * DV // 16], U16, name="column_list")
@@ -56,11 +62,16 @@ def tile_attend_pkv4_sink_kernel(tc, qT, k_words, k_scales, v_words, v_scales, v
         key_planes = keep.tile([P, PASSES, SLOTS], U8, name="key_planes", align_bytes=64)
         nc.vector.memset(key_planes[:].rearrange("p o n -> p (o n)").bitcast(I32), 0)
         nc.vector.memset(token_scale_pool[0 : P - 1, :], 0.0)
+        nc.vector.memset(value_scale_pool[0 : P - 16, :].bitcast(I32), 0)
+        value_plane = keep.tile([P, PAGES * DV], U8, name="value_plane", align_bytes=64)
+        nc.vector.memset(value_plane[:].bitcast(I32), 0)
 
         warm = keep.tile([P, 1], F32, name="warm")
         nc.scalar.activation(warm[:], zero_col[:], ACT.Exp)
         neg_sink = keep.tile([P, 1], F32, name="neg_sink")
         nc.scalar.activation(neg_sink[:], sink_col[:], ACT.Copy, scale=-1.0)
+        q_grouped = keep.tile([P, PASSES, NQ, PACK], BF16, name="q_grouped", tag="late_values", align_bytes=64)
+        nc.scalar.copy(q_grouped[:], q_raw[:].rearrange("p g j w -> p g w j"))
 
         key_scales = keep.tile([P, SLOTS], U8, name="key_scales")
         nc.vector.tensor_copy(key_scales[:], key_scale_pool[:].indirect(slot_list[:]))
@@ -71,13 +82,13 @@ def tile_attend_pkv4_sink_kernel(tc, qT, k_words, k_scales, v_words, v_scales, v
                     key_planes[32 * quad : 32 * quad + 4, o, :].bitcast(I32),
                     key_scales[row : row + 4, :].bitcast(I32),
                 )
-        q_grouped = keep.tile([P, PASSES, NQ, PACK], BF16, name="q_grouped", tag="late_values", align_bytes=64)
-        nc.vector.tensor_copy(q_grouped[:], q_raw[:].rearrange("p g j w -> p g w j"))
         token_scales = keep.tile([P, SLOTS], F32, name="token_scales")
         nc.vector.tensor_copy(token_scales[:], token_scale_pool[:].indirect(slot_list[:]))
         q_codes = keep.tile([P, PASSES * NQ], U32, name="q_codes", align_bytes=64)
         q_scales = keep.tile([P, PASSES * NQ], U8, name="q_scales", align_bytes=64)
         nc.vector.quantize_mx(q_codes[:].bitcast(FP8X4), q_scales[:], q_grouped[:].rearrange("p g w j -> p (g w j)"))
+        value_scales = keep.tile([P, PAGES * DV], U8, name="value_scales")
+        nc.vector.tensor_copy(value_scales[:], value_scale_pool[:].indirect(column_list[:]))
 
         slot_scales = []
         for u in range(PAGES):
@@ -89,25 +100,27 @@ def tile_attend_pkv4_sink_kernel(tc, qT, k_words, k_scales, v_words, v_scales, v
             value_pool[:].rearrange("p (u e) -> p u e", u=POOL_PAGES),
             v_words.rearrange("u p e r -> p u (e r)").bitcast(I32),
         )
-        value_scale_pool = keep.tile([P, POOL_PAGES * DV], U8, name="value_scale_pool", tag="scale_pool")
-        nc.vector.memset(value_scale_pool[:].bitcast(I32), 0)
         for quad in range(4):
-            nc.sync.dma_start(
-                value_scale_pool[32 * quad : 32 * quad + 4, :].bitcast(I32).rearrange("f (u e) -> f u e", u=POOL_PAGES),
-                v_scales[:, 4 * quad : 4 * quad + 4, :].bitcast(I32).rearrange("u f e -> f u e"),
-            )
+            row = P - 16 + 4 * quad
+            nc.sync.dma_start(value_plane[32 * quad : 32 * quad + 4, :].bitcast(I32), value_scales[row : row + 4, :].bitcast(I32))
 
-        neg_scores = []
-        neg_max = neg_sink
-        for u in range(PAGES):
-            key_pairs = keep.tile([P, PAGE], U32, name="key_pairs%d" % u, tag="pairs%d" % u, align_bytes=64)
-            nc.vector.tensor_copy(key_pairs[:], key_pool[:].bitcast(U32).indirect(slot_list[:, 32 * u : 32 * (u + 1)]))
+        key_pairs = []
+        scores = []
+
+        def gather_keys(u):
+            pairs = keep.tile([P, PAGE], U32, name="key_pairs%d" % u)
+            nc.vector.tensor_copy(pairs[:], key_pool[:].bitcast(U32).indirect(slot_list[:, 32 * u : 32 * (u + 1)]))
+            key_pairs.append(pairs)
+
+        def score_page(u, copies):
             keys = keep.tile([P, PASSES, PAGE], U16, name="keys%d" % u, align_bytes=64)
-            nc.vector.tensor_copy(keys[:], key_pairs[:].bitcast(U16).rearrange("p (n o) -> p o n", o=PASSES))
-            scores = psum.tile([NQ, PAGE], F32, name="scores%d" % u)
+            halves = key_pairs[u][:].bitcast(U16).rearrange("p (n o) -> p o n", o=PASSES)
+            for part in copies:
+                nc.vector.tensor_copy(keys[:, part, :], halves[:, part, :])
+            bank = psum.tile([NQ, PAGE], F32, name="scores%d" % u)
             for o in range(PASSES):
                 nc.tensor.matmul_mx(
-                    scores[:],
+                    bank[:],
                     lhsT=q_codes[:, NQ * o : NQ * (o + 1)].bitcast(FP8X4),
                     lhsT_scale=q_scales[:, NQ * o : NQ * (o + 1)],
                     rhs=keys[:, o, :].bitcast(FP4X4),
@@ -115,55 +128,83 @@ def tile_attend_pkv4_sink_kernel(tc, qT, k_words, k_scales, v_words, v_scales, v
                     start=(o == 0),
                     stop=(o == PASSES - 1),
                 )
-            neg_scores.append((scores, keep.tile([NQ, PACK, P], F32, name="neg_scores%d" % u)))
+            scores.append(bank)
+
+        gather_keys(0)
+        gather_keys(1)
+        score_page(0, [slice(0, 1), slice(1, 2)])
+        gather_keys(2)
+        score_page(1, [slice(0, 2)])
+        score_page(2, [slice(0, 2)])
+
+        neg_scores = []
+        neg_max = neg_sink
         for u in range(PAGES):
-            scores, negated = neg_scores[u]
+            negated = keep.tile([NQ, PACK, P], F32, name="neg_scores%d" % u)
             running = keep.tile([NQ, 1], F32, name="neg_max%d" % u, tag="max%d" % u, align_bytes=64)
             nc.vector.tensor_scalar(
-                negated[:], scores[:].rearrange("q (s t) -> q t s", t=PACK), -1.0, neg_max[:],
+                negated[:], scores[u][:].rearrange("q (s t) -> q t s", t=PACK), -1.0, neg_max[:],
                 op0=ALU.mult, op1=ALU.min, accum_out=running[:],
             )
+            neg_scores.append(negated)
             neg_max = running
 
         values = keep.tile([P, PAGES * DV], U32, name="values", tag="max%d" % (PAGES - 2), align_bytes=64)
         nc.vector.tensor_copy(values[:], value_pool[:].bitcast(U32).indirect(column_list[:]))
-        value_scales = keep.tile([P, PAGES * DV], U8, name="value_scales", tag="late_values", align_bytes=64)
-        nc.vector.tensor_copy(value_scales[:], value_scale_pool[:].indirect(column_list[:]))
 
-        terms = keep.tile([NQ, PAGES + 1], F32, name="terms")
-        sums = psum.tile([NQ, DV], F32, name="sums")
+        pieces = [(0, 0, 2), (0, 2, 4), (1, 0, 4), (2, 0, 2), (2, 2, 4)]
+        terms = keep.tile([NQ, len(pieces) + 1], F32, name="terms")
+        probs = [keep.tile([NQ, PACK, P], F32, name="probs%d" % u) for u in range(PAGES)]
+        turned = [psum.tile([P, PACK, NQ], F32, name="turned_probs%d" % u) for u in range(PAGES)]
+        for i, (u, t0, t1) in enumerate(pieces):
+            nc.scalar.activation(
+                probs[u][:, t0:t1, :], neg_scores[u][:, t0:t1, :], ACT.Exp, bias=neg_max[:], scale=-1.0, accum_out=terms[:, i : i + 1]
+            )
+            for t in range(t0, t1):
+                nc.tensor.transpose(turned[u][:, t, :], probs[u][:, t, :], ident[:])
+        nc.scalar.activation(terms[:, len(pieces) : len(pieces) + 1], sink_col[:], ACT.Exp, bias=neg_max[:])
+        total = keep.tile([NQ, 1], F32, name="total")
+        summed = keep.tile([NQ, len(pieces) + 1], F32, name="summed")
+        nc.scalar.activation(summed[:], terms[:], ACT.Copy, accum_out=total[:])
+
         weights = []
-        for u in range(PAGES):
-            probs = keep.tile([NQ, PACK, P], F32, name="probs%d" % u)
-            nc.scalar.activation(probs[:], neg_scores[u][1][:], ACT.Exp, bias=neg_max[:], scale=-1.0, accum_out=terms[:, u : u + 1])
-            turned = psum.tile([P, PACK, NQ], F32, name="turned_probs%d" % u)
-            for t in range(PACK):
-                nc.tensor.transpose(turned[:, t, :], probs[:, t, :], ident[:])
+        sums = [psum.tile([NQ, HALF], F32, name="sums%d" % h) for h in range(2)]
+
+        def weigh(u):
             w_grouped = keep.tile([P, NQ, PACK], BF16, name="w_grouped%d" % u, align_bytes=64)
             nc.vector.tensor_tensor(
-                w_grouped[:], turned[:].rearrange("p t q -> p q t"),
+                w_grouped[:], turned[u][:].rearrange("p t q -> p q t"),
                 slot_scales[u][:].unsqueeze(1).to_broadcast([P, NQ, PACK]), ALU.mult,
             )
             weights.append(w_grouped)
-        nc.scalar.activation(terms[:, PAGES : PAGES + 1], sink_col[:], ACT.Exp, bias=neg_max[:])
-        for u in range(PAGES):
+
+        def multiply(u):
             w_codes = keep.tile([P, NQ], U32, name="w_codes%d" % u, align_bytes=64)
             w_scales = keep.tile([P, NQ], U8, name="w_scales%d" % u, align_bytes=64)
             nc.vector.quantize_mx(w_codes[:].bitcast(FP8X4), w_scales[:], weights[u][:].rearrange("p q t -> p (q t)"))
-            nc.tensor.matmul_mx(
-                sums[:],
-                lhsT=w_codes[:].bitcast(FP8X4),
-                lhsT_scale=w_scales[:],
-                rhs=values[:, DV * u : DV * (u + 1)].bitcast(FP8X4),
-                rhs_scale=value_scales[:, DV * u : DV * (u + 1)],
-                start=(u == 0),
-                stop=(u == PAGES - 1),
-            )
-        total = keep.tile([NQ, 1], F32, name="total")
-        summed = keep.tile([NQ, PAGES + 1], F32, name="summed")
-        nc.scalar.activation(summed[:], terms[:], ACT.Copy, accum_out=total[:])
+            for h in range(2):
+                columns = slice(DV * u + HALF * h, DV * u + HALF * (h + 1))
+                nc.tensor.matmul_mx(
+                    sums[h][:],
+                    lhsT=w_codes[:].bitcast(FP8X4),
+                    lhsT_scale=w_scales[:],
+                    rhs=values[:, columns].bitcast(FP8X4),
+                    rhs_scale=value_plane[:, columns],
+                    start=(u == 0),
+                    stop=(u == PAGES - 1),
+                )
+
+        weigh(0)
+        weigh(1)
+        multiply(0)
+        weigh(2)
+        multiply(1)
         inverse = keep.tile([NQ, 1], F32, name="inverse")
         nc.vector.reciprocal(inverse[:], total[:])
-        result = keep.tile([NQ, DV], F32, name="result")
-        nc.scalar.activation(result[:], sums[:], ACT.Copy, scale=inverse[:])
-        nc.sync.dma_start(out[0], result[:])
+        multiply(2)
+
+        results = [keep.tile([NQ, HALF], F32, name="result%d" % h) for h in range(2)]
+        nc.scalar.activation(results[0][:], sums[0][:], ACT.Copy, scale=inverse[:])
+        nc.vector.tensor_scalar(results[1][:], sums[1][:], inverse[:], None, op0=ALU.mult)
+        nc.scalar.dma_start(out[0][:, 0:HALF], results[0][:])
+        nc.sync.dma_start(out[0][:, HALF:DV], results[1][:])

@@ -40,14 +40,14 @@ def tile_attend_pkv4_sink_kernel(tc, qT, k_words, k_scales, v_words, v_scales, v
         nc.vector.memset(key_scale_pool[0:ROW0, :].bitcast(I32), 0)
         nc.sync.dma_start(key_scale_pool[ROW0:P, :].bitcast(I32), k_scales.rearrange("o f t -> (o f) t").bitcast(I32))
         token_scale_pool = keep.tile([P, POOL], F32, name="token_scale_pool")
-        nc.sync.dma_start(token_scale_pool[P - 1 : P, :], vs[0:1, :])
+        nc.scalar.dma_start(token_scale_pool[P - 1 : P, :], vs[0:1, :])
         value_scale_pool = keep.tile([P, POOL_PAGES * DV], U8, name="value_scale_pool")
-        nc.sync.dma_start(
+        nc.scalar.dma_start(
             value_scale_pool[P - 16 : P, :].bitcast(I32).rearrange("f (u e) -> f u e", u=POOL_PAGES),
             v_scales.bitcast(I32).rearrange("u f e -> f u e"),
         )
         sink_col = keep.tile([P, 1], F32, name="sink_col")
-        nc.sync.dma_start(sink_col[:], sink[0])
+        nc.scalar.dma_start(sink_col[:], sink[0])
         column_list = lists.tile([P, PAGES * DV // 16], U16, name="column_list")
         nc.sync.dma_start(column_list[:], voffs)
         q_raw = keep.tile([P, PASSES, PACK, NQ], F32, name="q_raw")
@@ -59,29 +59,31 @@ def tile_attend_pkv4_sink_kernel(tc, qT, k_words, k_scales, v_words, v_scales, v
         make_identity(nc, ident[:])
         zero_col = keep.tile([P, 1], F32, name="zero_col")
         nc.vector.memset(zero_col[:], 0.0)
-        key_planes = keep.tile([P, PASSES, SLOTS], U8, name="key_planes", align_bytes=64)
-        nc.vector.memset(key_planes[:].rearrange("p o n -> p (o n)").bitcast(I32), 0)
-        nc.vector.memset(token_scale_pool[0 : P - 1, :], 0.0)
-        nc.vector.memset(value_scale_pool[0 : P - 16, :].bitcast(I32), 0)
-        value_plane = keep.tile([P, PAGES * DV], U8, name="value_plane", align_bytes=64)
-        nc.vector.memset(value_plane[:].bitcast(I32), 0)
+        key_planes = [keep.tile([P, SLOTS], U8, name="key_plane%d" % o, align_bytes=64) for o in range(PASSES)]
+        for plane in key_planes:
+            nc.vector.memset(plane[:].bitcast(I32), 0)
+        nc.vector.memset(token_scale_pool[0 : P - 1, 0 : POOL // 2], 0.0)
 
         warm = keep.tile([P, 1], F32, name="warm")
         nc.scalar.activation(warm[:], zero_col[:], ACT.Exp)
         neg_sink = keep.tile([P, 1], F32, name="neg_sink")
-        nc.scalar.activation(neg_sink[:], sink_col[:], ACT.Copy, scale=-1.0)
-        q_grouped = keep.tile([P, PASSES, NQ, PACK], BF16, name="q_grouped", tag="late_values", align_bytes=64)
-        nc.scalar.copy(q_grouped[:], q_raw[:].rearrange("p g j w -> p g w j"))
+        nc.gpsimd.tensor_scalar(neg_sink[:], sink_col[:], -1.0, 0.0, op0=ALU.mult, op1=ALU.add)
 
         key_scales = keep.tile([P, SLOTS], U8, name="key_scales")
         nc.vector.tensor_copy(key_scales[:], key_scale_pool[:].indirect(slot_list[:]))
-        for o in range(PASSES):
+        for o in reversed(range(PASSES)):
             for quad in range(4):
                 row = ROW0 + 16 * o + 4 * quad
                 nc.scalar.dma_start(
-                    key_planes[32 * quad : 32 * quad + 4, o, :].bitcast(I32),
+                    key_planes[o][32 * quad : 32 * quad + 4, :].bitcast(I32),
                     key_scales[row : row + 4, :].bitcast(I32),
                 )
+        nc.vector.memset(token_scale_pool[0 : P - 1, POOL // 2 : POOL], 0.0)
+        nc.vector.memset(value_scale_pool[0 : P - 16, :].bitcast(I32), 0)
+        value_plane = keep.tile([P, PAGES * DV], U8, name="value_plane", align_bytes=64)
+        nc.vector.memset(value_plane[:].bitcast(I32), 0)
+        q_grouped = keep.tile([P, PASSES, NQ, PACK], BF16, name="q_grouped", tag="late_values", align_bytes=64)
+        nc.vector.tensor_copy(q_grouped[:], q_raw[:].rearrange("p g j w -> p g w j"))
         token_scales = keep.tile([P, SLOTS], F32, name="token_scales")
         nc.vector.tensor_copy(token_scales[:], token_scale_pool[:].indirect(slot_list[:]))
         q_codes = keep.tile([P, PASSES * NQ], U32, name="q_codes", align_bytes=64)
@@ -90,19 +92,19 @@ def tile_attend_pkv4_sink_kernel(tc, qT, k_words, k_scales, v_words, v_scales, v
         value_scales = keep.tile([P, PAGES * DV], U8, name="value_scales")
         nc.vector.tensor_copy(value_scales[:], value_scale_pool[:].indirect(column_list[:]))
 
-        slot_scales = []
-        for u in range(PAGES):
-            spread = keep.tile([P, PACK], F32, name="slot_scales%d" % u)
-            nc.sync.dma_start(spread[:], token_scales[P - 1 : P, PAGE * u : PAGE * (u + 1)])
-            slot_scales.append(spread)
         value_pool = keep.tile([P, POOL_PAGES * DV], I32, name="value_pool", tag="late_values", align_bytes=64)
-        nc.sync.dma_start(
+        nc.scalar.dma_start(
             value_pool[:].rearrange("p (u e) -> p u e", u=POOL_PAGES),
             v_words.rearrange("u p e r -> p u (e r)").bitcast(I32),
         )
+        slot_scales = []
+        for u in range(PAGES):
+            spread = keep.tile([P, PACK], F32, name="slot_scales%d" % u)
+            nc.scalar.dma_start(spread[:], token_scales[P - 1 : P, PAGE * u : PAGE * (u + 1)])
+            slot_scales.append(spread)
         for quad in range(4):
             row = P - 16 + 4 * quad
-            nc.sync.dma_start(value_plane[32 * quad : 32 * quad + 4, :].bitcast(I32), value_scales[row : row + 4, :].bitcast(I32))
+            nc.scalar.dma_start(value_plane[32 * quad : 32 * quad + 4, :].bitcast(I32), value_scales[row : row + 4, :].bitcast(I32))
 
         key_pairs = []
         scores = []
@@ -124,7 +126,7 @@ def tile_attend_pkv4_sink_kernel(tc, qT, k_words, k_scales, v_words, v_scales, v
                     lhsT=q_codes[:, NQ * o : NQ * (o + 1)].bitcast(FP8X4),
                     lhsT_scale=q_scales[:, NQ * o : NQ * (o + 1)],
                     rhs=keys[:, o, :].bitcast(FP4X4),
-                    rhs_scale=key_planes[:, o, PAGE * u : PAGE * (u + 1)],
+                    rhs_scale=key_planes[o][:, PAGE * u : PAGE * (u + 1)],
                     start=(o == 0),
                     stop=(o == PASSES - 1),
                 )

@@ -22,7 +22,7 @@ SLOTS, POOL, D, DV, NQ = 1536, 4096, 1024, 256, 128
 PAGES = SLOTS // PAGE
 POOL_PAGES = POOL // PAGE
 PASSES = D // PAGE
-ROW0 = P - 16 * PASSES
+QUADS = 4
 HALF = DV // 2
 FLOPS = 2 * NQ * SLOTS * (D + DV)
 
@@ -36,81 +36,67 @@ def tile_attend_pkv4_sink_kernel(tc, qT, k_words, k_scales, v_words, v_scales, v
 
         slot_list = lists.tile([P, SLOTS // 16], U16, name="slot_list")
         nc.sync.dma_start(slot_list[:], offs)
-        key_scale_pool = keep.tile([P, POOL], U8, name="key_scale_pool")
-        nc.vector.memset(key_scale_pool[0:ROW0, :].bitcast(I32), 0)
-        nc.sync.dma_start(key_scale_pool[ROW0:P, :].bitcast(I32), k_scales.rearrange("o f t -> (o f) t").bitcast(I32))
-        token_scale_pool = keep.tile([P, POOL], F32, name="token_scale_pool")
-        nc.scalar.dma_start(token_scale_pool[P - 1 : P, :], vs[0:1, :])
-        value_scale_pool = keep.tile([P, POOL_PAGES * DV], U8, name="value_scale_pool")
-        nc.scalar.dma_start(
-            value_scale_pool[P - 16 : P, :].bitcast(I32).rearrange("f (u e) -> f u e", u=POOL_PAGES),
-            v_scales.bitcast(I32).rearrange("u f e -> f u e"),
-        )
         sink_col = keep.tile([P, 1], F32, name="sink_col")
         nc.scalar.dma_start(sink_col[:], sink[0])
-        column_list = lists.tile([P, PAGES * DV // 16], U16, name="column_list")
-        nc.sync.dma_start(column_list[:], voffs)
+        token_scale_pool = keep.tile([P, POOL], F32, name="token_scale_pool")
+        nc.sync.dma_start(token_scale_pool[P - 1 : P, :], vs[0:1, :])
+        key_scale_pool = keep.tile([P, POOL], U8, name="key_scale_pool")
+        nc.vector.memset(key_scale_pool[:].bitcast(I32), 0)
+        nc.scalar.dma_start(key_scale_pool[0 : 16 * PASSES, :].bitcast(I32), k_scales.bitcast(I32).rearrange("o f t -> f o t"))
         q_raw = keep.tile([P, PASSES, PACK, NQ], F32, name="q_raw")
         nc.sync.dma_start(q_raw[:], qT[0].rearrange("(g p j) w -> p g j w", g=PASSES, j=PACK))
         key_pool = keep.tile([P, POOL], I32, name="key_pool")
         nc.sync.dma_start(key_pool[:], k_words[0].rearrange("p t b -> p (t b)").bitcast(I32))
 
-        ident = keep.tile([P, P], F32, name="ident")
-        make_identity(nc, ident[:])
         zero_col = keep.tile([P, 1], F32, name="zero_col")
         nc.vector.memset(zero_col[:], 0.0)
-        key_planes = [keep.tile([P, SLOTS], U8, name="key_plane%d" % o, align_bytes=64) for o in range(PASSES)]
-        for plane in key_planes:
-            nc.vector.memset(plane[:].bitcast(I32), 0)
-        nc.vector.memset(token_scale_pool[0 : P - 1, 0 : POOL // 2], 0.0)
+        key_planes = keep.tile([P, PASSES, SLOTS], U8, name="key_planes", align_bytes=64)
+        plane_words = key_planes[:].rearrange("p o n -> p (o n)").bitcast(I32)
+        nc.vector.memset(plane_words, 0)
+        nc.vector.memset(token_scale_pool[0 : P - 1, :], 0.0)
 
         warm = keep.tile([P, 1], F32, name="warm")
         nc.scalar.activation(warm[:], zero_col[:], ACT.Exp)
         neg_sink = keep.tile([P, 1], F32, name="neg_sink")
-        nc.gpsimd.tensor_scalar(neg_sink[:], sink_col[:], -1.0, 0.0, op0=ALU.mult, op1=ALU.add)
+        nc.scalar.activation(neg_sink[:], sink_col[:], ACT.Copy, scale=-1.0)
+        q_grouped = keep.tile([P, PASSES, NQ, PACK], BF16, name="q_grouped", align_bytes=64)
+        nc.scalar.activation(q_grouped[:], q_raw[:].rearrange("p g j w -> p g w j"), ACT.Copy, scale=-1.0)
 
         key_scales = keep.tile([P, SLOTS], U8, name="key_scales")
         nc.vector.tensor_copy(key_scales[:], key_scale_pool[:].indirect(slot_list[:]))
-        for o in reversed(range(PASSES)):
-            for quad in range(4):
-                row = ROW0 + 16 * o + 4 * quad
-                nc.scalar.dma_start(
-                    key_planes[o][32 * quad : 32 * quad + 4, :].bitcast(I32),
-                    key_scales[row : row + 4, :].bitcast(I32),
-                )
-        nc.vector.memset(token_scale_pool[0 : P - 1, POOL // 2 : POOL], 0.0)
-        nc.vector.memset(value_scale_pool[0 : P - 16, :].bitcast(I32), 0)
-        value_plane = keep.tile([P, PAGES * DV], U8, name="value_plane", align_bytes=64)
-        nc.vector.memset(value_plane[:].bitcast(I32), 0)
-        q_grouped = keep.tile([P, PASSES, NQ, PACK], BF16, name="q_grouped", tag="late_values", align_bytes=64)
-        nc.vector.tensor_copy(q_grouped[:], q_raw[:].rearrange("p g j w -> p g w j"))
+        for quad in range(QUADS):
+            nc.sync.dma_start(plane_words[32 * quad : 32 * quad + 4, :], key_scales[8 * quad : 8 * quad + 8, :].bitcast(I32))
+        value_scale_pool = keep.tile([P, POOL_PAGES * DV], U8, name="value_scale_pool")
+        nc.vector.memset(value_scale_pool[:].bitcast(I32), 0)
         token_scales = keep.tile([P, SLOTS], F32, name="token_scales")
         nc.vector.tensor_copy(token_scales[:], token_scale_pool[:].indirect(slot_list[:]))
         q_codes = keep.tile([P, PASSES * NQ], U32, name="q_codes", align_bytes=64)
         q_scales = keep.tile([P, PASSES * NQ], U8, name="q_scales", align_bytes=64)
         nc.vector.quantize_mx(q_codes[:].bitcast(FP8X4), q_scales[:], q_grouped[:].rearrange("p g w j -> p (g w j)"))
-        value_scales = keep.tile([P, PAGES * DV], U8, name="value_scales")
-        nc.vector.tensor_copy(value_scales[:], value_scale_pool[:].indirect(column_list[:]))
 
-        value_pool = keep.tile([P, POOL_PAGES * DV], I32, name="value_pool", tag="late_values", align_bytes=64)
-        nc.scalar.dma_start(
+        value_pool = keep.tile([P, POOL_PAGES * DV], I32, name="value_pool")
+        nc.sync.dma_start(
             value_pool[:].rearrange("p (u e) -> p u e", u=POOL_PAGES),
             v_words.rearrange("u p e r -> p u (e r)").bitcast(I32),
         )
+        column_list = lists.tile([P, PAGES * DV // 16], U16, name="column_list")
+        nc.sync.dma_start(column_list[:], voffs)
+        for quad in range(QUADS):
+            nc.sync.dma_start(
+                value_scale_pool[32 * quad : 32 * quad + 4, :].bitcast(I32).rearrange("f (u e) -> f u e", u=POOL_PAGES),
+                v_scales.bitcast(I32)[:, 4 * quad : 4 * quad + 4, :].rearrange("u f e -> f u e"),
+            )
         slot_scales = []
         for u in range(PAGES):
             spread = keep.tile([P, PACK], F32, name="slot_scales%d" % u)
-            nc.scalar.dma_start(spread[:], token_scales[P - 1 : P, PAGE * u : PAGE * (u + 1)])
+            nc.sync.dma_start(spread[:], token_scales[P - 1 : P, PAGE * u : PAGE * (u + 1)])
             slot_scales.append(spread)
-        for quad in range(4):
-            row = P - 16 + 4 * quad
-            nc.scalar.dma_start(value_plane[32 * quad : 32 * quad + 4, :].bitcast(I32), value_scales[row : row + 4, :].bitcast(I32))
 
         key_pairs = []
         scores = []
 
         def gather_keys(u):
-            pairs = keep.tile([P, PAGE], U32, name="key_pairs%d" % u)
+            pairs = keep.tile([P, PAGE], U32, name="key_pairs%d" % u, tag="pairs%d" % u)
             nc.vector.tensor_copy(pairs[:], key_pool[:].bitcast(U32).indirect(slot_list[:, 32 * u : 32 * (u + 1)]))
             key_pairs.append(pairs)
 
@@ -126,7 +112,7 @@ def tile_attend_pkv4_sink_kernel(tc, qT, k_words, k_scales, v_words, v_scales, v
                     lhsT=q_codes[:, NQ * o : NQ * (o + 1)].bitcast(FP8X4),
                     lhsT_scale=q_scales[:, NQ * o : NQ * (o + 1)],
                     rhs=keys[:, o, :].bitcast(FP4X4),
-                    rhs_scale=key_planes[o][:, PAGE * u : PAGE * (u + 1)],
+                    rhs_scale=key_planes[:, o, PAGE * u : PAGE * (u + 1)],
                     start=(o == 0),
                     stop=(o == PASSES - 1),
                 )
@@ -139,28 +125,29 @@ def tile_attend_pkv4_sink_kernel(tc, qT, k_words, k_scales, v_words, v_scales, v
         score_page(1, [slice(0, 2)])
         score_page(2, [slice(0, 2)])
 
-        neg_scores = []
-        neg_max = neg_sink
-        for u in range(PAGES):
-            negated = keep.tile([NQ, PACK, P], F32, name="neg_scores%d" % u)
-            running = keep.tile([NQ, 1], F32, name="neg_max%d" % u, tag="max%d" % u, align_bytes=64)
-            nc.vector.tensor_scalar(
-                negated[:], scores[u][:].rearrange("q (s t) -> q t s", t=PACK), -1.0, neg_max[:],
-                op0=ALU.mult, op1=ALU.min, accum_out=running[:],
-            )
-            neg_scores.append(negated)
-            neg_max = running
+        ident = keep.tile([P, P], F32, name="ident", tag="pairs%d" % (PAGES - 1))
+        make_identity(nc, ident[:])
 
-        values = keep.tile([P, PAGES * DV], U32, name="values", tag="max%d" % (PAGES - 2), align_bytes=64)
+        clipped = keep.tile([NQ, PAGE], F32, name="clipped")
+        least = [keep.tile([NQ, 1], F32, name="least%d" % u) for u in range(PAGES)]
+        nc.vector.tensor_scalar(clipped[:], scores[0][:], neg_sink[:], None, op0=ALU.min, op1=ALU.min, accum_out=least[0][:])
+        nc.vector.tensor_reduce(least[1][:], scores[1][:], AXIS.X, ALU.min)
+        nc.vector.tensor_scalar(clipped[:], scores[2][:], least[0][:], least[1][:], op0=ALU.min, op1=ALU.min, accum_out=least[2][:])
+        neg_max = least[2]
+
+        values = keep.tile([P, PAGES * DV], U32, name="values", align_bytes=64)
         nc.vector.tensor_copy(values[:], value_pool[:].bitcast(U32).indirect(column_list[:]))
+        value_plane = keep.tile([P, PAGES * DV], U8, name="value_plane", align_bytes=64)
+        nc.vector.tensor_copy(value_plane[:], value_scale_pool[:].indirect(column_list[:]))
 
         pieces = [(0, 0, 2), (0, 2, 4), (1, 0, 4), (2, 0, 2), (2, 2, 4)]
         terms = keep.tile([NQ, len(pieces) + 1], F32, name="terms")
         probs = [keep.tile([NQ, PACK, P], F32, name="probs%d" % u) for u in range(PAGES)]
         turned = [psum.tile([P, PACK, NQ], F32, name="turned_probs%d" % u) for u in range(PAGES)]
         for i, (u, t0, t1) in enumerate(pieces):
+            dealt = scores[u][:].rearrange("q (s t) -> q t s", t=PACK)
             nc.scalar.activation(
-                probs[u][:, t0:t1, :], neg_scores[u][:, t0:t1, :], ACT.Exp, bias=neg_max[:], scale=-1.0, accum_out=terms[:, i : i + 1]
+                probs[u][:, t0:t1, :], dealt[:, t0:t1, :], ACT.Exp, bias=neg_max[:], scale=-1.0, accum_out=terms[:, i : i + 1]
             )
             for t in range(t0, t1):
                 nc.tensor.transpose(turned[u][:, t, :], probs[u][:, t, :], ident[:])
@@ -173,7 +160,7 @@ def tile_attend_pkv4_sink_kernel(tc, qT, k_words, k_scales, v_words, v_scales, v
         sums = [psum.tile([NQ, HALF], F32, name="sums%d" % h) for h in range(2)]
 
         def weigh(u):
-            w_grouped = keep.tile([P, NQ, PACK], BF16, name="w_grouped%d" % u, align_bytes=64)
+            w_grouped = keep.tile([P, NQ, PACK], BF16, name="w_grouped%d" % u, tag="weights%d" % u, align_bytes=64)
             nc.vector.tensor_tensor(
                 w_grouped[:], turned[u][:].rearrange("p t q -> p q t"),
                 slot_scales[u][:].unsqueeze(1).to_broadcast([P, NQ, PACK]), ALU.mult,
@@ -201,7 +188,7 @@ def tile_attend_pkv4_sink_kernel(tc, qT, k_words, k_scales, v_words, v_scales, v
         multiply(0)
         weigh(2)
         multiply(1)
-        inverse = keep.tile([NQ, 1], F32, name="inverse")
+        inverse = keep.tile([NQ, 1], F32, name="inverse", tag="weights0", align_bytes=64)
         nc.vector.reciprocal(inverse[:], total[:])
         multiply(2)
 

@@ -23,6 +23,9 @@ PAGES = SLOTS // PAGE
 POOL_PAGES = POOL // PAGE
 PASSES = D // PAGE
 QUADS = 4
+W_BYTES = 2 * NQ * PACK
+ROW0 = P - 16 * PASSES
+EARLY = 3 * POOL // 4
 HALF = DV // 2
 FLOPS = 2 * NQ * SLOTS * (D + DV)
 
@@ -32,41 +35,46 @@ def tile_attend_pkv4_sink_kernel(tc, qT, k_words, k_scales, v_words, v_scales, v
     with ExitStack() as ctx:
         lists = ctx.enter_context(tc.tile_pool(name="lists", bufs=1))
         keep = ctx.enter_context(tc.tile_pool(name="keep", bufs=1))
+        late = ctx.enter_context(tc.tile_pool(name="late", bufs=1))
         psum = ctx.enter_context(tc.psum_pool(name="psum", bufs=1))
 
         slot_list = lists.tile([P, SLOTS // 16], U16, name="slot_list")
         nc.sync.dma_start(slot_list[:], offs)
-        sink_col = keep.tile([P, 1], F32, name="sink_col")
-        nc.scalar.dma_start(sink_col[:], sink[0])
         token_scale_pool = keep.tile([P, POOL], F32, name="token_scale_pool")
-        nc.sync.dma_start(token_scale_pool[P - 1 : P, :], vs[0:1, :])
-        key_scale_pool = keep.tile([P, POOL], U8, name="key_scale_pool")
-        nc.vector.memset(key_scale_pool[:].bitcast(I32), 0)
-        nc.scalar.dma_start(key_scale_pool[0 : 16 * PASSES, :].bitcast(I32), k_scales.bitcast(I32).rearrange("o f t -> f o t"))
+        nc.scalar.dma_start(token_scale_pool[P - 1 : P, :], vs[0:1, :])
+        key_scale_pool = keep.tile([P, POOL], U8, name="key_scale_pool", tag="pools")
+        nc.vector.memset(key_scale_pool[0:ROW0, :].bitcast(I32), 0)
+        nc.sync.dma_start(key_scale_pool[ROW0:P, :].bitcast(I32), k_scales.bitcast(I32).rearrange("o f t -> f o t"))
         q_raw = keep.tile([P, PASSES, PACK, NQ], F32, name="q_raw")
         nc.sync.dma_start(q_raw[:], qT[0].rearrange("(g p j) w -> p g j w", g=PASSES, j=PACK))
         key_pool = keep.tile([P, POOL], I32, name="key_pool")
         nc.sync.dma_start(key_pool[:], k_words[0].rearrange("p t b -> p (t b)").bitcast(I32))
+        sink_col = keep.tile([P, 1], F32, name="sink_col")
+        nc.scalar.dma_start(sink_col[:], sink[0])
 
+        ident = keep.tile([P, P], F32, name="ident")
+        make_identity(nc, ident[:])
         zero_col = keep.tile([P, 1], F32, name="zero_col")
         nc.vector.memset(zero_col[:], 0.0)
         key_planes = keep.tile([P, PASSES, SLOTS], U8, name="key_planes", align_bytes=64)
         plane_words = key_planes[:].rearrange("p o n -> p (o n)").bitcast(I32)
         nc.vector.memset(plane_words, 0)
-        nc.vector.memset(token_scale_pool[0 : P - 1, :], 0.0)
+        nc.vector.memset(token_scale_pool[0 : P - 1, 0:EARLY], 0.0)
 
         warm = keep.tile([P, 1], F32, name="warm")
         nc.scalar.activation(warm[:], zero_col[:], ACT.Exp)
-        neg_sink = keep.tile([P, 1], F32, name="neg_sink")
-        nc.scalar.activation(neg_sink[:], sink_col[:], ACT.Copy, scale=-1.0)
         q_grouped = keep.tile([P, PASSES, NQ, PACK], BF16, name="q_grouped", align_bytes=64)
         nc.scalar.activation(q_grouped[:], q_raw[:].rearrange("p g j w -> p g w j"), ACT.Copy, scale=-1.0)
+        neg_sink = keep.tile([P, 1], F32, name="neg_sink")
+        nc.scalar.activation(neg_sink[:], sink_col[:], ACT.Copy, scale=-1.0)
 
         key_scales = keep.tile([P, SLOTS], U8, name="key_scales")
         nc.vector.tensor_copy(key_scales[:], key_scale_pool[:].indirect(slot_list[:]))
         for quad in range(QUADS):
-            nc.sync.dma_start(plane_words[32 * quad : 32 * quad + 4, :], key_scales[8 * quad : 8 * quad + 8, :].bitcast(I32))
-        value_scale_pool = keep.tile([P, POOL_PAGES * DV], U8, name="value_scale_pool")
+            row = ROW0 + 8 * quad
+            nc.sync.dma_start(plane_words[32 * quad : 32 * quad + 4, :], key_scales[row : row + 8, :].bitcast(I32))
+        nc.vector.memset(token_scale_pool[0 : P - 1, EARLY:POOL], 0.0)
+        value_scale_pool = late.tile([P, POOL_PAGES * DV], U8, name="value_scale_pool", offset=W_BYTES // 2, align_bytes=64)
         nc.vector.memset(value_scale_pool[:].bitcast(I32), 0)
         token_scales = keep.tile([P, SLOTS], F32, name="token_scales")
         nc.vector.tensor_copy(token_scales[:], token_scale_pool[:].indirect(slot_list[:]))
@@ -74,23 +82,28 @@ def tile_attend_pkv4_sink_kernel(tc, qT, k_words, k_scales, v_words, v_scales, v
         q_scales = keep.tile([P, PASSES * NQ], U8, name="q_scales", align_bytes=64)
         nc.vector.quantize_mx(q_codes[:].bitcast(FP8X4), q_scales[:], q_grouped[:].rearrange("p g w j -> p (g w j)"))
 
-        value_pool = keep.tile([P, POOL_PAGES * DV], I32, name="value_pool")
+        column_list = lists.tile([P, PAGES * DV // 16], U16, name="column_list")
+        nc.sync.dma_start(column_list[:], voffs)
+        slot_scales = []
+
+        def spread_scales(u):
+            spread = keep.tile([P, PACK], F32, name="slot_scales%d" % u)
+            nc.sync.dma_start(spread[:], token_scales[P - 1 : P, PAGE * u : PAGE * (u + 1)])
+            slot_scales.append(spread)
+
+        spread_scales(0)
+        value_pool = keep.tile([P, POOL_PAGES * DV], I32, name="value_pool", tag="pools")
         nc.sync.dma_start(
             value_pool[:].rearrange("p (u e) -> p u e", u=POOL_PAGES),
             v_words.rearrange("u p e r -> p u (e r)").bitcast(I32),
         )
-        column_list = lists.tile([P, PAGES * DV // 16], U16, name="column_list")
-        nc.sync.dma_start(column_list[:], voffs)
+        spread_scales(1)
+        spread_scales(2)
         for quad in range(QUADS):
             nc.sync.dma_start(
                 value_scale_pool[32 * quad : 32 * quad + 4, :].bitcast(I32).rearrange("f (u e) -> f u e", u=POOL_PAGES),
                 v_scales.bitcast(I32)[:, 4 * quad : 4 * quad + 4, :].rearrange("u f e -> f u e"),
             )
-        slot_scales = []
-        for u in range(PAGES):
-            spread = keep.tile([P, PACK], F32, name="slot_scales%d" % u)
-            nc.sync.dma_start(spread[:], token_scales[P - 1 : P, PAGE * u : PAGE * (u + 1)])
-            slot_scales.append(spread)
 
         key_pairs = []
         scores = []
@@ -125,15 +138,14 @@ def tile_attend_pkv4_sink_kernel(tc, qT, k_words, k_scales, v_words, v_scales, v
         score_page(1, [slice(0, 2)])
         score_page(2, [slice(0, 2)])
 
-        ident = keep.tile([P, P], F32, name="ident", tag="pairs%d" % (PAGES - 1))
-        make_identity(nc, ident[:])
-
-        clipped = keep.tile([NQ, PAGE], F32, name="clipped")
+        dealt = [scores[u][:].rearrange("q (s t) -> q t s", t=PACK) for u in range(PAGES)]
         least = [keep.tile([NQ, 1], F32, name="least%d" % u) for u in range(PAGES)]
-        nc.vector.tensor_scalar(clipped[:], scores[0][:], neg_sink[:], None, op0=ALU.min, op1=ALU.min, accum_out=least[0][:])
-        nc.vector.tensor_reduce(least[1][:], scores[1][:], AXIS.X, ALU.min)
-        nc.vector.tensor_scalar(clipped[:], scores[2][:], least[0][:], least[1][:], op0=ALU.min, op1=ALU.min, accum_out=least[2][:])
+        copies = [keep.tile([NQ, PACK, P], F32, name="neg_scores%d" % u) for u in range(PAGES)]
+        nc.vector.tensor_scalar(copies[0][:], dealt[0], 1.0, neg_sink[:], op0=ALU.mult, op1=ALU.min, accum_out=least[0][:])
+        nc.vector.tensor_scalar(copies[1][:], dealt[1], 1.0, None, op0=ALU.mult, op1=ALU.min, accum_out=least[1][:])
+        nc.vector.tensor_scalar(copies[2][:], dealt[2], least[0][:], least[1][:], op0=ALU.min, op1=ALU.min, accum_out=least[2][:])
         neg_max = least[2]
+        neg_scores = [copies[0][:], copies[1][:], dealt[2]]
 
         values = keep.tile([P, PAGES * DV], U32, name="values", align_bytes=64)
         nc.vector.tensor_copy(values[:], value_pool[:].bitcast(U32).indirect(column_list[:]))
@@ -145,9 +157,8 @@ def tile_attend_pkv4_sink_kernel(tc, qT, k_words, k_scales, v_words, v_scales, v
         probs = [keep.tile([NQ, PACK, P], F32, name="probs%d" % u) for u in range(PAGES)]
         turned = [psum.tile([P, PACK, NQ], F32, name="turned_probs%d" % u) for u in range(PAGES)]
         for i, (u, t0, t1) in enumerate(pieces):
-            dealt = scores[u][:].rearrange("q (s t) -> q t s", t=PACK)
             nc.scalar.activation(
-                probs[u][:, t0:t1, :], dealt[:, t0:t1, :], ACT.Exp, bias=neg_max[:], scale=-1.0, accum_out=terms[:, i : i + 1]
+                probs[u][:, t0:t1, :], neg_scores[u][:, t0:t1, :], ACT.Exp, bias=neg_max[:], scale=-1.0, accum_out=terms[:, i : i + 1]
             )
             for t in range(t0, t1):
                 nc.tensor.transpose(turned[u][:, t, :], probs[u][:, t, :], ident[:])
@@ -160,7 +171,7 @@ def tile_attend_pkv4_sink_kernel(tc, qT, k_words, k_scales, v_words, v_scales, v
         sums = [psum.tile([NQ, HALF], F32, name="sums%d" % h) for h in range(2)]
 
         def weigh(u):
-            w_grouped = keep.tile([P, NQ, PACK], BF16, name="w_grouped%d" % u, tag="weights%d" % u, align_bytes=64)
+            w_grouped = late.tile([P, NQ, PACK], BF16, name="w_grouped%d" % u, offset=W_BYTES * u, align_bytes=64)
             nc.vector.tensor_tensor(
                 w_grouped[:], turned[u][:].rearrange("p t q -> p q t"),
                 slot_scales[u][:].unsqueeze(1).to_broadcast([P, NQ, PACK]), ALU.mult,
@@ -188,7 +199,7 @@ def tile_attend_pkv4_sink_kernel(tc, qT, k_words, k_scales, v_words, v_scales, v
         multiply(0)
         weigh(2)
         multiply(1)
-        inverse = keep.tile([NQ, 1], F32, name="inverse", tag="weights0", align_bytes=64)
+        inverse = late.tile([NQ, 1], F32, name="inverse", offset=0, align_bytes=64)
         nc.vector.reciprocal(inverse[:], total[:])
         multiply(2)
 

@@ -54,7 +54,7 @@ def tile_attend_pkv4_sink_kernel(tc, qT, k_words, k_scales, v_words, v_scales, v
 
         ident = keep.tile([P, P], F32, name="ident")
         make_identity(nc, ident[:])
-        zero_col = keep.tile([P, 1], F32, name="zero_col")
+        zero_col = late.tile([P, 1], F32, name="zero_col", offset=W_BYTES, align_bytes=64)
         nc.vector.memset(zero_col[:], 0.0)
         key_planes = keep.tile([P, PASSES, SLOTS], U8, name="key_planes", align_bytes=64)
         plane_words = key_planes[:].rearrange("p o n -> p (o n)").bitcast(I32)
@@ -73,9 +73,9 @@ def tile_attend_pkv4_sink_kernel(tc, qT, k_words, k_scales, v_words, v_scales, v
         for quad in range(QUADS):
             row = ROW0 + 8 * quad
             nc.sync.dma_start(plane_words[32 * quad : 32 * quad + 4, :], key_scales[row : row + 8, :].bitcast(I32))
-        nc.vector.memset(token_scale_pool[0 : P - 1, EARLY:POOL], 0.0)
+        nc.gpsimd.memset(token_scale_pool[0 : P - 1, EARLY - 8 : POOL], 0.0)
         value_scale_pool = late.tile([P, POOL_PAGES * DV], U8, name="value_scale_pool", offset=W_BYTES // 2, align_bytes=64)
-        nc.vector.memset(value_scale_pool[:].bitcast(I32), 0)
+        nc.gpsimd.memset(value_scale_pool[:].bitcast(I32), 0)
         token_scales = keep.tile([P, SLOTS], F32, name="token_scales")
         nc.vector.tensor_copy(token_scales[:], token_scale_pool[:].indirect(slot_list[:]))
         q_codes = keep.tile([P, PASSES * NQ], U32, name="q_codes", align_bytes=64)

@@ -24,8 +24,8 @@ POOL_PAGES = POOL // PAGE
 PASSES = D // PAGE
 QUADS = 4
 W_BYTES = 2 * NQ * PACK
-ROW0 = P - 16 * PASSES
-EARLY = 3 * POOL // 4
+EARLY = 1536
+BESIDE = 3040
 HALF = DV // 2
 FLOPS = 2 * NQ * SLOTS * (D + DV)
 
@@ -43,26 +43,21 @@ def tile_attend_pkv4_sink_kernel(tc, qT, k_words, k_scales, v_words, v_scales, v
         token_scale_pool = keep.tile([P, POOL], F32, name="token_scale_pool")
         nc.scalar.dma_start(token_scale_pool[P - 1 : P, :], vs[0:1, :])
         key_scale_pool = keep.tile([P, POOL], U8, name="key_scale_pool", tag="pools")
-        nc.vector.memset(key_scale_pool[0:ROW0, :].bitcast(I32), 0)
-        nc.sync.dma_start(key_scale_pool[ROW0:P, :].bitcast(I32), k_scales.bitcast(I32).rearrange("o f t -> f o t"))
-        q_raw = keep.tile([P, PASSES, PACK, NQ], F32, name="q_raw")
+        nc.vector.memset(key_scale_pool[32:64, :].bitcast(I32), 0)
+        nc.vector.memset(key_scale_pool[64:P, :].bitcast(I32), 0)
+        nc.sync.dma_start(key_scale_pool[0:32, :].bitcast(I32), k_scales.bitcast(I32).rearrange("o f t -> f o t"))
+        q_raw = late.tile([P, PASSES, PACK, NQ], F32, name="q_raw", offset=W_BYTES // 2, align_bytes=64)
         nc.sync.dma_start(q_raw[:], qT[0].rearrange("(g p j) w -> p g j w", g=PASSES, j=PACK))
         key_pool = keep.tile([P, POOL], I32, name="key_pool")
         nc.sync.dma_start(key_pool[:], k_words[0].rearrange("p t b -> p (t b)").bitcast(I32))
         sink_col = keep.tile([P, 1], F32, name="sink_col")
         nc.scalar.dma_start(sink_col[:], sink[0])
 
-        ident = keep.tile([P, P], F32, name="ident")
-        make_identity(nc, ident[:])
-        zero_col = late.tile([P, 1], F32, name="zero_col", offset=W_BYTES, align_bytes=64)
-        nc.vector.memset(zero_col[:], 0.0)
         key_planes = keep.tile([P, PASSES, SLOTS], U8, name="key_planes", align_bytes=64)
         plane_words = key_planes[:].rearrange("p o n -> p (o n)").bitcast(I32)
         nc.vector.memset(plane_words, 0)
         nc.vector.memset(token_scale_pool[0 : P - 1, 0:EARLY], 0.0)
 
-        warm = keep.tile([P, 1], F32, name="warm")
-        nc.scalar.activation(warm[:], zero_col[:], ACT.Exp)
         q_grouped = keep.tile([P, PASSES, NQ, PACK], BF16, name="q_grouped", align_bytes=64)
         nc.scalar.activation(q_grouped[:], q_raw[:].rearrange("p g j w -> p g w j"), ACT.Copy, scale=-1.0)
         neg_sink = keep.tile([P, 1], F32, name="neg_sink")
@@ -71,11 +66,14 @@ def tile_attend_pkv4_sink_kernel(tc, qT, k_words, k_scales, v_words, v_scales, v
         key_scales = keep.tile([P, SLOTS], U8, name="key_scales")
         nc.vector.tensor_copy(key_scales[:], key_scale_pool[:].indirect(slot_list[:]))
         for quad in range(QUADS):
-            row = ROW0 + 8 * quad
+            row = 8 * quad
             nc.sync.dma_start(plane_words[32 * quad : 32 * quad + 4, :], key_scales[row : row + 8, :].bitcast(I32))
-        nc.gpsimd.memset(token_scale_pool[0 : P - 1, EARLY - 8 : POOL], 0.0)
+        nc.gpsimd.memset(token_scale_pool[0 : P - 1, EARLY - 8 : BESIDE], 0.0)
+        nc.vector.memset(token_scale_pool[0 : P - 1, BESIDE:POOL], 0.0)
         value_scale_pool = late.tile([P, POOL_PAGES * DV], U8, name="value_scale_pool", offset=W_BYTES // 2, align_bytes=64)
         nc.gpsimd.memset(value_scale_pool[:].bitcast(I32), 0)
+        ident = late.tile([P, P], F32, name="ident", offset=PAGES * W_BYTES, align_bytes=64)
+        make_identity(nc, ident[:])
         token_scales = keep.tile([P, SLOTS], F32, name="token_scales")
         nc.vector.tensor_copy(token_scales[:], token_scale_pool[:].indirect(slot_list[:]))
         q_codes = keep.tile([P, PASSES * NQ], U32, name="q_codes", align_bytes=64)
@@ -152,7 +150,7 @@ def tile_attend_pkv4_sink_kernel(tc, qT, k_words, k_scales, v_words, v_scales, v
         value_plane = keep.tile([P, PAGES * DV], U8, name="value_plane", align_bytes=64)
         nc.vector.tensor_copy(value_plane[:], value_scale_pool[:].indirect(column_list[:]))
 
-        pieces = [(0, 0, 2), (0, 2, 4), (1, 0, 4), (2, 0, 2), (2, 2, 4)]
+        pieces = [(u, t, t + 2) for u in range(PAGES) for t in (0, 2)]
         terms = keep.tile([NQ, len(pieces) + 1], F32, name="terms")
         probs = [keep.tile([NQ, PACK, P], F32, name="probs%d" % u) for u in range(PAGES)]
         turned = [psum.tile([P, PACK, NQ], F32, name="turned_probs%d" % u) for u in range(PAGES)]

@@ -24,8 +24,8 @@ POOL_PAGES = POOL // PAGE
 PASSES = D // PAGE
 QUADS = 4
 W_BYTES = 2 * NQ * PACK
-EARLY = 1536
-BESIDE = 3040
+ROW0 = P - 16 * PASSES
+EARLY = 3 * POOL // 4
 HALF = DV // 2
 FLOPS = 2 * NQ * SLOTS * (D + DV)
 
@@ -43,9 +43,8 @@ def tile_attend_pkv4_sink_kernel(tc, qT, k_words, k_scales, v_words, v_scales, v
         token_scale_pool = keep.tile([P, POOL], F32, name="token_scale_pool")
         nc.scalar.dma_start(token_scale_pool[P - 1 : P, :], vs[0:1, :])
         key_scale_pool = keep.tile([P, POOL], U8, name="key_scale_pool", tag="pools")
-        nc.vector.memset(key_scale_pool[32:64, :].bitcast(I32), 0)
-        nc.vector.memset(key_scale_pool[64:P, :].bitcast(I32), 0)
-        nc.sync.dma_start(key_scale_pool[0:32, :].bitcast(I32), k_scales.bitcast(I32).rearrange("o f t -> f o t"))
+        nc.vector.memset(key_scale_pool[0:ROW0, :].bitcast(I32), 0)
+        nc.sync.dma_start(key_scale_pool[ROW0:P, :].bitcast(I32), k_scales.bitcast(I32).rearrange("o f t -> f o t"))
         q_raw = late.tile([P, PASSES, PACK, NQ], F32, name="q_raw", offset=W_BYTES // 2, align_bytes=64)
         nc.sync.dma_start(q_raw[:], qT[0].rearrange("(g p j) w -> p g j w", g=PASSES, j=PACK))
         key_pool = keep.tile([P, POOL], I32, name="key_pool")
@@ -66,10 +65,9 @@ def tile_attend_pkv4_sink_kernel(tc, qT, k_words, k_scales, v_words, v_scales, v
         key_scales = keep.tile([P, SLOTS], U8, name="key_scales")
         nc.vector.tensor_copy(key_scales[:], key_scale_pool[:].indirect(slot_list[:]))
         for quad in range(QUADS):
-            row = 8 * quad
+            row = ROW0 + 8 * quad
             nc.sync.dma_start(plane_words[32 * quad : 32 * quad + 4, :], key_scales[row : row + 8, :].bitcast(I32))
-        nc.gpsimd.memset(token_scale_pool[0 : P - 1, EARLY - 8 : BESIDE], 0.0)
-        nc.vector.memset(token_scale_pool[0 : P - 1, BESIDE:POOL], 0.0)
+        nc.gpsimd.memset(token_scale_pool[0 : P - 1, EARLY - 8 : POOL], 0.0)
         value_scale_pool = late.tile([P, POOL_PAGES * DV], U8, name="value_scale_pool", offset=W_BYTES // 2, align_bytes=64)
         nc.gpsimd.memset(value_scale_pool[:].bitcast(I32), 0)
         ident = late.tile([P, P], F32, name="ident", offset=PAGES * W_BYTES, align_bytes=64)
@@ -80,28 +78,23 @@ def tile_attend_pkv4_sink_kernel(tc, qT, k_words, k_scales, v_words, v_scales, v
         q_scales = keep.tile([P, PASSES * NQ], U8, name="q_scales", align_bytes=64)
         nc.vector.quantize_mx(q_codes[:].bitcast(FP8X4), q_scales[:], q_grouped[:].rearrange("p g w j -> p (g w j)"))
 
-        column_list = lists.tile([P, PAGES * DV // 16], U16, name="column_list")
-        nc.sync.dma_start(column_list[:], voffs)
-        slot_scales = []
-
-        def spread_scales(u):
-            spread = keep.tile([P, PACK], F32, name="slot_scales%d" % u)
-            nc.sync.dma_start(spread[:], token_scales[P - 1 : P, PAGE * u : PAGE * (u + 1)])
-            slot_scales.append(spread)
-
-        spread_scales(0)
         value_pool = keep.tile([P, POOL_PAGES * DV], I32, name="value_pool", tag="pools")
         nc.sync.dma_start(
             value_pool[:].rearrange("p (u e) -> p u e", u=POOL_PAGES),
             v_words.rearrange("u p e r -> p u (e r)").bitcast(I32),
         )
-        spread_scales(1)
-        spread_scales(2)
+        column_list = lists.tile([P, PAGES * DV // 16], U16, name="column_list")
+        nc.sync.dma_start(column_list[:], voffs)
         for quad in range(QUADS):
             nc.sync.dma_start(
                 value_scale_pool[32 * quad : 32 * quad + 4, :].bitcast(I32).rearrange("f (u e) -> f u e", u=POOL_PAGES),
                 v_scales.bitcast(I32)[:, 4 * quad : 4 * quad + 4, :].rearrange("u f e -> f u e"),
             )
+        slot_scales = []
+        for u in range(PAGES):
+            spread = keep.tile([P, PACK], F32, name="slot_scales%d" % u)
+            nc.sync.dma_start(spread[:], token_scales[P - 1 : P, PAGE * u : PAGE * (u + 1)])
+            slot_scales.append(spread)
 
         key_pairs = []
         scores = []

@@ -38,13 +38,13 @@ def tile_attend_pkv4_sink_kernel(tc, qT, k_words, k_scales, v_words, v_scales, v
         late = ctx.enter_context(tc.tile_pool(name="late", bufs=1))
         psum = ctx.enter_context(tc.psum_pool(name="psum", bufs=1))
 
-        slot_list = lists.tile([P, SLOTS // 16], U16, name="slot_list")
-        nc.sync.dma_start(slot_list[:], offs)
         token_scale_pool = keep.tile([P, POOL], F32, name="token_scale_pool")
         nc.scalar.dma_start(token_scale_pool[P - 1 : P, :], vs[0:1, :])
         key_scale_pool = keep.tile([P, POOL], U8, name="key_scale_pool", tag="pools")
         nc.vector.memset(key_scale_pool[0:ROW0, :].bitcast(I32), 0)
         nc.sync.dma_start(key_scale_pool[ROW0:P, :].bitcast(I32), k_scales.bitcast(I32).rearrange("o f t -> f o t"))
+        slot_list = lists.tile([P, SLOTS // 16], U16, name="slot_list")
+        nc.sync.dma_start(slot_list[:], offs)
         q_raw = late.tile([P, PASSES, PACK, NQ], F32, name="q_raw", offset=W_BYTES // 2, align_bytes=64)
         nc.sync.dma_start(q_raw[:], qT[0].rearrange("(g p j) w -> p g j w", g=PASSES, j=PACK))
         key_pool = keep.tile([P, POOL], I32, name="key_pool")
@@ -54,8 +54,10 @@ def tile_attend_pkv4_sink_kernel(tc, qT, k_words, k_scales, v_words, v_scales, v
 
         key_planes = keep.tile([P, PASSES, SLOTS], U8, name="key_planes", align_bytes=64)
         plane_words = key_planes[:].rearrange("p o n -> p (o n)").bitcast(I32)
-        nc.vector.memset(plane_words, 0)
         nc.vector.memset(token_scale_pool[0 : P - 1, 0:EARLY], 0.0)
+        nc.gpsimd.memset(token_scale_pool[0 : P - 1, EARLY - 8 : POOL], 0.0)
+        nc.vector.memset(plane_words[:, 0:16], 0)
+        nc.gpsimd.memset(plane_words[:, 8 : PASSES * SLOTS // 4], 0)
 
         q_grouped = keep.tile([P, PASSES, NQ, PACK], BF16, name="q_grouped", align_bytes=64)
         nc.scalar.activation(q_grouped[:], q_raw[:].rearrange("p g j w -> p g w j"), ACT.Copy, scale=-1.0)
@@ -67,7 +69,6 @@ def tile_attend_pkv4_sink_kernel(tc, qT, k_words, k_scales, v_words, v_scales, v
         for quad in range(QUADS):
             row = ROW0 + 8 * quad
             nc.sync.dma_start(plane_words[32 * quad : 32 * quad + 4, :], key_scales[row : row + 8, :].bitcast(I32))
-        nc.gpsimd.memset(token_scale_pool[0 : P - 1, EARLY - 8 : POOL], 0.0)
         value_scale_pool = late.tile([P, POOL_PAGES * DV], U8, name="value_scale_pool", offset=W_BYTES // 2, align_bytes=64)
         nc.gpsimd.memset(value_scale_pool[:].bitcast(I32), 0)
         ident = late.tile([P, P], F32, name="ident", offset=PAGES * W_BYTES, align_bytes=64)
@@ -126,7 +127,7 @@ def tile_attend_pkv4_sink_kernel(tc, qT, k_words, k_scales, v_words, v_scales, v
         gather_keys(1)
         score_page(0, [slice(0, 1), slice(1, 2)])
         gather_keys(2)
-        score_page(1, [slice(0, 2)])
+        score_page(1, [slice(0, 1), slice(1, 2)])
         score_page(2, [slice(0, 2)])
 
         dealt = [scores[u][:].rearrange("q (s t) -> q t s", t=PACK) for u in range(PAGES)]

@@ -24,6 +24,7 @@ POOL_PAGES = POOL // PAGE
 PASSES = D // PAGE
 QUADS = 4
 W_BYTES = 2 * NQ * PACK
+SECOND = 4 * W_BYTES
 ROW0 = P - 16 * PASSES
 EARLY = 3 * POOL // 4
 HALF = DV // 2
@@ -45,10 +46,15 @@ def tile_attend_pkv4_sink_kernel(tc, qT, k_words, k_scales, v_words, v_scales, v
         nc.sync.dma_start(key_scale_pool[ROW0:P, :].bitcast(I32), k_scales.bitcast(I32).rearrange("o f t -> f o t"))
         slot_list = lists.tile([P, SLOTS // 16], U16, name="slot_list")
         nc.sync.dma_start(slot_list[:], offs)
-        q_raw = late.tile([P, PASSES, PACK, NQ], F32, name="q_raw", offset=W_BYTES // 2, align_bytes=64)
-        nc.sync.dma_start(q_raw[:], qT[0].rearrange("(g p j) w -> p g j w", g=PASSES, j=PACK))
+        q_rows = qT[0].rearrange("(g p j) w -> g p j w", g=PASSES, j=PACK)
+        q_raw = [
+            late.tile([P, PACK, NQ], F32, name="q_raw0", offset=3 * W_BYTES // 2, align_bytes=64),
+            late.tile([P, PACK, NQ], F32, name="q_raw1", offset=SECOND + W_BYTES, align_bytes=64),
+        ]
+        nc.sync.dma_start(q_raw[0][:], q_rows[0])
         key_pool = keep.tile([P, POOL], I32, name="key_pool")
         nc.sync.dma_start(key_pool[:], k_words[0].rearrange("p t b -> p (t b)").bitcast(I32))
+        nc.sync.dma_start(q_raw[1][:], q_rows[1])
         sink_col = keep.tile([P, 1], F32, name="sink_col")
         nc.scalar.dma_start(sink_col[:], sink[0])
 
@@ -59,12 +65,13 @@ def tile_attend_pkv4_sink_kernel(tc, qT, k_words, k_scales, v_words, v_scales, v
         nc.vector.memset(plane_words[:, 0:16], 0)
         nc.gpsimd.memset(plane_words[:, 8 : PASSES * SLOTS // 4], 0)
 
-        q_grouped = keep.tile([P, PASSES, NQ, PACK], BF16, name="q_grouped", align_bytes=64)
-        nc.scalar.activation(q_grouped[:], q_raw[:].rearrange("p g j w -> p g w j"), ACT.Copy, scale=-1.0)
+        q_grouped = [keep.tile([P, NQ, PACK], BF16, name="q_grouped%d" % o, align_bytes=64) for o in range(PASSES)]
+        nc.scalar.activation(q_grouped[0][:], q_raw[0][:].rearrange("p j w -> p w j"), ACT.Copy, scale=-1.0)
         neg_sink = keep.tile([P, 1], F32, name="neg_sink")
         nc.scalar.activation(neg_sink[:], sink_col[:], ACT.Copy, scale=-1.0)
+        nc.scalar.activation(q_grouped[1][:], q_raw[1][:].rearrange("p j w -> p w j"), ACT.Copy, scale=-1.0)
 
-        key_scales = keep.tile([P, SLOTS], U8, name="key_scales")
+        key_scales = keep.tile([P, SLOTS], U8, name="key_scales", align_bytes=64)
         nc.vector.tensor_copy(key_scales[:], key_scale_pool[:].indirect(slot_list[:]))
         for quad in range(QUADS):
             row = ROW0 + 8 * quad
@@ -75,9 +82,13 @@ def tile_attend_pkv4_sink_kernel(tc, qT, k_words, k_scales, v_words, v_scales, v
         make_identity(nc, ident[:])
         token_scales = keep.tile([P, SLOTS], F32, name="token_scales")
         nc.vector.tensor_copy(token_scales[:], token_scale_pool[:].indirect(slot_list[:]))
-        q_codes = keep.tile([P, PASSES * NQ], U32, name="q_codes", align_bytes=64)
-        q_scales = keep.tile([P, PASSES * NQ], U8, name="q_scales", align_bytes=64)
-        nc.vector.quantize_mx(q_codes[:].bitcast(FP8X4), q_scales[:], q_grouped[:].rearrange("p g w j -> p (g w j)"))
+        q_codes = [keep.tile([P, NQ], U32, name="q_codes%d" % o, align_bytes=64) for o in range(PASSES)]
+        q_scales = [keep.tile([P, NQ], U8, name="q_scales%d" % o, align_bytes=64) for o in range(PASSES)]
+
+        def quantize_queries(o):
+            nc.vector.quantize_mx(q_codes[o][:].bitcast(FP8X4), q_scales[o][:], q_grouped[o][:].rearrange("p w j -> p (w j)"))
+
+        quantize_queries(0)
 
         value_pool = keep.tile([P, POOL_PAGES * DV], I32, name="value_pool", tag="pools")
         nc.sync.dma_start(
@@ -101,22 +112,33 @@ def tile_attend_pkv4_sink_kernel(tc, qT, k_words, k_scales, v_words, v_scales, v
         scores = []
 
         def gather_keys(u):
-            pairs = keep.tile([P, PAGE], U32, name="key_pairs%d" % u, tag="pairs%d" % u)
+            if u == PAGES - 1:
+                pairs = late.tile([P, PAGE], U32, name="key_pairs%d" % u, offset=SECOND, align_bytes=64)
+            else:
+                pairs = keep.tile([P, PAGE], U32, name="key_pairs%d" % u, align_bytes=64)
             nc.vector.tensor_copy(pairs[:], key_pool[:].bitcast(U32).indirect(slot_list[:, 32 * u : 32 * (u + 1)]))
             key_pairs.append(pairs)
 
-        def score_page(u, copies):
-            keys = keep.tile([P, PASSES, PAGE], U16, name="keys%d" % u, align_bytes=64)
+        keys = []
+
+        def part_keys(u, copies):
+            if u == 1:
+                parted = late.tile([P, PASSES, PAGE], U16, name="keys%d" % u, offset=SECOND + 2 * W_BYTES, align_bytes=64)
+            else:
+                parted = keep.tile([P, PASSES, PAGE], U16, name="keys%d" % u, align_bytes=64)
             halves = key_pairs[u][:].bitcast(U16).rearrange("p (n o) -> p o n", o=PASSES)
             for part in copies:
-                nc.vector.tensor_copy(keys[:, part, :], halves[:, part, :])
+                nc.vector.tensor_copy(parted[:, part, :], halves[:, part, :])
+            keys.append(parted)
+
+        def score_page(u):
             bank = psum.tile([NQ, PAGE], F32, name="scores%d" % u)
             for o in range(PASSES):
                 nc.tensor.matmul_mx(
                     bank[:],
-                    lhsT=q_codes[:, NQ * o : NQ * (o + 1)].bitcast(FP8X4),
-                    lhsT_scale=q_scales[:, NQ * o : NQ * (o + 1)],
-                    rhs=keys[:, o, :].bitcast(FP4X4),
+                    lhsT=q_codes[o][:].bitcast(FP8X4),
+                    lhsT_scale=q_scales[o][:],
+                    rhs=keys[u][:, o, :].bitcast(FP4X4),
                     rhs_scale=key_planes[:, o, PAGE * u : PAGE * (u + 1)],
                     start=(o == 0),
                     stop=(o == PASSES - 1),
@@ -124,11 +146,26 @@ def tile_attend_pkv4_sink_kernel(tc, qT, k_words, k_scales, v_words, v_scales, v
             scores.append(bank)
 
         gather_keys(0)
+        idle_bank = psum.tile([NQ, PAGE], F32, name="idle_bank", tag="turned%d" % (PAGES - 1))
+        for columns in (PAGE, NQ):
+            nc.tensor.matmul_mx(
+                idle_bank[:, 0:columns],
+                lhsT=q_codes[0][:].bitcast(FP8X4),
+                lhsT_scale=q_scales[0][:],
+                rhs=key_pairs[0][:].bitcast(U16)[:, 0:columns].bitcast(FP4X4),
+                rhs_scale=key_scales[:, 0:columns],
+                start=True,
+                stop=True,
+            )
         gather_keys(1)
-        score_page(0, [slice(0, 1), slice(1, 2)])
+        part_keys(0, [slice(0, 1), slice(1, 2)])
+        quantize_queries(1)
+        score_page(0)
         gather_keys(2)
-        score_page(1, [slice(0, 1), slice(1, 2)])
-        score_page(2, [slice(0, 2)])
+        part_keys(1, [slice(0, 1), slice(1, 2)])
+        score_page(1)
+        part_keys(2, [slice(0, 2)])
+        score_page(2)
 
         dealt = [scores[u][:].rearrange("q (s t) -> q t s", t=PACK) for u in range(PAGES)]
         least = [keep.tile([NQ, 1], F32, name="least%d" % u) for u in range(PAGES)]
@@ -147,7 +184,7 @@ def tile_attend_pkv4_sink_kernel(tc, qT, k_words, k_scales, v_words, v_scales, v
         pieces = [(u, t, t + 2) for u in range(PAGES) for t in (0, 2)]
         terms = keep.tile([NQ, len(pieces) + 1], F32, name="terms")
         probs = [keep.tile([NQ, PACK, P], F32, name="probs%d" % u) for u in range(PAGES)]
-        turned = [psum.tile([P, PACK, NQ], F32, name="turned_probs%d" % u) for u in range(PAGES)]
+        turned = [psum.tile([P, PACK, NQ], F32, name="turned_probs%d" % u, tag="turned%d" % u) for u in range(PAGES)]
         for i, (u, t0, t1) in enumerate(pieces):
             nc.scalar.activation(
                 probs[u][:, t0:t1, :], neg_scores[u][:, t0:t1, :], ACT.Exp, bias=neg_max[:], scale=-1.0, accum_out=terms[:, i : i + 1]

@@ -146,17 +146,6 @@ def tile_attend_pkv4_sink_kernel(tc, qT, k_words, k_scales, v_words, v_scales, v
             scores.append(bank)
 
         gather_keys(0)
-        idle_bank = psum.tile([NQ, PAGE], F32, name="idle_bank", tag="turned%d" % (PAGES - 1))
-        for columns in (PAGE, NQ):
-            nc.tensor.matmul_mx(
-                idle_bank[:, 0:columns],
-                lhsT=q_codes[0][:].bitcast(FP8X4),
-                lhsT_scale=q_scales[0][:],
-                rhs=key_pairs[0][:].bitcast(U16)[:, 0:columns].bitcast(FP4X4),
-                rhs_scale=key_scales[:, 0:columns],
-                start=True,
-                stop=True,
-            )
         gather_keys(1)
         part_keys(0, [slice(0, 1), slice(1, 2)])
         quantize_queries(1)

@@ -26,7 +26,9 @@ QUADS = 4
 W_BYTES = 2 * NQ * PACK
 SECOND = 4 * W_BYTES
 ROW0 = P - 16 * PASSES
-EARLY = 3 * POOL // 4
+VALUE_ROW0 = P - 16
+EARLY = 5 * POOL // 16
+KEY_PLANES = PASSES * SLOTS
 HALF = DV // 2
 FLOPS = 2 * NQ * SLOTS * (D + DV)
 
@@ -39,13 +41,21 @@ def tile_attend_pkv4_sink_kernel(tc, qT, k_words, k_scales, v_words, v_scales, v
         late = ctx.enter_context(tc.tile_pool(name="late", bufs=1))
         psum = ctx.enter_context(tc.psum_pool(name="psum", bufs=1))
 
-        token_scale_pool = keep.tile([P, POOL], F32, name="token_scale_pool")
-        nc.scalar.dma_start(token_scale_pool[P - 1 : P, :], vs[0:1, :])
+        value_scale_pool = keep.tile([P, POOL_PAGES * DV], U8, name="value_scale_pool")
+        nc.vector.memset(value_scale_pool[0:VALUE_ROW0, :].bitcast(I32), 0)
+        nc.sync.dma_start(
+            value_scale_pool[VALUE_ROW0:P, :].bitcast(I32).rearrange("f (u e) -> f u e", u=POOL_PAGES),
+            v_scales.bitcast(I32).rearrange("u f e -> f u e"),
+        )
+        column_list = lists.tile([P, PAGES * DV // 16], U16, name="column_list")
+        nc.sync.dma_start(column_list[:], voffs)
         key_scale_pool = keep.tile([P, POOL], U8, name="key_scale_pool", tag="pools")
         nc.vector.memset(key_scale_pool[0:ROW0, :].bitcast(I32), 0)
         nc.sync.dma_start(key_scale_pool[ROW0:P, :].bitcast(I32), k_scales.bitcast(I32).rearrange("o f t -> f o t"))
         slot_list = lists.tile([P, SLOTS // 16], U16, name="slot_list")
         nc.sync.dma_start(slot_list[:], offs)
+        token_scale_pool = keep.tile([P, POOL], F32, name="token_scale_pool")
+        nc.sync.dma_start(token_scale_pool[P - 1 : P, :], vs[0:1, :])
         q_rows = qT[0].rearrange("(g p j) w -> g p j w", g=PASSES, j=PACK)
         q_raw = [
             late.tile([P, PACK, NQ], F32, name="q_raw0", offset=3 * W_BYTES // 2, align_bytes=64),
@@ -58,12 +68,12 @@ def tile_attend_pkv4_sink_kernel(tc, qT, k_words, k_scales, v_words, v_scales, v
         sink_col = keep.tile([P, 1], F32, name="sink_col")
         nc.scalar.dma_start(sink_col[:], sink[0])
 
-        key_planes = keep.tile([P, PASSES, SLOTS], U8, name="key_planes", align_bytes=64)
-        plane_words = key_planes[:].rearrange("p o n -> p (o n)").bitcast(I32)
+        planes = keep.tile([P, KEY_PLANES + PAGES * DV], U8, name="planes", align_bytes=64)
+        plane_words = planes[:].bitcast(I32)
         nc.vector.memset(token_scale_pool[0 : P - 1, 0:EARLY], 0.0)
         nc.gpsimd.memset(token_scale_pool[0 : P - 1, EARLY - 8 : POOL], 0.0)
         nc.vector.memset(plane_words[:, 0:16], 0)
-        nc.gpsimd.memset(plane_words[:, 8 : PASSES * SLOTS // 4], 0)
+        nc.gpsimd.memset(plane_words[:, 8 : (KEY_PLANES + PAGES * DV) // 4], 0)
 
         q_grouped = [keep.tile([P, NQ, PACK], BF16, name="q_grouped%d" % o, align_bytes=64) for o in range(PASSES)]
         nc.scalar.activation(q_grouped[0][:], q_raw[0][:].rearrange("p j w -> p w j"), ACT.Copy, scale=-1.0)
@@ -71,13 +81,13 @@ def tile_attend_pkv4_sink_kernel(tc, qT, k_words, k_scales, v_words, v_scales, v
         nc.scalar.activation(neg_sink[:], sink_col[:], ACT.Copy, scale=-1.0)
         nc.scalar.activation(q_grouped[1][:], q_raw[1][:].rearrange("p j w -> p w j"), ACT.Copy, scale=-1.0)
 
+        value_scales = keep.tile([P, PAGES * DV], U8, name="value_scales", align_bytes=64)
+        nc.vector.tensor_copy(value_scales[:], value_scale_pool[:].indirect(column_list[:]))
         key_scales = keep.tile([P, SLOTS], U8, name="key_scales", align_bytes=64)
         nc.vector.tensor_copy(key_scales[:], key_scale_pool[:].indirect(slot_list[:]))
         for quad in range(QUADS):
             row = ROW0 + 8 * quad
-            nc.sync.dma_start(plane_words[32 * quad : 32 * quad + 4, :], key_scales[row : row + 8, :].bitcast(I32))
-        value_scale_pool = late.tile([P, POOL_PAGES * DV], U8, name="value_scale_pool", offset=W_BYTES // 2, align_bytes=64)
-        nc.gpsimd.memset(value_scale_pool[:].bitcast(I32), 0)
+            nc.sync.dma_start(plane_words[32 * quad : 32 * quad + 4, 0 : KEY_PLANES // 4], key_scales[row : row + 8, :].bitcast(I32))
         ident = late.tile([P, P], F32, name="ident", offset=PAGES * W_BYTES, align_bytes=64)
         make_identity(nc, ident[:])
         token_scales = keep.tile([P, SLOTS], F32, name="token_scales")
@@ -95,18 +105,17 @@ def tile_attend_pkv4_sink_kernel(tc, qT, k_words, k_scales, v_words, v_scales, v
             value_pool[:].rearrange("p (u e) -> p u e", u=POOL_PAGES),
             v_words.rearrange("u p e r -> p u (e r)").bitcast(I32),
         )
-        column_list = lists.tile([P, PAGES * DV // 16], U16, name="column_list")
-        nc.sync.dma_start(column_list[:], voffs)
-        for quad in range(QUADS):
-            nc.sync.dma_start(
-                value_scale_pool[32 * quad : 32 * quad + 4, :].bitcast(I32).rearrange("f (u e) -> f u e", u=POOL_PAGES),
-                v_scales.bitcast(I32)[:, 4 * quad : 4 * quad + 4, :].rearrange("u f e -> f u e"),
-            )
         slot_scales = []
         for u in range(PAGES):
             spread = keep.tile([P, PACK], F32, name="slot_scales%d" % u)
             nc.sync.dma_start(spread[:], token_scales[P - 1 : P, PAGE * u : PAGE * (u + 1)])
             slot_scales.append(spread)
+        for quad in range(QUADS):
+            row = VALUE_ROW0 + 4 * quad
+            nc.sync.dma_start(
+                plane_words[32 * quad : 32 * quad + 4, KEY_PLANES // 4 : (KEY_PLANES + PAGES * DV) // 4],
+                value_scales[row : row + 4, :].bitcast(I32),
+            )
 
         key_pairs = []
         scores = []
@@ -139,7 +148,7 @@ def tile_attend_pkv4_sink_kernel(tc, qT, k_words, k_scales, v_words, v_scales, v
                     lhsT=q_codes[o][:].bitcast(FP8X4),
                     lhsT_scale=q_scales[o][:],
                     rhs=keys[u][:, o, :].bitcast(FP4X4),
-                    rhs_scale=key_planes[:, o, PAGE * u : PAGE * (u + 1)],
+                    rhs_scale=planes[:, SLOTS * o + PAGE * u : SLOTS * o + PAGE * (u + 1)],
                     start=(o == 0),
                     stop=(o == PASSES - 1),
                 )
@@ -167,8 +176,7 @@ def tile_attend_pkv4_sink_kernel(tc, qT, k_words, k_scales, v_words, v_scales, v
 
         values = keep.tile([P, PAGES * DV], U32, name="values", align_bytes=64)
         nc.vector.tensor_copy(values[:], value_pool[:].bitcast(U32).indirect(column_list[:]))
-        value_plane = keep.tile([P, PAGES * DV], U8, name="value_plane", align_bytes=64)
-        nc.vector.tensor_copy(value_plane[:], value_scale_pool[:].indirect(column_list[:]))
+        value_plane = planes[:, KEY_PLANES : KEY_PLANES + PAGES * DV]
 
         pieces = [(u, t, t + 2) for u in range(PAGES) for t in (0, 2)]
         terms = keep.tile([NQ, len(pieces) + 1], F32, name="terms")

@@ -85,9 +85,13 @@ def tile_attend_pkv4_sink_kernel(tc, qT, k_words, k_scales, v_words, v_scales, v
         nc.vector.tensor_copy(value_scales[:], value_scale_pool[:].indirect(column_list[:]))
         key_scales = keep.tile([P, SLOTS], U8, name="key_scales", align_bytes=64)
         nc.vector.tensor_copy(key_scales[:], key_scale_pool[:].indirect(slot_list[:]))
-        for quad in range(QUADS):
-            row = ROW0 + 8 * quad
-            nc.sync.dma_start(plane_words[32 * quad : 32 * quad + 4, 0 : KEY_PLANES // 4], key_scales[row : row + 8, :].bitcast(I32))
+        for first, last in ((0, PAGE), (PAGE, SLOTS)):
+            for quad in range(QUADS):
+                row = ROW0 + 8 * quad
+                nc.sync.dma_start(
+                    plane_words[32 * quad : 32 * quad + 4, PASSES * first // 4 : PASSES * last // 4],
+                    key_scales[row : row + 8, first:last].bitcast(I32),
+                )
         ident = late.tile([P, P], F32, name="ident", offset=PAGES * W_BYTES, align_bytes=64)
         make_identity(nc, ident[:])
         token_scales = keep.tile([P, SLOTS], F32, name="token_scales")
@@ -143,12 +147,13 @@ def tile_attend_pkv4_sink_kernel(tc, qT, k_words, k_scales, v_words, v_scales, v
         def score_page(u):
             bank = psum.tile([NQ, PAGE], F32, name="scores%d" % u)
             for o in range(PASSES):
+                plane = PAGE * o if u == 0 else PASSES * PAGE + (SLOTS - PAGE) * o + PAGE * (u - 1)
                 nc.tensor.matmul_mx(
                     bank[:],
                     lhsT=q_codes[o][:].bitcast(FP8X4),
                     lhsT_scale=q_scales[o][:],
                     rhs=keys[u][:, o, :].bitcast(FP4X4),
-                    rhs_scale=planes[:, SLOTS * o + PAGE * u : SLOTS * o + PAGE * (u + 1)],
+                    rhs_scale=planes[:, plane : plane + PAGE],
                     start=(o == 0),
                     stop=(o == PASSES - 1),
                 )
@@ -179,19 +184,17 @@ def tile_attend_pkv4_sink_kernel(tc, qT, k_words, k_scales, v_words, v_scales, v
         value_plane = planes[:, KEY_PLANES : KEY_PLANES + PAGES * DV]
 
         pieces = [(u, t, t + 2) for u in range(PAGES) for t in (0, 2)]
-        terms = keep.tile([NQ, len(pieces) + 1], F32, name="terms")
-        probs = [keep.tile([NQ, PACK, P], F32, name="probs%d" % u) for u in range(PAGES)]
+        terms = keep.tile([NQ, SLOTS + 8], F32, name="terms")
+        probs = [terms[:, PAGE * u : PAGE * (u + 1)].rearrange("q (t s) -> q t s", t=PACK) for u in range(PAGES)]
         turned = [psum.tile([P, PACK, NQ], F32, name="turned_probs%d" % u, tag="turned%d" % u) for u in range(PAGES)]
-        for i, (u, t0, t1) in enumerate(pieces):
-            nc.scalar.activation(
-                probs[u][:, t0:t1, :], neg_scores[u][:, t0:t1, :], ACT.Exp, bias=neg_max[:], scale=-1.0, accum_out=terms[:, i : i + 1]
-            )
+        for u, t0, t1 in pieces:
+            nc.scalar.activation(probs[u][:, t0:t1, :], neg_scores[u][:, t0:t1, :], ACT.Exp, bias=neg_max[:], scale=-1.0)
             for t in range(t0, t1):
                 nc.tensor.transpose(turned[u][:, t, :], probs[u][:, t, :], ident[:])
-        nc.scalar.activation(terms[:, len(pieces) : len(pieces) + 1], sink_col[:], ACT.Exp, bias=neg_max[:])
+        nc.scalar.activation(terms[:, SLOTS : SLOTS + 1], sink_col[:], ACT.Exp, bias=neg_max[:])
         total = keep.tile([NQ, 1], F32, name="total")
-        summed = keep.tile([NQ, len(pieces) + 1], F32, name="summed")
-        nc.scalar.activation(summed[:], terms[:], ACT.Copy, accum_out=total[:])
+        summed = keep.tile([NQ, SLOTS + 1], F32, name="summed")
+        nc.scalar.activation(summed[:], terms[:, 0 : SLOTS + 1], ACT.Copy, accum_out=total[:])
 
         weights = []
         sums = [psum.tile([NQ, HALF], F32, name="sums%d" % h) for h in range(2)]
@@ -225,9 +228,9 @@ def tile_attend_pkv4_sink_kernel(tc, qT, k_words, k_scales, v_words, v_scales, v
         multiply(0)
         weigh(2)
         multiply(1)
-        inverse = late.tile([NQ, 1], F32, name="inverse", offset=0, align_bytes=64)
-        nc.vector.reciprocal(inverse[:], total[:])
         multiply(2)
+        inverse = late.tile([NQ, 1], F32, name="inverse", offset=2 * W_BYTES, align_bytes=64)
+        nc.vector.reciprocal(inverse[:], total[:])
 
         results = [keep.tile([NQ, HALF], F32, name="result%d" % h) for h in range(2)]
         nc.scalar.activation(results[0][:], sums[0][:], ACT.Copy, scale=inverse[:])

@@ -13,7 +13,6 @@ FP8X4 = mybir.dt.float8_e4m3fn_x4
 FP4X4 = mybir.dt.float4_e2m1fn_x4
 ALU = mybir.AluOpType
 ACT = mybir.ActivationFunctionType
-AXIS = mybir.AxisListType
 
 P = 128
 PACK = 4
@@ -23,14 +22,27 @@ PAGES = SLOTS // PAGE
 POOL_PAGES = POOL // PAGE
 PASSES = D // PAGE
 QUADS = 4
-W_BYTES = 2 * NQ * PACK
-SECOND = 4 * W_BYTES
-ROW0 = P - 16 * PASSES
-VALUE_ROW0 = P - 16
-EARLY = 5 * POOL // 16
-KEY_PLANES = PASSES * SLOTS
+REST = SLOTS - PAGE
 HALF = DV // 2
+KEY_ROW0 = 32
+VALUE_ROW0 = P - 16
+EARLY = 1152
 FLOPS = 2 * NQ * SLOTS * (D + DV)
+
+KEY_WINDOW = 0
+VALUE_PLANE = KEY_WINDOW + PASSES * REST
+SLOT_SCALES = VALUE_PLANE + PAGES * DV
+VALUE_POOL = SLOT_SCALES + 128
+VALUE_WINDOW = VALUE_POOL + 4 * POOL_PAGES * DV
+Q_BYTES = 4 * PACK * NQ
+W_BYTES = 2 * NQ * PACK
+LAST_PAIRS = VALUE_WINDOW + POOL_PAGES * DV
+Q_SECOND = LAST_PAIRS + 4 * PAGE - 64
+LAST_TOKEN_SCALES = Q_SECOND + Q_BYTES - 64
+Q_FIRST = LAST_TOKEN_SCALES + 4 * PAGE
+SECOND_KEYS = Q_FIRST + Q_BYTES
+VALUES = SECOND_KEYS + 4 * PAGE
+WEIGHTS = VALUES + 4 * PAGES * DV
 
 
 def tile_attend_pkv4_sink_kernel(tc, qT, k_words, k_scales, v_words, v_scales, vs, sink, offs, voffs, out):
@@ -38,122 +50,135 @@ def tile_attend_pkv4_sink_kernel(tc, qT, k_words, k_scales, v_words, v_scales, v
     with ExitStack() as ctx:
         lists = ctx.enter_context(tc.tile_pool(name="lists", bufs=1))
         keep = ctx.enter_context(tc.tile_pool(name="keep", bufs=1))
-        late = ctx.enter_context(tc.tile_pool(name="late", bufs=1))
+        shared = ctx.enter_context(tc.tile_pool(name="shared", bufs=1))
         psum = ctx.enter_context(tc.psum_pool(name="psum", bufs=1))
 
-        value_scale_pool = keep.tile([P, POOL_PAGES * DV], U8, name="value_scale_pool")
-        nc.vector.memset(value_scale_pool[0:VALUE_ROW0, :].bitcast(I32), 0)
+        def placed(shape, dtype, name, offset):
+            return shared.tile(shape, dtype, name=name, offset=offset, align_bytes=64)
+
+        sink_col = keep.tile([P, 1], F32, name="sink_col")
+        nc.scalar.dma_start(sink_col[:], sink[0])
+        slot_list = lists.tile([P, SLOTS // 16], U16, name="slot_list")
+        nc.sync.dma_start(slot_list[:], offs)
+        key_scale_pool = placed([P, POOL], U8, "key_scale_pool", KEY_WINDOW)
+        nc.sync.dma_start(
+            key_scale_pool[KEY_ROW0 : KEY_ROW0 + 32, :].bitcast(I32), k_scales.bitcast(I32).rearrange("o f t -> f o t")
+        )
+        column_list = lists.tile([P, PAGES * DV // 16], U16, name="column_list")
+        nc.sync.dma_start(column_list[:], voffs)
+        value_scale_pool = placed([P, POOL_PAGES * DV], U8, "value_scale_pool", VALUE_WINDOW)
         nc.sync.dma_start(
             value_scale_pool[VALUE_ROW0:P, :].bitcast(I32).rearrange("f (u e) -> f u e", u=POOL_PAGES),
             v_scales.bitcast(I32).rearrange("u f e -> f u e"),
         )
-        column_list = lists.tile([P, PAGES * DV // 16], U16, name="column_list")
-        nc.sync.dma_start(column_list[:], voffs)
-        key_scale_pool = keep.tile([P, POOL], U8, name="key_scale_pool", tag="pools")
-        nc.vector.memset(key_scale_pool[0:ROW0, :].bitcast(I32), 0)
-        nc.sync.dma_start(key_scale_pool[ROW0:P, :].bitcast(I32), k_scales.bitcast(I32).rearrange("o f t -> f o t"))
-        slot_list = lists.tile([P, SLOTS // 16], U16, name="slot_list")
-        nc.sync.dma_start(slot_list[:], offs)
+        q_rows = qT[0].rearrange("(g p j) w -> g p j w", g=PASSES, j=PACK)
+        q_raw = [placed([P, PACK, NQ], F32, "q_raw0", Q_FIRST)]
+        nc.sync.dma_start(q_raw[0][:], q_rows[0])
         token_scale_pool = keep.tile([P, POOL], F32, name="token_scale_pool")
         nc.sync.dma_start(token_scale_pool[P - 1 : P, :], vs[0:1, :])
-        q_rows = qT[0].rearrange("(g p j) w -> g p j w", g=PASSES, j=PACK)
-        q_raw = [
-            late.tile([P, PACK, NQ], F32, name="q_raw0", offset=3 * W_BYTES // 2, align_bytes=64),
-            late.tile([P, PACK, NQ], F32, name="q_raw1", offset=SECOND + W_BYTES, align_bytes=64),
-        ]
-        nc.sync.dma_start(q_raw[0][:], q_rows[0])
         key_pool = keep.tile([P, POOL], I32, name="key_pool")
         nc.sync.dma_start(key_pool[:], k_words[0].rearrange("p t b -> p (t b)").bitcast(I32))
-        nc.sync.dma_start(q_raw[1][:], q_rows[1])
-        sink_col = keep.tile([P, 1], F32, name="sink_col")
-        nc.scalar.dma_start(sink_col[:], sink[0])
 
-        planes = keep.tile([P, KEY_PLANES + PAGES * DV], U8, name="planes", align_bytes=64)
-        plane_words = planes[:].bitcast(I32)
+        nc.vector.memset(key_scale_pool[0:KEY_ROW0, :].bitcast(I32), 0)
+        nc.vector.memset(key_scale_pool[KEY_ROW0 + 32 : P, :].bitcast(I32), 0)
+        nc.vector.memset(value_scale_pool[0:VALUE_ROW0, :].bitcast(I32), 0)
         nc.vector.memset(token_scale_pool[0 : P - 1, 0:EARLY], 0.0)
         nc.gpsimd.memset(token_scale_pool[0 : P - 1, EARLY - 8 : POOL], 0.0)
-        nc.vector.memset(plane_words[:, 0:16], 0)
-        nc.gpsimd.memset(plane_words[:, 8 : (KEY_PLANES + PAGES * DV) // 4], 0)
 
-        q_grouped = [keep.tile([P, NQ, PACK], BF16, name="q_grouped%d" % o, align_bytes=64) for o in range(PASSES)]
-        nc.scalar.activation(q_grouped[0][:], q_raw[0][:].rearrange("p j w -> p w j"), ACT.Copy, scale=-1.0)
         neg_sink = keep.tile([P, 1], F32, name="neg_sink")
         nc.scalar.activation(neg_sink[:], sink_col[:], ACT.Copy, scale=-1.0)
-        nc.scalar.activation(q_grouped[1][:], q_raw[1][:].rearrange("p j w -> p w j"), ACT.Copy, scale=-1.0)
-
-        value_scales = keep.tile([P, PAGES * DV], U8, name="value_scales", align_bytes=64)
-        nc.vector.tensor_copy(value_scales[:], value_scale_pool[:].indirect(column_list[:]))
-        key_scales = keep.tile([P, SLOTS], U8, name="key_scales", align_bytes=64)
-        nc.vector.tensor_copy(key_scales[:], key_scale_pool[:].indirect(slot_list[:]))
-        for first, last in ((0, PAGE), (PAGE, SLOTS)):
-            for quad in range(QUADS):
-                row = ROW0 + 8 * quad
-                nc.sync.dma_start(
-                    plane_words[32 * quad : 32 * quad + 4, PASSES * first // 4 : PASSES * last // 4],
-                    key_scales[row : row + 8, first:last].bitcast(I32),
-                )
-        ident = late.tile([P, P], F32, name="ident", offset=PAGES * W_BYTES, align_bytes=64)
-        make_identity(nc, ident[:])
-        token_scales = keep.tile([P, SLOTS], F32, name="token_scales")
-        nc.vector.tensor_copy(token_scales[:], token_scale_pool[:].indirect(slot_list[:]))
+        q_grouped = [
+            keep.tile([P, NQ, PACK], BF16, name="q_grouped0", align_bytes=64),
+            placed([P, NQ, PACK], BF16, "q_grouped1", SECOND_KEYS),
+        ]
         q_codes = [keep.tile([P, NQ], U32, name="q_codes%d" % o, align_bytes=64) for o in range(PASSES)]
         q_scales = [keep.tile([P, NQ], U8, name="q_scales%d" % o, align_bytes=64) for o in range(PASSES)]
+
+        def cast_queries(o):
+            nc.scalar.activation(q_grouped[o][:], q_raw[o][:].rearrange("p j w -> p w j"), ACT.Copy, scale=-1.0)
 
         def quantize_queries(o):
             nc.vector.quantize_mx(q_codes[o][:].bitcast(FP8X4), q_scales[o][:], q_grouped[o][:].rearrange("p w j -> p (w j)"))
 
-        quantize_queries(0)
+        def move_rows(plane, gathered, row0, rows):
+            for quad in range(QUADS):
+                row = row0 + rows * quad
+                nc.sync.dma_start(plane[32 * quad : 32 * quad + 4, :].bitcast(I32), gathered[row : row + rows].bitcast(I32))
 
-        value_pool = keep.tile([P, POOL_PAGES * DV], I32, name="value_pool", tag="pools")
+        cast_queries(0)
+        key_scales = keep.tile([P, SLOTS], U8, name="key_scales", align_bytes=64)
+        nc.vector.tensor_copy(key_scales[:], key_scale_pool[:].indirect(slot_list[:]))
+        value_scales = keep.tile([P, PAGES * DV], U8, name="value_scales", align_bytes=64)
+        nc.vector.tensor_copy(value_scales[:], value_scale_pool[:].indirect(column_list[:]))
+        first_plane = placed([P, PASSES * PAGE], U8, "first_plane", VALUE_WINDOW)
+        move_rows(first_plane, key_scales[:, 0:PAGE], KEY_ROW0, 8)
+        q_raw.append(placed([P, PACK, NQ], F32, "q_raw1", Q_SECOND))
+        nc.sync.dma_start(q_raw[1][:], q_rows[1])
+        quantize_queries(0)
+        rest_plane = placed([P, PASSES * REST], U8, "rest_plane", KEY_WINDOW)
+        move_rows(rest_plane, key_scales[:, PAGE:SLOTS], KEY_ROW0, 8)
+        value_pool = placed([P, POOL_PAGES * DV], I32, "value_pool", VALUE_POOL)
         nc.sync.dma_start(
             value_pool[:].rearrange("p (u e) -> p u e", u=POOL_PAGES),
             v_words.rearrange("u p e r -> p u (e r)").bitcast(I32),
         )
+
+        token_scales = [keep.tile([P, PAGE], F32, name="token_scales%d" % u) for u in range(PAGES - 1)]
+
+        def gather_token_scales(u):
+            nc.scalar.activation(token_scales[u][:], token_scale_pool[:].indirect(slot_list[:, 32 * u : 32 * (u + 1)]), ACT.Copy)
+
+        gather_token_scales(0)
+        gather_token_scales(1)
+        cast_queries(1)
+        token_scales.append(placed([P, PAGE], F32, "token_scales2", LAST_TOKEN_SCALES))
+        gather_token_scales(2)
         slot_scales = []
         for u in range(PAGES):
-            spread = keep.tile([P, PACK], F32, name="slot_scales%d" % u)
-            nc.sync.dma_start(spread[:], token_scales[P - 1 : P, PAGE * u : PAGE * (u + 1)])
+            spread = shared.tile([P, PACK], F32, name="slot_scales%d" % u, offset=SLOT_SCALES + 32 * u)
+            nc.sync.dma_start(spread[:], token_scales[u][P - 1 : P, :])
             slot_scales.append(spread)
-        for quad in range(QUADS):
-            row = VALUE_ROW0 + 4 * quad
-            nc.sync.dma_start(
-                plane_words[32 * quad : 32 * quad + 4, KEY_PLANES // 4 : (KEY_PLANES + PAGES * DV) // 4],
-                value_scales[row : row + 4, :].bitcast(I32),
-            )
+        value_plane = placed([P, PAGES * DV], U8, "value_plane", VALUE_PLANE)
+        move_rows(value_plane, value_scales[:], VALUE_ROW0, 4)
+
+        ident = placed([P, P], F32, "ident", Q_FIRST)
+        make_identity(nc, ident[:])
 
         key_pairs = []
+        keys = []
         scores = []
 
         def gather_keys(u):
             if u == PAGES - 1:
-                pairs = late.tile([P, PAGE], U32, name="key_pairs%d" % u, offset=SECOND, align_bytes=64)
+                pairs = placed([P, PAGE], U32, "key_pairs%d" % u, LAST_PAIRS)
             else:
                 pairs = keep.tile([P, PAGE], U32, name="key_pairs%d" % u, align_bytes=64)
             nc.vector.tensor_copy(pairs[:], key_pool[:].bitcast(U32).indirect(slot_list[:, 32 * u : 32 * (u + 1)]))
             key_pairs.append(pairs)
 
-        keys = []
-
-        def part_keys(u, copies):
+        def part_keys(u):
             if u == 1:
-                parted = late.tile([P, PASSES, PAGE], U16, name="keys%d" % u, offset=SECOND + 2 * W_BYTES, align_bytes=64)
+                parted = placed([P, PASSES, PAGE], U16, "keys%d" % u, SECOND_KEYS)
             else:
                 parted = keep.tile([P, PASSES, PAGE], U16, name="keys%d" % u, align_bytes=64)
             halves = key_pairs[u][:].bitcast(U16).rearrange("p (n o) -> p o n", o=PASSES)
-            for part in copies:
-                nc.vector.tensor_copy(parted[:, part, :], halves[:, part, :])
+            for o in range(PASSES):
+                nc.vector.tensor_copy(parted[:, o, :], halves[:, o, :])
             keys.append(parted)
 
         def score_page(u):
             bank = psum.tile([NQ, PAGE], F32, name="scores%d" % u)
             for o in range(PASSES):
-                plane = PAGE * o if u == 0 else PASSES * PAGE + (SLOTS - PAGE) * o + PAGE * (u - 1)
+                if u == 0:
+                    plane = first_plane[:, PAGE * o : PAGE * (o + 1)]
+                else:
+                    plane = rest_plane[:, REST * o + PAGE * (u - 1) : REST * o + PAGE * u]
                 nc.tensor.matmul_mx(
                     bank[:],
                     lhsT=q_codes[o][:].bitcast(FP8X4),
                     lhsT_scale=q_scales[o][:],
                     rhs=keys[u][:, o, :].bitcast(FP4X4),
-                    rhs_scale=planes[:, plane : plane + PAGE],
+                    rhs_scale=plane,
                     start=(o == 0),
                     stop=(o == PASSES - 1),
                 )
@@ -161,17 +186,21 @@ def tile_attend_pkv4_sink_kernel(tc, qT, k_words, k_scales, v_words, v_scales, v
 
         gather_keys(0)
         gather_keys(1)
-        part_keys(0, [slice(0, 1), slice(1, 2)])
+        part_keys(0)
         quantize_queries(1)
         score_page(0)
         gather_keys(2)
-        part_keys(1, [slice(0, 1), slice(1, 2)])
+        part_keys(1)
         score_page(1)
-        part_keys(2, [slice(0, 2)])
+        part_keys(2)
         score_page(2)
 
         dealt = [scores[u][:].rearrange("q (s t) -> q t s", t=PACK) for u in range(PAGES)]
-        least = [keep.tile([NQ, 1], F32, name="least%d" % u) for u in range(PAGES)]
+        least = [
+            keep.tile([NQ, 1], F32, name="least0"),
+            placed([NQ, 1], F32, "least1", VALUES),
+            keep.tile([NQ, 1], F32, name="least2"),
+        ]
         copies = [keep.tile([NQ, PACK, P], F32, name="neg_scores%d" % u) for u in range(PAGES)]
         nc.vector.tensor_scalar(copies[0][:], dealt[0], 1.0, neg_sink[:], op0=ALU.mult, op1=ALU.min, accum_out=least[0][:])
         nc.vector.tensor_scalar(copies[1][:], dealt[1], 1.0, None, op0=ALU.mult, op1=ALU.min, accum_out=least[1][:])
@@ -179,9 +208,8 @@ def tile_attend_pkv4_sink_kernel(tc, qT, k_words, k_scales, v_words, v_scales, v
         neg_max = least[2]
         neg_scores = [copies[0][:], copies[1][:], dealt[2]]
 
-        values = keep.tile([P, PAGES * DV], U32, name="values", align_bytes=64)
+        values = placed([P, PAGES * DV], U32, "values", VALUES)
         nc.vector.tensor_copy(values[:], value_pool[:].bitcast(U32).indirect(column_list[:]))
-        value_plane = planes[:, KEY_PLANES : KEY_PLANES + PAGES * DV]
 
         pieces = [(u, t, t + 2) for u in range(PAGES) for t in (0, 2)]
         terms = keep.tile([NQ, SLOTS + 8], F32, name="terms")
@@ -200,7 +228,7 @@ def tile_attend_pkv4_sink_kernel(tc, qT, k_words, k_scales, v_words, v_scales, v
         sums = [psum.tile([NQ, HALF], F32, name="sums%d" % h) for h in range(2)]
 
         def weigh(u):
-            w_grouped = late.tile([P, NQ, PACK], BF16, name="w_grouped%d" % u, offset=W_BYTES * u, align_bytes=64)
+            w_grouped = placed([P, NQ, PACK], BF16, "w_grouped%d" % u, WEIGHTS + W_BYTES * u)
             nc.vector.tensor_tensor(
                 w_grouped[:], turned[u][:].rearrange("p t q -> p q t"),
                 slot_scales[u][:].unsqueeze(1).to_broadcast([P, NQ, PACK]), ALU.mult,
@@ -229,7 +257,7 @@ def tile_attend_pkv4_sink_kernel(tc, qT, k_words, k_scales, v_words, v_scales, v
         weigh(2)
         multiply(1)
         multiply(2)
-        inverse = late.tile([NQ, 1], F32, name="inverse", offset=2 * W_BYTES, align_bytes=64)
+        inverse = placed([NQ, 1], F32, "inverse", WEIGHTS + 2 * W_BYTES)
         nc.vector.reciprocal(inverse[:], total[:])
 
         results = [keep.tile([NQ, HALF], F32, name="result%d" % h) for h in range(2)]

@@ -21,16 +21,13 @@ SLOTS, POOL, D, DV, NQ = 1536, 4096, 1024, 256, 128
 PAGES = SLOTS // PAGE
 POOL_PAGES = POOL // PAGE
 PASSES = D // PAGE
-QUADS = 4
-REST = SLOTS - PAGE
 HALF = DV // 2
-KEY_ROW0 = 32
-VALUE_ROW0 = P - 16
-EARLY = 1152
+STEP = 4
+VALUE_ROW0 = 32
 FLOPS = 2 * NQ * SLOTS * (D + DV)
 
 KEY_WINDOW = 0
-VALUE_PLANE = KEY_WINDOW + PASSES * REST
+VALUE_PLANE = KEY_WINDOW + SLOTS
 SLOT_SCALES = VALUE_PLANE + PAGES * DV
 VALUE_POOL = SLOT_SCALES + 128
 VALUE_WINDOW = VALUE_POOL + 4 * POOL_PAGES * DV
@@ -39,9 +36,9 @@ W_BYTES = 2 * NQ * PACK
 LAST_PAIRS = VALUE_WINDOW + POOL_PAGES * DV
 Q_SECOND = LAST_PAIRS + 4 * PAGE - 64
 LAST_TOKEN_SCALES = Q_SECOND + Q_BYTES - 64
-Q_FIRST = LAST_TOKEN_SCALES + 4 * PAGE
-SECOND_KEYS = Q_FIRST + Q_BYTES
-VALUES = SECOND_KEYS + 4 * PAGE
+LATER_KEYS = LAST_TOKEN_SCALES + 4 * PAGE
+KEY_SCALES = LATER_KEYS + 4 * PAGE - SLOTS // 2
+VALUES = LATER_KEYS + 8 * PAGE
 WEIGHTS = VALUES + 4 * PAGES * DV
 
 
@@ -58,39 +55,34 @@ def tile_attend_pkv4_sink_kernel(tc, qT, k_words, k_scales, v_words, v_scales, v
 
         sink_col = keep.tile([P, 1], F32, name="sink_col")
         nc.scalar.dma_start(sink_col[:], sink[0])
+        ident = keep.tile([P, P], F32, name="ident")
+        make_identity(nc, ident[:])
+        key_scale_pool = placed([P, POOL], U8, "key_scale_pool", KEY_WINDOW)
+        nc.vector.memset(key_scale_pool[:].bitcast(I32), 0)
+        value_scale_pool = placed([P, POOL_PAGES * DV], U8, "value_scale_pool", VALUE_WINDOW)
+        nc.vector.memset(value_scale_pool[:].bitcast(I32), 0)
+        token_scale_pool = keep.tile([P, POOL], F32, name="token_scale_pool")
+        nc.vector.memset(token_scale_pool[0 : P - 1, :], 0.0)
+
         slot_list = lists.tile([P, SLOTS // 16], U16, name="slot_list")
         nc.sync.dma_start(slot_list[:], offs)
-        key_scale_pool = placed([P, POOL], U8, "key_scale_pool", KEY_WINDOW)
-        nc.sync.dma_start(
-            key_scale_pool[KEY_ROW0 : KEY_ROW0 + 32, :].bitcast(I32), k_scales.bitcast(I32).rearrange("o f t -> f o t")
-        )
+        q_rows = qT[0].rearrange("(g p j) w -> g p j w", g=PASSES, j=PACK)
+        q_raw = [keep.tile([P, PACK, NQ], F32, name="q_raw0")]
+        nc.sync.dma_start(q_raw[0][:], q_rows[0])
         column_list = lists.tile([P, PAGES * DV // 16], U16, name="column_list")
         nc.sync.dma_start(column_list[:], voffs)
-        value_scale_pool = placed([P, POOL_PAGES * DV], U8, "value_scale_pool", VALUE_WINDOW)
+        nc.sync.dma_start(key_scale_pool[0:P:STEP, :].bitcast(I32), k_scales.bitcast(I32).rearrange("o f t -> f o t"))
         nc.sync.dma_start(
-            value_scale_pool[VALUE_ROW0:P, :].bitcast(I32).rearrange("f (u e) -> f u e", u=POOL_PAGES),
+            value_scale_pool[VALUE_ROW0 : VALUE_ROW0 + 16 * STEP : STEP, :].bitcast(I32).rearrange("f (u e) -> f u e", u=POOL_PAGES),
             v_scales.bitcast(I32).rearrange("u f e -> f u e"),
         )
-        q_rows = qT[0].rearrange("(g p j) w -> g p j w", g=PASSES, j=PACK)
-        q_raw = [placed([P, PACK, NQ], F32, "q_raw0", Q_FIRST)]
-        nc.sync.dma_start(q_raw[0][:], q_rows[0])
-        token_scale_pool = keep.tile([P, POOL], F32, name="token_scale_pool")
         nc.sync.dma_start(token_scale_pool[P - 1 : P, :], vs[0:1, :])
         key_pool = keep.tile([P, POOL], I32, name="key_pool")
         nc.sync.dma_start(key_pool[:], k_words[0].rearrange("p t b -> p (t b)").bitcast(I32))
 
-        nc.vector.memset(key_scale_pool[0:KEY_ROW0, :].bitcast(I32), 0)
-        nc.vector.memset(key_scale_pool[KEY_ROW0 + 32 : P, :].bitcast(I32), 0)
-        nc.vector.memset(value_scale_pool[0:VALUE_ROW0, :].bitcast(I32), 0)
-        nc.vector.memset(token_scale_pool[0 : P - 1, 0:EARLY], 0.0)
-        nc.gpsimd.memset(token_scale_pool[0 : P - 1, EARLY - 8 : POOL], 0.0)
-
         neg_sink = keep.tile([P, 1], F32, name="neg_sink")
         nc.scalar.activation(neg_sink[:], sink_col[:], ACT.Copy, scale=-1.0)
-        q_grouped = [
-            keep.tile([P, NQ, PACK], BF16, name="q_grouped0", align_bytes=64),
-            placed([P, NQ, PACK], BF16, "q_grouped1", SECOND_KEYS),
-        ]
+        q_grouped = [keep.tile([P, NQ, PACK], BF16, name="q_grouped%d" % o, align_bytes=64) for o in range(PASSES)]
         q_codes = [keep.tile([P, NQ], U32, name="q_codes%d" % o, align_bytes=64) for o in range(PASSES)]
         q_scales = [keep.tile([P, NQ], U8, name="q_scales%d" % o, align_bytes=64) for o in range(PASSES)]
 
@@ -100,23 +92,24 @@ def tile_attend_pkv4_sink_kernel(tc, qT, k_words, k_scales, v_words, v_scales, v
         def quantize_queries(o):
             nc.vector.quantize_mx(q_codes[o][:].bitcast(FP8X4), q_scales[o][:], q_grouped[o][:].rearrange("p w j -> p (w j)"))
 
-        def move_rows(plane, gathered, row0, rows):
-            for quad in range(QUADS):
-                row = row0 + rows * quad
-                nc.sync.dma_start(plane[32 * quad : 32 * quad + 4, :].bitcast(I32), gathered[row : row + rows].bitcast(I32))
+        def move_rows(plane, gathered, row0, row_step):
+            for j in range(4):
+                first = row0 + row_step * j
+                rows = gathered[first : first + 3 * 4 * row_step + 1 : 4 * row_step, :]
+                nc.sync.dma_start(plane[j:P:32, :].bitcast(I32), rows.bitcast(I32))
 
         cast_queries(0)
-        key_scales = keep.tile([P, SLOTS], U8, name="key_scales", align_bytes=64)
+        key_scales = placed([P, SLOTS], U8, "key_scales", KEY_SCALES)
         nc.vector.tensor_copy(key_scales[:], key_scale_pool[:].indirect(slot_list[:]))
         value_scales = keep.tile([P, PAGES * DV], U8, name="value_scales", align_bytes=64)
         nc.vector.tensor_copy(value_scales[:], value_scale_pool[:].indirect(column_list[:]))
-        first_plane = placed([P, PASSES * PAGE], U8, "first_plane", VALUE_WINDOW)
-        move_rows(first_plane, key_scales[:, 0:PAGE], KEY_ROW0, 8)
         q_raw.append(placed([P, PACK, NQ], F32, "q_raw1", Q_SECOND))
         nc.sync.dma_start(q_raw[1][:], q_rows[1])
+        key_planes = [placed([P, SLOTS], U8, "key_plane0", VALUE_WINDOW)]
+        move_rows(key_planes[0], key_scales, 0, PASSES * STEP)
         quantize_queries(0)
-        rest_plane = placed([P, PASSES * REST], U8, "rest_plane", KEY_WINDOW)
-        move_rows(rest_plane, key_scales[:, PAGE:SLOTS], KEY_ROW0, 8)
+        key_planes.append(placed([P, SLOTS], U8, "key_plane1", KEY_WINDOW))
+        move_rows(key_planes[1], key_scales, STEP, PASSES * STEP)
         value_pool = placed([P, POOL_PAGES * DV], I32, "value_pool", VALUE_POOL)
         nc.sync.dma_start(
             value_pool[:].rearrange("p (u e) -> p u e", u=POOL_PAGES),
@@ -139,10 +132,7 @@ def tile_attend_pkv4_sink_kernel(tc, qT, k_words, k_scales, v_words, v_scales, v
             nc.sync.dma_start(spread[:], token_scales[u][P - 1 : P, :])
             slot_scales.append(spread)
         value_plane = placed([P, PAGES * DV], U8, "value_plane", VALUE_PLANE)
-        move_rows(value_plane, value_scales[:], VALUE_ROW0, 4)
-
-        ident = placed([P, P], F32, "ident", Q_FIRST)
-        make_identity(nc, ident[:])
+        move_rows(value_plane, value_scales, VALUE_ROW0, STEP)
 
         key_pairs = []
         keys = []
@@ -157,8 +147,8 @@ def tile_attend_pkv4_sink_kernel(tc, qT, k_words, k_scales, v_words, v_scales, v
             key_pairs.append(pairs)
 
         def part_keys(u):
-            if u == 1:
-                parted = placed([P, PASSES, PAGE], U16, "keys%d" % u, SECOND_KEYS)
+            if u > 0:
+                parted = placed([P, PASSES, PAGE], U16, "keys%d" % u, LATER_KEYS + 4 * PAGE * (u - 1))
             else:
                 parted = keep.tile([P, PASSES, PAGE], U16, name="keys%d" % u, align_bytes=64)
             halves = key_pairs[u][:].bitcast(U16).rearrange("p (n o) -> p o n", o=PASSES)
@@ -169,16 +159,12 @@ def tile_attend_pkv4_sink_kernel(tc, qT, k_words, k_scales, v_words, v_scales, v
         def score_page(u):
             bank = psum.tile([NQ, PAGE], F32, name="scores%d" % u)
             for o in range(PASSES):
-                if u == 0:
-                    plane = first_plane[:, PAGE * o : PAGE * (o + 1)]
-                else:
-                    plane = rest_plane[:, REST * o + PAGE * (u - 1) : REST * o + PAGE * u]
                 nc.tensor.matmul_mx(
                     bank[:],
                     lhsT=q_codes[o][:].bitcast(FP8X4),
                     lhsT_scale=q_scales[o][:],
                     rhs=keys[u][:, o, :].bitcast(FP4X4),
-                    rhs_scale=plane,
+                    rhs_scale=key_planes[o][:, PAGE * u : PAGE * (u + 1)],
                     start=(o == 0),
                     stop=(o == PASSES - 1),
                 )

@@ -23,23 +23,24 @@ POOL_PAGES = POOL // PAGE
 PASSES = D // PAGE
 HALF = DV // 2
 STEP = 4
+EARLY = 3072
 VALUE_ROW0 = 32
 FLOPS = 2 * NQ * SLOTS * (D + DV)
 
 KEY_WINDOW = 0
 VALUE_PLANE = KEY_WINDOW + SLOTS
-SLOT_SCALES = VALUE_PLANE + PAGES * DV
-VALUE_POOL = SLOT_SCALES + 128
+VALUE_POOL = VALUE_PLANE + PAGES * DV
 VALUE_WINDOW = VALUE_POOL + 4 * POOL_PAGES * DV
 Q_BYTES = 4 * PACK * NQ
 W_BYTES = 2 * NQ * PACK
 LAST_PAIRS = VALUE_WINDOW + POOL_PAGES * DV
 Q_SECOND = LAST_PAIRS + 4 * PAGE - 64
-LAST_TOKEN_SCALES = Q_SECOND + Q_BYTES - 64
-LATER_KEYS = LAST_TOKEN_SCALES + 4 * PAGE
-KEY_SCALES = LATER_KEYS + 4 * PAGE - SLOTS // 2
-VALUES = LATER_KEYS + 8 * PAGE
-WEIGHTS = VALUES + 4 * PAGES * DV
+SLOT_SCALES = Q_SECOND + Q_BYTES - 128
+Q_CAST = Q_SECOND + Q_BYTES
+LAST_KEYS = Q_CAST + W_BYTES
+KEY_SCALES = LAST_KEYS + 2 * PAGE - SLOTS // 2
+WEIGHTS = LAST_KEYS + 4 * PAGE
+HELD_KEYS = {(1, 1): Q_CAST, (2, 0): LAST_KEYS, (2, 1): LAST_KEYS + 2 * PAGE}
 
 
 def tile_attend_pkv4_sink_kernel(tc, qT, k_words, k_scales, v_words, v_scales, vs, sink, offs, voffs, out):
@@ -53,22 +54,26 @@ def tile_attend_pkv4_sink_kernel(tc, qT, k_words, k_scales, v_words, v_scales, v
         def placed(shape, dtype, name, offset):
             return shared.tile(shape, dtype, name=name, offset=offset, align_bytes=64)
 
-        sink_col = keep.tile([P, 1], F32, name="sink_col")
-        nc.scalar.dma_start(sink_col[:], sink[0])
-        ident = keep.tile([P, P], F32, name="ident")
-        make_identity(nc, ident[:])
+        sink_rows = keep.tile([P, NQ], F32, name="sink_rows")
+        nc.scalar.dma_start(sink_rows[P - 1 : P, :], sink[0].rearrange("q one -> one q"))
         key_scale_pool = placed([P, POOL], U8, "key_scale_pool", KEY_WINDOW)
         nc.vector.memset(key_scale_pool[:].bitcast(I32), 0)
         value_scale_pool = placed([P, POOL_PAGES * DV], U8, "value_scale_pool", VALUE_WINDOW)
         nc.vector.memset(value_scale_pool[:].bitcast(I32), 0)
+        ident = keep.tile([P, P], F32, name="ident")
+        nc.vector.memset(ident[:], 0.0)
+        make_identity(nc, ident[:], nomemset=True)
+        nc.vector.memset(sink_rows[0 : P - 1, :], 0.0)
         token_scale_pool = keep.tile([P, POOL], F32, name="token_scale_pool")
-        nc.vector.memset(token_scale_pool[0 : P - 1, :], 0.0)
+        nc.vector.memset(token_scale_pool[0 : P - 1, 0:EARLY], 0.0)
+        nc.gpsimd.memset(token_scale_pool[0 : P - 1, EARLY - 8 : POOL], 0.0)
 
         slot_list = lists.tile([P, SLOTS // 16], U16, name="slot_list")
         nc.sync.dma_start(slot_list[:], offs)
         q_rows = qT[0].rearrange("(g p j) w -> g p j w", g=PASSES, j=PACK)
         q_raw = [keep.tile([P, PACK, NQ], F32, name="q_raw0")]
         nc.sync.dma_start(q_raw[0][:], q_rows[0])
+        nc.sync.dma_start(token_scale_pool[P - 1 : P, :], vs[0:1, :])
         column_list = lists.tile([P, PAGES * DV // 16], U16, name="column_list")
         nc.sync.dma_start(column_list[:], voffs)
         nc.sync.dma_start(key_scale_pool[0:P:STEP, :].bitcast(I32), k_scales.bitcast(I32).rearrange("o f t -> f o t"))
@@ -76,13 +81,17 @@ def tile_attend_pkv4_sink_kernel(tc, qT, k_words, k_scales, v_words, v_scales, v
             value_scale_pool[VALUE_ROW0 : VALUE_ROW0 + 16 * STEP : STEP, :].bitcast(I32).rearrange("f (u e) -> f u e", u=POOL_PAGES),
             v_scales.bitcast(I32).rearrange("u f e -> f u e"),
         )
-        nc.sync.dma_start(token_scale_pool[P - 1 : P, :], vs[0:1, :])
         key_pool = keep.tile([P, POOL], I32, name="key_pool")
         nc.sync.dma_start(key_pool[:], k_words[0].rearrange("p t b -> p (t b)").bitcast(I32))
 
         neg_sink = keep.tile([P, 1], F32, name="neg_sink")
-        nc.scalar.activation(neg_sink[:], sink_col[:], ACT.Copy, scale=-1.0)
-        q_grouped = [keep.tile([P, NQ, PACK], BF16, name="q_grouped%d" % o, align_bytes=64) for o in range(PASSES)]
+        turned_sink = psum.tile([NQ, P], F32, name="turned_sink", tag="sums0")
+        nc.tensor.transpose(turned_sink[:], sink_rows[:], ident[:])
+        nc.scalar.activation(neg_sink[:], turned_sink[:, P - 1 : P], ACT.Copy, scale=-1.0)
+        q_grouped = [
+            keep.tile([P, NQ, PACK], BF16, name="q_grouped0", align_bytes=64),
+            placed([P, NQ, PACK], BF16, "q_grouped1", Q_CAST),
+        ]
         q_codes = [keep.tile([P, NQ], U32, name="q_codes%d" % o, align_bytes=64) for o in range(PASSES)]
         q_scales = [keep.tile([P, NQ], U8, name="q_scales%d" % o, align_bytes=64) for o in range(PASSES)]
 
@@ -116,27 +125,27 @@ def tile_attend_pkv4_sink_kernel(tc, qT, k_words, k_scales, v_words, v_scales, v
             v_words.rearrange("u p e r -> p u (e r)").bitcast(I32),
         )
 
-        token_scales = [keep.tile([P, PAGE], F32, name="token_scales%d" % u) for u in range(PAGES - 1)]
-
-        def gather_token_scales(u):
-            nc.scalar.activation(token_scales[u][:], token_scale_pool[:].indirect(slot_list[:, 32 * u : 32 * (u + 1)]), ACT.Copy)
-
-        gather_token_scales(0)
-        gather_token_scales(1)
-        cast_queries(1)
-        token_scales.append(placed([P, PAGE], F32, "token_scales2", LAST_TOKEN_SCALES))
-        gather_token_scales(2)
-        slot_scales = []
-        for u in range(PAGES):
-            spread = shared.tile([P, PACK], F32, name="slot_scales%d" % u, offset=SLOT_SCALES + 32 * u)
-            nc.sync.dma_start(spread[:], token_scales[u][P - 1 : P, :])
-            slot_scales.append(spread)
         value_plane = placed([P, PAGES * DV], U8, "value_plane", VALUE_PLANE)
         move_rows(value_plane, value_scales, VALUE_ROW0, STEP)
 
+        turned_scales = []
+        for u in range(PAGES):
+            token_scales = keep.tile([P, PAGE], F32, name="token_scales%d" % u)
+            nc.scalar.activation(token_scales[:], token_scale_pool[:].indirect(slot_list[:, 32 * u : 32 * (u + 1)]), ACT.Copy)
+            bank = psum.tile([P, PACK, P], F32, name="turned_scales%d" % u, tag="turned%d" % u)
+            for t in range(PACK):
+                nc.tensor.transpose(bank[:, t, :], token_scales[:, t:PAGE:PACK], ident[:])
+            turned_scales.append(bank)
+        cast_queries(1)
+        slot_scales = []
+        for u in range(PAGES):
+            spread = shared.tile([P, PACK], F32, name="slot_scales%d" % u, offset=SLOT_SCALES + 32 * u)
+            nc.scalar.activation(spread[:], turned_scales[u][:, :, P - 1], ACT.Copy)
+            slot_scales.append(spread)
+
         key_pairs = []
-        keys = []
-        scores = []
+        keys = {}
+        scores = [psum.tile([NQ, PAGE], F32, name="scores%d" % u) for u in range(PAGES)]
 
         def gather_keys(u):
             if u == PAGES - 1:
@@ -146,47 +155,40 @@ def tile_attend_pkv4_sink_kernel(tc, qT, k_words, k_scales, v_words, v_scales, v
             nc.vector.tensor_copy(pairs[:], key_pool[:].bitcast(U32).indirect(slot_list[:, 32 * u : 32 * (u + 1)]))
             key_pairs.append(pairs)
 
-        def part_keys(u):
-            if u > 0:
-                parted = placed([P, PASSES, PAGE], U16, "keys%d" % u, LATER_KEYS + 4 * PAGE * (u - 1))
+        def part_keys(u, o):
+            if (u, o) in HELD_KEYS:
+                parted = placed([P, PAGE], U16, "keys%d_%d" % (u, o), HELD_KEYS[(u, o)])
             else:
-                parted = keep.tile([P, PASSES, PAGE], U16, name="keys%d" % u, align_bytes=64)
-            halves = key_pairs[u][:].bitcast(U16).rearrange("p (n o) -> p o n", o=PASSES)
-            for o in range(PASSES):
-                nc.vector.tensor_copy(parted[:, o, :], halves[:, o, :])
-            keys.append(parted)
+                parted = keep.tile([P, PAGE], U16, name="keys%d_%d" % (u, o), align_bytes=64)
+            nc.vector.tensor_copy(parted[:], key_pairs[u][:].bitcast(U16)[:, o : PASSES * PAGE : PASSES])
+            keys[(u, o)] = parted
 
-        def score_page(u):
-            bank = psum.tile([NQ, PAGE], F32, name="scores%d" % u)
-            for o in range(PASSES):
-                nc.tensor.matmul_mx(
-                    bank[:],
-                    lhsT=q_codes[o][:].bitcast(FP8X4),
-                    lhsT_scale=q_scales[o][:],
-                    rhs=keys[u][:, o, :].bitcast(FP4X4),
-                    rhs_scale=key_planes[o][:, PAGE * u : PAGE * (u + 1)],
-                    start=(o == 0),
-                    stop=(o == PASSES - 1),
-                )
-            scores.append(bank)
+        def score(u, o):
+            nc.tensor.matmul_mx(
+                scores[u][:],
+                lhsT=q_codes[o][:].bitcast(FP8X4),
+                lhsT_scale=q_scales[o][:],
+                rhs=keys[(u, o)][:].bitcast(FP4X4),
+                rhs_scale=key_planes[o][:, PAGE * u : PAGE * (u + 1)],
+                start=(o == 0),
+                stop=(o == PASSES - 1),
+            )
 
         gather_keys(0)
         gather_keys(1)
-        part_keys(0)
+        part_keys(0, 0)
+        part_keys(1, 0)
+        part_keys(0, 1)
         quantize_queries(1)
-        score_page(0)
         gather_keys(2)
-        part_keys(1)
-        score_page(1)
-        part_keys(2)
-        score_page(2)
+        part_keys(1, 1)
+        part_keys(2, 0)
+        part_keys(2, 1)
+        for u, o in ((0, 0), (1, 0), (0, 1), (1, 1), (2, 0), (2, 1)):
+            score(u, o)
 
         dealt = [scores[u][:].rearrange("q (s t) -> q t s", t=PACK) for u in range(PAGES)]
-        least = [
-            keep.tile([NQ, 1], F32, name="least0"),
-            placed([NQ, 1], F32, "least1", VALUES),
-            keep.tile([NQ, 1], F32, name="least2"),
-        ]
+        least = [keep.tile([NQ, 1], F32, name="least%d" % u) for u in range(PAGES)]
         copies = [keep.tile([NQ, PACK, P], F32, name="neg_scores%d" % u) for u in range(PAGES)]
         nc.vector.tensor_scalar(copies[0][:], dealt[0], 1.0, neg_sink[:], op0=ALU.mult, op1=ALU.min, accum_out=least[0][:])
         nc.vector.tensor_scalar(copies[1][:], dealt[1], 1.0, None, op0=ALU.mult, op1=ALU.min, accum_out=least[1][:])
@@ -194,7 +196,7 @@ def tile_attend_pkv4_sink_kernel(tc, qT, k_words, k_scales, v_words, v_scales, v
         neg_max = least[2]
         neg_scores = [copies[0][:], copies[1][:], dealt[2]]
 
-        values = placed([P, PAGES * DV], U32, "values", VALUES)
+        values = keep.tile([P, PAGES * DV], U32, name="values", align_bytes=64)
         nc.vector.tensor_copy(values[:], value_pool[:].bitcast(U32).indirect(column_list[:]))
 
         pieces = [(u, t, t + 2) for u in range(PAGES) for t in (0, 2)]
@@ -205,13 +207,13 @@ def tile_attend_pkv4_sink_kernel(tc, qT, k_words, k_scales, v_words, v_scales, v
             nc.scalar.activation(probs[u][:, t0:t1, :], neg_scores[u][:, t0:t1, :], ACT.Exp, bias=neg_max[:], scale=-1.0)
             for t in range(t0, t1):
                 nc.tensor.transpose(turned[u][:, t, :], probs[u][:, t, :], ident[:])
-        nc.scalar.activation(terms[:, SLOTS : SLOTS + 1], sink_col[:], ACT.Exp, bias=neg_max[:])
+        nc.scalar.activation(terms[:, SLOTS : SLOTS + 1], neg_sink[:], ACT.Exp, bias=neg_max[:], scale=-1.0)
         total = keep.tile([NQ, 1], F32, name="total")
         summed = keep.tile([NQ, SLOTS + 1], F32, name="summed")
         nc.scalar.activation(summed[:], terms[:, 0 : SLOTS + 1], ACT.Copy, accum_out=total[:])
 
         weights = []
-        sums = [psum.tile([NQ, HALF], F32, name="sums%d" % h) for h in range(2)]
+        sums = [psum.tile([NQ, HALF], F32, name="sums%d" % h, tag="sums%d" % h) for h in range(2)]
 
         def weigh(u):
             w_grouped = placed([P, NQ, PACK], BF16, "w_grouped%d" % u, WEIGHTS + W_BYTES * u)

@@ -13,6 +13,7 @@ FP8X4 = mybir.dt.float8_e4m3fn_x4
 FP4X4 = mybir.dt.float4_e2m1fn_x4
 ALU = mybir.AluOpType
 ACT = mybir.ActivationFunctionType
+AXIS = mybir.AxisListType
 
 P = 128
 PACK = 4
@@ -28,19 +29,18 @@ VALUE_ROW0 = 32
 FLOPS = 2 * NQ * SLOTS * (D + DV)
 
 KEY_WINDOW = 0
-VALUE_PLANE = KEY_WINDOW + SLOTS
+VALUE_PLANE = KEY_WINDOW + PASSES * SLOTS
 VALUE_POOL = VALUE_PLANE + PAGES * DV
-VALUE_WINDOW = VALUE_POOL + 4 * POOL_PAGES * DV
 Q_BYTES = 4 * PACK * NQ
 W_BYTES = 2 * NQ * PACK
-LAST_PAIRS = VALUE_WINDOW + POOL_PAGES * DV
+LAST_PAIRS = VALUE_POOL + 4 * POOL_PAGES * DV
 Q_SECOND = LAST_PAIRS + 4 * PAGE - 64
 SLOT_SCALES = Q_SECOND + Q_BYTES - 128
 Q_CAST = Q_SECOND + Q_BYTES
 LAST_KEYS = Q_CAST + W_BYTES
 KEY_SCALES = LAST_KEYS + 2 * PAGE - SLOTS // 2
 WEIGHTS = LAST_KEYS + 4 * PAGE
-HELD_KEYS = {(1, 1): Q_CAST, (2, 0): LAST_KEYS, (2, 1): LAST_KEYS + 2 * PAGE}
+HELD_KEYS = {(0, 1): Q_SECOND + PAGE, (1, 1): Q_CAST, (2, 0): LAST_KEYS, (2, 1): LAST_KEYS + 2 * PAGE}
 
 
 def tile_attend_pkv4_sink_kernel(tc, qT, k_words, k_scales, v_words, v_scales, vs, sink, offs, voffs, out):
@@ -58,7 +58,7 @@ def tile_attend_pkv4_sink_kernel(tc, qT, k_words, k_scales, v_words, v_scales, v
         nc.scalar.dma_start(sink_rows[P - 1 : P, :], sink[0].rearrange("q one -> one q"))
         key_scale_pool = placed([P, POOL], U8, "key_scale_pool", KEY_WINDOW)
         nc.vector.memset(key_scale_pool[:].bitcast(I32), 0)
-        value_scale_pool = placed([P, POOL_PAGES * DV], U8, "value_scale_pool", VALUE_WINDOW)
+        value_scale_pool = keep.tile([P, POOL_PAGES * DV], U8, name="value_scale_pool")
         nc.vector.memset(value_scale_pool[:].bitcast(I32), 0)
         ident = keep.tile([P, P], F32, name="ident")
         nc.vector.memset(ident[:], 0.0)
@@ -96,7 +96,12 @@ def tile_attend_pkv4_sink_kernel(tc, qT, k_words, k_scales, v_words, v_scales, v
         q_scales = [keep.tile([P, NQ], U8, name="q_scales%d" % o, align_bytes=64) for o in range(PASSES)]
 
         def cast_queries(o):
-            nc.scalar.activation(q_grouped[o][:], q_raw[o][:].rearrange("p j w -> p w j"), ACT.Copy, scale=-1.0)
+            nc.scalar.activation(
+                q_grouped[o][:].rearrange("p (c i) j -> p c j i", i=4),
+                q_raw[o][:].rearrange("p j (c i) -> p c j i", i=4),
+                ACT.Copy,
+                scale=-1.0,
+            )
 
         def quantize_queries(o):
             nc.vector.quantize_mx(q_codes[o][:].bitcast(FP8X4), q_scales[o][:], q_grouped[o][:].rearrange("p w j -> p (w j)"))
@@ -114,10 +119,10 @@ def tile_attend_pkv4_sink_kernel(tc, qT, k_words, k_scales, v_words, v_scales, v
         nc.vector.tensor_copy(value_scales[:], value_scale_pool[:].indirect(column_list[:]))
         q_raw.append(placed([P, PACK, NQ], F32, "q_raw1", Q_SECOND))
         nc.sync.dma_start(q_raw[1][:], q_rows[1])
-        key_planes = [placed([P, SLOTS], U8, "key_plane0", VALUE_WINDOW)]
+        key_planes = [placed([P, SLOTS], U8, "key_plane0", KEY_WINDOW)]
         move_rows(key_planes[0], key_scales, 0, PASSES * STEP)
         quantize_queries(0)
-        key_planes.append(placed([P, SLOTS], U8, "key_plane1", KEY_WINDOW))
+        key_planes.append(placed([P, SLOTS], U8, "key_plane1", KEY_WINDOW + SLOTS))
         move_rows(key_planes[1], key_scales, STEP, PASSES * STEP)
         value_pool = placed([P, POOL_PAGES * DV], I32, "value_pool", VALUE_POOL)
         nc.sync.dma_start(
@@ -178,8 +183,8 @@ def tile_attend_pkv4_sink_kernel(tc, qT, k_words, k_scales, v_words, v_scales, v
         gather_keys(1)
         part_keys(0, 0)
         part_keys(1, 0)
-        part_keys(0, 1)
         quantize_queries(1)
+        part_keys(0, 1)
         gather_keys(2)
         part_keys(1, 1)
         part_keys(2, 0)
@@ -189,17 +194,17 @@ def tile_attend_pkv4_sink_kernel(tc, qT, k_words, k_scales, v_words, v_scales, v
 
         dealt = [scores[u][:].rearrange("q (s t) -> q t s", t=PACK) for u in range(PAGES)]
         least = [keep.tile([NQ, 1], F32, name="least%d" % u) for u in range(PAGES)]
-        copies = [keep.tile([NQ, PACK, P], F32, name="neg_scores%d" % u) for u in range(PAGES)]
+        copies = {u: keep.tile([NQ, PACK, P], F32, name="neg_scores%d" % u) for u in (0, 2)}
         nc.vector.tensor_scalar(copies[0][:], dealt[0], 1.0, neg_sink[:], op0=ALU.mult, op1=ALU.min, accum_out=least[0][:])
-        nc.vector.tensor_scalar(copies[1][:], dealt[1], 1.0, None, op0=ALU.mult, op1=ALU.min, accum_out=least[1][:])
+        nc.vector.tensor_reduce(least[1][:], scores[1][:], axis=AXIS.X, op=ALU.min)
         nc.vector.tensor_scalar(copies[2][:], dealt[2], least[0][:], least[1][:], op0=ALU.min, op1=ALU.min, accum_out=least[2][:])
         neg_max = least[2]
-        neg_scores = [copies[0][:], copies[1][:], dealt[2]]
+        neg_scores = [copies[0][:], dealt[1], dealt[2]]
 
         values = keep.tile([P, PAGES * DV], U32, name="values", align_bytes=64)
         nc.vector.tensor_copy(values[:], value_pool[:].bitcast(U32).indirect(column_list[:]))
 
-        pieces = [(u, t, t + 2) for u in range(PAGES) for t in (0, 2)]
+        pieces = [(0, 0, 2), (0, 2, 3), (0, 3, 4)] + [(u, t, t + 2) for u in range(1, PAGES) for t in (0, 2)]
         terms = keep.tile([NQ, SLOTS + 8], F32, name="terms")
         probs = [terms[:, PAGE * u : PAGE * (u + 1)].rearrange("q (t s) -> q t s", t=PACK) for u in range(PAGES)]
         turned = [psum.tile([P, PACK, NQ], F32, name="turned_probs%d" % u, tag="turned%d" % u) for u in range(PAGES)]

@@ -40,7 +40,7 @@ Q_CAST = Q_SECOND + Q_BYTES
 LAST_KEYS = Q_CAST + W_BYTES
 KEY_SCALES = LAST_KEYS + 2 * PAGE - SLOTS // 2
 WEIGHTS = LAST_KEYS + 4 * PAGE
-HELD_KEYS = {(0, 1): Q_SECOND + PAGE, (1, 1): Q_CAST, (2, 0): LAST_KEYS, (2, 1): LAST_KEYS + 2 * PAGE}
+HELD_KEYS = {(0, 1): Q_SECOND + PAGE, (1, 1): Q_CAST}
 
 
 def tile_attend_pkv4_sink_kernel(tc, qT, k_words, k_scales, v_words, v_scales, vs, sink, offs, voffs, out):
@@ -166,14 +166,14 @@ def tile_attend_pkv4_sink_kernel(tc, qT, k_words, k_scales, v_words, v_scales, v
             else:
                 parted = keep.tile([P, PAGE], U16, name="keys%d_%d" % (u, o), align_bytes=64)
             nc.vector.tensor_copy(parted[:], key_pairs[u][:].bitcast(U16)[:, o : PASSES * PAGE : PASSES])
-            keys[(u, o)] = parted
+            keys[(u, o)] = parted[:]
 
         def score(u, o):
             nc.tensor.matmul_mx(
                 scores[u][:],
                 lhsT=q_codes[o][:].bitcast(FP8X4),
                 lhsT_scale=q_scales[o][:],
-                rhs=keys[(u, o)][:].bitcast(FP4X4),
+                rhs=keys[(u, o)].bitcast(FP4X4),
                 rhs_scale=key_planes[o][:, PAGE * u : PAGE * (u + 1)],
                 start=(o == 0),
                 stop=(o == PASSES - 1),
@@ -187,8 +187,10 @@ def tile_attend_pkv4_sink_kernel(tc, qT, k_words, k_scales, v_words, v_scales, v
         part_keys(0, 1)
         gather_keys(2)
         part_keys(1, 1)
-        part_keys(2, 0)
-        part_keys(2, 1)
+        last_keys = placed([P, PASSES, PAGE], U16, "keys2", LAST_KEYS)
+        nc.vector.tensor_copy(last_keys[:], key_pairs[2][:].bitcast(U16).rearrange("p (n o) -> p o n", o=PASSES))
+        for o in range(PASSES):
+            keys[(2, o)] = last_keys[:, o, :]
         for u, o in ((0, 0), (1, 0), (0, 1), (1, 1), (2, 0), (2, 1)):
             score(u, o)
 
@@ -204,7 +206,7 @@ def tile_attend_pkv4_sink_kernel(tc, qT, k_words, k_scales, v_words, v_scales, v
         values = keep.tile([P, PAGES * DV], U32, name="values", align_bytes=64)
         nc.vector.tensor_copy(values[:], value_pool[:].bitcast(U32).indirect(column_list[:]))
 
-        pieces = [(0, 0, 2), (0, 2, 3), (0, 3, 4)] + [(u, t, t + 2) for u in range(1, PAGES) for t in (0, 2)]
+        pieces = [(0, t, t + 1) for t in range(PACK)] + [(u, t, t + 2) for u in range(1, PAGES) for t in (0, 2)]
         terms = keep.tile([NQ, SLOTS + 8], F32, name="terms")
         probs = [terms[:, PAGE * u : PAGE * (u + 1)].rearrange("q (t s) -> q t s", t=PACK) for u in range(PAGES)]
         turned = [psum.tile([P, PACK, NQ], F32, name="turned_probs%d" % u, tag="turned%d" % u) for u in range(PAGES)]
@@ -250,11 +252,11 @@ def tile_attend_pkv4_sink_kernel(tc, qT, k_words, k_scales, v_words, v_scales, v
         weigh(2)
         multiply(1)
         multiply(2)
-        inverse = placed([NQ, 1], F32, "inverse", WEIGHTS + 2 * W_BYTES)
+        inverse = placed([NQ, 1], F32, "inverse", WEIGHTS + W_BYTES)
         nc.vector.reciprocal(inverse[:], total[:])
 
         results = [keep.tile([NQ, HALF], F32, name="result%d" % h) for h in range(2)]
-        nc.scalar.activation(results[0][:], sums[0][:], ACT.Copy, scale=inverse[:])
-        nc.vector.tensor_scalar(results[1][:], sums[1][:], inverse[:], None, op0=ALU.mult)
-        nc.scalar.dma_start(out[0][:, 0:HALF], results[0][:])
-        nc.sync.dma_start(out[0][:, HALF:DV], results[1][:])
+        nc.vector.tensor_scalar(results[0][:], sums[0][:], inverse[:], None, op0=ALU.mult)
+        nc.scalar.activation(results[1][:], sums[1][:], ACT.Copy, scale=inverse[:])
+        nc.sync.dma_start(out[0][:, 0:HALF], results[0][:])
+        nc.scalar.dma_start(out[0][:, HALF:DV], results[1][:])

@@ -37,9 +37,7 @@ LAST_PAIRS = VALUE_POOL + 4 * POOL_PAGES * DV
 Q_SECOND = LAST_PAIRS + 4 * PAGE - 64
 SLOT_SCALES = Q_SECOND + Q_BYTES - 128
 Q_CAST = Q_SECOND + Q_BYTES
-LAST_KEYS = Q_CAST + W_BYTES
-KEY_SCALES = LAST_KEYS + 2 * PAGE - SLOTS // 2
-WEIGHTS = LAST_KEYS + 4 * PAGE
+WEIGHTS = Q_CAST + W_BYTES
 HELD_KEYS = {(0, 1): Q_SECOND + PAGE, (1, 1): Q_CAST}
 
 
@@ -112,18 +110,23 @@ def tile_attend_pkv4_sink_kernel(tc, qT, k_words, k_scales, v_words, v_scales, v
                 rows = gathered[first : first + 3 * 4 * row_step + 1 : 4 * row_step, :]
                 nc.sync.dma_start(plane[j:P:32, :].bitcast(I32), rows.bitcast(I32))
 
+        def move_key_rows(planes, gathered):
+            for quad in (0, 2, 1, 3):
+                rows = gathered[32 * quad : 32 * (quad + 1) : STEP]
+                nc.sync.dma_start(planes[32 * quad : 32 * quad + 4].rearrange("p o n -> p (o n)").bitcast(I32), rows.bitcast(I32))
+
         cast_queries(0)
-        key_scales = placed([P, SLOTS], U8, "key_scales", KEY_SCALES)
+        key_scales = keep.tile([P, SLOTS], U8, name="key_scales", align_bytes=64)
         nc.vector.tensor_copy(key_scales[:], key_scale_pool[:].indirect(slot_list[:]))
         value_scales = keep.tile([P, PAGES * DV], U8, name="value_scales", align_bytes=64)
         nc.vector.tensor_copy(value_scales[:], value_scale_pool[:].indirect(column_list[:]))
         q_raw.append(placed([P, PACK, NQ], F32, "q_raw1", Q_SECOND))
         nc.sync.dma_start(q_raw[1][:], q_rows[1])
-        key_planes = [placed([P, SLOTS], U8, "key_plane0", KEY_WINDOW)]
-        move_rows(key_planes[0], key_scales, 0, PASSES * STEP)
+        early_planes = placed([P, PASSES, 2 * PAGE], U8, "early_planes", KEY_WINDOW)
+        move_key_rows(early_planes[:], key_scales[:, 0 : 2 * PAGE])
         quantize_queries(0)
-        key_planes.append(placed([P, SLOTS], U8, "key_plane1", KEY_WINDOW + SLOTS))
-        move_rows(key_planes[1], key_scales, STEP, PASSES * STEP)
+        last_planes = placed([P, PASSES, PAGE], U8, "last_planes", KEY_WINDOW + PASSES * 2 * PAGE)
+        move_key_rows(last_planes[:], key_scales[:, 2 * PAGE : SLOTS])
         value_pool = placed([P, POOL_PAGES * DV], I32, "value_pool", VALUE_POOL)
         nc.sync.dma_start(
             value_pool[:].rearrange("p (u e) -> p u e", u=POOL_PAGES),
@@ -174,7 +177,7 @@ def tile_attend_pkv4_sink_kernel(tc, qT, k_words, k_scales, v_words, v_scales, v
                 lhsT=q_codes[o][:].bitcast(FP8X4),
                 lhsT_scale=q_scales[o][:],
                 rhs=keys[(u, o)].bitcast(FP4X4),
-                rhs_scale=key_planes[o][:, PAGE * u : PAGE * (u + 1)],
+                rhs_scale=last_planes[:, o, :] if u == PAGES - 1 else early_planes[:, o, PAGE * u : PAGE * (u + 1)],
                 start=(o == 0),
                 stop=(o == PASSES - 1),
             )
@@ -187,7 +190,7 @@ def tile_attend_pkv4_sink_kernel(tc, qT, k_words, k_scales, v_words, v_scales, v
         part_keys(0, 1)
         gather_keys(2)
         part_keys(1, 1)
-        last_keys = placed([P, PASSES, PAGE], U16, "keys2", LAST_KEYS)
+        last_keys = keep.tile([P, PASSES, PAGE], U16, name="keys2", align_bytes=64)
         nc.vector.tensor_copy(last_keys[:], key_pairs[2][:].bitcast(U16).rearrange("p (n o) -> p o n", o=PASSES))
         for o in range(PASSES):
             keys[(2, o)] = last_keys[:, o, :]

@@ -66,16 +66,16 @@ def tile_attend_pkv4_sink_kernel(tc, qT, k_words, k_scales, v_words, v_scales, v
         nc.vector.memset(token_scale_pool[0 : P - 1, 0:EARLY], 0.0)
         nc.gpsimd.memset(token_scale_pool[0 : P - 1, EARLY - 8 : POOL], 0.0)
 
-        slot_list = lists.tile([P, SLOTS // 16], U16, name="slot_list")
-        nc.sync.dma_start(slot_list[:], offs)
         q_rows = qT[0].rearrange("(g p j) w -> g p j w", g=PASSES, j=PACK)
         q_raw = [keep.tile([P, PACK, NQ], F32, name="q_raw0")]
         nc.sync.dma_start(q_raw[0][:], q_rows[0])
-        nc.sync.dma_start(token_scale_pool[P - 1 : P, :], vs[0:1, :])
+        slot_list = lists.tile([P, SLOTS // 16], U16, name="slot_list")
+        nc.sync.dma_start(slot_list[:], offs)
+        nc.scalar.dma_start(token_scale_pool[P - 1 : P, :], vs[0:1, :])
         column_list = lists.tile([P, PAGES * DV // 16], U16, name="column_list")
         nc.sync.dma_start(column_list[:], voffs)
         nc.sync.dma_start(key_scale_pool[0:P:STEP, :].bitcast(I32), k_scales.bitcast(I32).rearrange("o f t -> f o t"))
-        nc.sync.dma_start(
+        nc.scalar.dma_start(
             value_scale_pool[VALUE_ROW0 : VALUE_ROW0 + 16 * STEP : STEP, :].bitcast(I32).rearrange("f (u e) -> f u e", u=POOL_PAGES),
             v_scales.bitcast(I32).rearrange("u f e -> f u e"),
         )

@@ -24,7 +24,6 @@ POOL_PAGES = POOL // PAGE
 PASSES = D // PAGE
 HALF = DV // 2
 STEP = 4
-EARLY = 3072
 VALUE_ROW0 = 32
 FLOPS = 2 * NQ * SLOTS * (D + DV)
 
@@ -63,8 +62,7 @@ def tile_attend_pkv4_sink_kernel(tc, qT, k_words, k_scales, v_words, v_scales, v
         make_identity(nc, ident[:], nomemset=True)
         nc.vector.memset(sink_rows[0 : P - 1, :], 0.0)
         token_scale_pool = keep.tile([P, POOL], F32, name="token_scale_pool")
-        nc.vector.memset(token_scale_pool[0 : P - 1, 0:EARLY], 0.0)
-        nc.gpsimd.memset(token_scale_pool[0 : P - 1, EARLY - 8 : POOL], 0.0)
+        nc.vector.memset(token_scale_pool[0 : P - 1, :], 0.0)
 
         q_rows = qT[0].rearrange("(g p j) w -> g p j w", g=PASSES, j=PACK)
         q_raw = [keep.tile([P, PACK, NQ], F32, name="q_raw0")]

@@ -23,21 +23,21 @@ PAGES = SLOTS // PAGE
 POOL_PAGES = POOL // PAGE
 PASSES = D // PAGE
 HALF = DV // 2
-STEP = 4
-VALUE_ROW0 = 32
+SCALE_ROWS = 16
+KEY_ROW0 = 32
 FLOPS = 2 * NQ * SLOTS * (D + DV)
 
-KEY_WINDOW = 0
-VALUE_PLANE = KEY_WINDOW + PASSES * SLOTS
-VALUE_POOL = VALUE_PLANE + PAGES * DV
 Q_BYTES = 4 * PACK * NQ
 W_BYTES = 2 * NQ * PACK
-LAST_PAIRS = VALUE_POOL + 4 * POOL_PAGES * DV
+KEYS_BYTES = 2 * PAGE
+KEY_WINDOW = 0
+Q_FIRST = KEY_WINDOW + POOL
+LAST_PAIRS = Q_FIRST + Q_BYTES
 Q_SECOND = LAST_PAIRS + 4 * PAGE - 64
 SLOT_SCALES = Q_SECOND + Q_BYTES - 128
-Q_CAST = Q_SECOND + Q_BYTES
-WEIGHTS = Q_CAST + W_BYTES
-HELD_KEYS = {(0, 1): Q_SECOND + PAGE, (1, 1): Q_CAST}
+LAST_KEYS = Q_SECOND + Q_BYTES
+VALUE_POOL = LAST_KEYS + KEYS_BYTES
+HELD_KEYS = {(1, 0): Q_FIRST, (0, 1): Q_FIRST + KEYS_BYTES, (1, 1): Q_SECOND + 64, (2, 1): LAST_KEYS}
 
 
 def tile_attend_pkv4_sink_kernel(tc, qT, k_words, k_scales, v_words, v_scales, vs, sink, offs, voffs, out):
@@ -51,78 +51,50 @@ def tile_attend_pkv4_sink_kernel(tc, qT, k_words, k_scales, v_words, v_scales, v
         def placed(shape, dtype, name, offset):
             return shared.tile(shape, dtype, name=name, offset=offset, align_bytes=64)
 
+        token_scale_pool = keep.tile([P, POOL], F32, name="token_scale_pool")
+        nc.scalar.dma_start(token_scale_pool[P - 1 : P, :], vs[0:1, :])
         sink_rows = keep.tile([P, NQ], F32, name="sink_rows")
         nc.scalar.dma_start(sink_rows[P - 1 : P, :], sink[0].rearrange("q one -> one q"))
         key_scale_pool = placed([P, POOL], U8, "key_scale_pool", KEY_WINDOW)
-        nc.vector.memset(key_scale_pool[:].bitcast(I32), 0)
-        value_scale_pool = keep.tile([P, POOL_PAGES * DV], U8, name="value_scale_pool")
-        nc.vector.memset(value_scale_pool[:].bitcast(I32), 0)
+        nc.sync.dma_start(
+            key_scale_pool[KEY_ROW0 : KEY_ROW0 + PASSES * SCALE_ROWS, :].bitcast(I32),
+            k_scales.bitcast(I32).rearrange("o f t -> f o t"),
+        )
+        slot_list = lists.tile([P, SLOTS // 16], U16, name="slot_list")
+        nc.sync.dma_start(slot_list[:], offs)
+        column_list = lists.tile([P, PAGES * DV // 16], U16, name="column_list")
+        nc.sync.dma_start(column_list[:], voffs)
+        key_pool = keep.tile([P, POOL], I32, name="key_pool")
+        nc.sync.dma_start(key_pool[:], k_words[0].rearrange("p t b -> p (t b)").bitcast(I32))
+        q_rows = qT[0].rearrange("(g p j) w -> g p j w", g=PASSES, j=PACK)
+        q_raw = [placed([P, PACK, NQ], F32, "q_raw%d" % o, (Q_FIRST, Q_SECOND)[o]) for o in range(PASSES)]
+        for o in range(PASSES):
+            nc.sync.dma_start(q_raw[o][:], q_rows[o])
+
         ident = keep.tile([P, P], F32, name="ident")
         nc.vector.memset(ident[:], 0.0)
         make_identity(nc, ident[:], nomemset=True)
         nc.vector.memset(sink_rows[0 : P - 1, :], 0.0)
-        token_scale_pool = keep.tile([P, POOL], F32, name="token_scale_pool")
         nc.vector.memset(token_scale_pool[0 : P - 1, :], 0.0)
-
-        q_rows = qT[0].rearrange("(g p j) w -> g p j w", g=PASSES, j=PACK)
-        q_raw = [keep.tile([P, PACK, NQ], F32, name="q_raw0")]
-        nc.sync.dma_start(q_raw[0][:], q_rows[0])
-        slot_list = lists.tile([P, SLOTS // 16], U16, name="slot_list")
-        nc.sync.dma_start(slot_list[:], offs)
-        nc.scalar.dma_start(token_scale_pool[P - 1 : P, :], vs[0:1, :])
-        column_list = lists.tile([P, PAGES * DV // 16], U16, name="column_list")
-        nc.sync.dma_start(column_list[:], voffs)
-        nc.sync.dma_start(key_scale_pool[0:P:STEP, :].bitcast(I32), k_scales.bitcast(I32).rearrange("o f t -> f o t"))
-        nc.scalar.dma_start(
-            value_scale_pool[VALUE_ROW0 : VALUE_ROW0 + 16 * STEP : STEP, :].bitcast(I32).rearrange("f (u e) -> f u e", u=POOL_PAGES),
-            v_scales.bitcast(I32).rearrange("u f e -> f u e"),
-        )
-        key_pool = keep.tile([P, POOL], I32, name="key_pool")
-        nc.sync.dma_start(key_pool[:], k_words[0].rearrange("p t b -> p (t b)").bitcast(I32))
-
-        neg_sink = keep.tile([P, 1], F32, name="neg_sink")
-        turned_sink = psum.tile([NQ, P], F32, name="turned_sink", tag="sums0")
-        nc.tensor.transpose(turned_sink[:], sink_rows[:], ident[:])
-        nc.scalar.activation(neg_sink[:], turned_sink[:, P - 1 : P], ACT.Copy, scale=-1.0)
-        q_grouped = [
-            keep.tile([P, NQ, PACK], BF16, name="q_grouped0", align_bytes=64),
-            placed([P, NQ, PACK], BF16, "q_grouped1", Q_CAST),
-        ]
-        q_codes = [keep.tile([P, NQ], U32, name="q_codes%d" % o, align_bytes=64) for o in range(PASSES)]
-        q_scales = [keep.tile([P, NQ], U8, name="q_scales%d" % o, align_bytes=64) for o in range(PASSES)]
-
-        def cast_queries(o):
-            nc.scalar.activation(
-                q_grouped[o][:].rearrange("p (c i) j -> p c j i", i=4),
-                q_raw[o][:].rearrange("p j (c i) -> p c j i", i=4),
-                ACT.Copy,
-                scale=-1.0,
-            )
-
-        def quantize_queries(o):
-            nc.vector.quantize_mx(q_codes[o][:].bitcast(FP8X4), q_scales[o][:], q_grouped[o][:].rearrange("p w j -> p (w j)"))
-
-        def move_rows(plane, gathered, row0, row_step):
-            for j in range(4):
-                first = row0 + row_step * j
-                rows = gathered[first : first + 3 * 4 * row_step + 1 : 4 * row_step, :]
-                nc.sync.dma_start(plane[j:P:32, :].bitcast(I32), rows.bitcast(I32))
+        nc.vector.memset(key_scale_pool[0:KEY_ROW0, :].bitcast(I32), 0)
+        nc.vector.memset(key_scale_pool[KEY_ROW0 + PASSES * SCALE_ROWS : P, :].bitcast(I32), 0)
+        key_scales = keep.tile([P, SLOTS], U8, name="key_scales", align_bytes=64)
+        nc.vector.tensor_copy(key_scales[:], key_scale_pool[:].indirect(slot_list[:]))
+        value_scale_pool = keep.tile([P, POOL_PAGES * DV], U8, name="value_scale_pool")
+        nc.vector.memset(value_scale_pool[:].bitcast(I32), 0)
 
         def move_key_rows(planes, gathered):
             for quad in (0, 2, 1, 3):
-                rows = gathered[32 * quad : 32 * (quad + 1) : STEP]
+                rows = gathered[KEY_ROW0 + 8 * quad : KEY_ROW0 + 8 * (quad + 1)]
                 nc.sync.dma_start(planes[32 * quad : 32 * quad + 4].rearrange("p o n -> p (o n)").bitcast(I32), rows.bitcast(I32))
 
-        cast_queries(0)
-        key_scales = keep.tile([P, SLOTS], U8, name="key_scales", align_bytes=64)
-        nc.vector.tensor_copy(key_scales[:], key_scale_pool[:].indirect(slot_list[:]))
-        value_scales = keep.tile([P, PAGES * DV], U8, name="value_scales", align_bytes=64)
-        nc.vector.tensor_copy(value_scales[:], value_scale_pool[:].indirect(column_list[:]))
-        q_raw.append(placed([P, PACK, NQ], F32, "q_raw1", Q_SECOND))
-        nc.sync.dma_start(q_raw[1][:], q_rows[1])
         early_planes = placed([P, PASSES, 2 * PAGE], U8, "early_planes", KEY_WINDOW)
         move_key_rows(early_planes[:], key_scales[:, 0 : 2 * PAGE])
-        quantize_queries(0)
+        value_scale_rows = v_scales.bitcast(I32).rearrange("u (s j) e -> j s u e", j=4)
+        for j in range(4):
+            nc.sync.dma_start(
+                value_scale_pool[j:P:32, :].bitcast(I32).rearrange("s (u e) -> s u e", u=POOL_PAGES), value_scale_rows[j]
+            )
         last_planes = placed([P, PASSES, PAGE], U8, "last_planes", KEY_WINDOW + PASSES * 2 * PAGE)
         move_key_rows(last_planes[:], key_scales[:, 2 * PAGE : SLOTS])
         value_pool = placed([P, POOL_PAGES * DV], I32, "value_pool", VALUE_POOL)
@@ -131,8 +103,10 @@ def tile_attend_pkv4_sink_kernel(tc, qT, k_words, k_scales, v_words, v_scales, v
             v_words.rearrange("u p e r -> p u (e r)").bitcast(I32),
         )
 
-        value_plane = placed([P, PAGES * DV], U8, "value_plane", VALUE_PLANE)
-        move_rows(value_plane, value_scales, VALUE_ROW0, STEP)
+        neg_sink = keep.tile([P, 1], F32, name="neg_sink")
+        turned_sink = psum.tile([NQ, P], F32, name="turned_sink", tag="sums0")
+        nc.tensor.transpose(turned_sink[:], sink_rows[:], ident[:])
+        nc.scalar.activation(neg_sink[:], turned_sink[:, P - 1 : P], ACT.Copy, scale=-1.0)
 
         turned_scales = []
         for u in range(PAGES):
@@ -142,7 +116,17 @@ def tile_attend_pkv4_sink_kernel(tc, qT, k_words, k_scales, v_words, v_scales, v
             for t in range(PACK):
                 nc.tensor.transpose(bank[:, t, :], token_scales[:, t:PAGE:PACK], ident[:])
             turned_scales.append(bank)
-        cast_queries(1)
+
+        q_grouped = [keep.tile([P, NQ, PACK], BF16, name="q_grouped%d" % o, align_bytes=64) for o in range(PASSES)]
+        q_codes = [keep.tile([P, NQ], U32, name="q_codes%d" % o, align_bytes=64) for o in range(PASSES)]
+        q_scales = [keep.tile([P, NQ], U8, name="q_scales%d" % o, align_bytes=64) for o in range(PASSES)]
+        for o in range(PASSES):
+            nc.scalar.activation(
+                q_grouped[o][:].rearrange("p (c i) j -> p c j i", i=4),
+                q_raw[o][:].rearrange("p j (c i) -> p c j i", i=4),
+                ACT.Copy,
+                scale=-1.0,
+            )
         slot_scales = []
         for u in range(PAGES):
             spread = shared.tile([P, PACK], F32, name="slot_scales%d" % u, offset=SLOT_SCALES + 32 * u)
@@ -152,6 +136,9 @@ def tile_attend_pkv4_sink_kernel(tc, qT, k_words, k_scales, v_words, v_scales, v
         key_pairs = []
         keys = {}
         scores = [psum.tile([NQ, PAGE], F32, name="scores%d" % u) for u in range(PAGES)]
+
+        def quantize_queries(o):
+            nc.vector.quantize_mx(q_codes[o][:].bitcast(FP8X4), q_scales[o][:], q_grouped[o][:].rearrange("p w j -> p (w j)"))
 
         def gather_keys(u):
             if u == PAGES - 1:
@@ -183,27 +170,32 @@ def tile_attend_pkv4_sink_kernel(tc, qT, k_words, k_scales, v_words, v_scales, v
         gather_keys(0)
         gather_keys(1)
         part_keys(0, 0)
+        quantize_queries(0)
         part_keys(1, 0)
-        quantize_queries(1)
         part_keys(0, 1)
+        quantize_queries(1)
         gather_keys(2)
         part_keys(1, 1)
-        last_keys = keep.tile([P, PASSES, PAGE], U16, name="keys2", align_bytes=64)
-        nc.vector.tensor_copy(last_keys[:], key_pairs[2][:].bitcast(U16).rearrange("p (n o) -> p o n", o=PASSES))
-        for o in range(PASSES):
-            keys[(2, o)] = last_keys[:, o, :]
+        part_keys(2, 0)
+        part_keys(2, 1)
         for u, o in ((0, 0), (1, 0), (0, 1), (1, 1), (2, 0), (2, 1)):
             score(u, o)
 
         dealt = [scores[u][:].rearrange("q (s t) -> q t s", t=PACK) for u in range(PAGES)]
         least = [keep.tile([NQ, 1], F32, name="least%d" % u) for u in range(PAGES)]
-        copies = {u: keep.tile([NQ, PACK, P], F32, name="neg_scores%d" % u) for u in (0, 2)}
-        nc.vector.tensor_scalar(copies[0][:], dealt[0], 1.0, neg_sink[:], op0=ALU.mult, op1=ALU.min, accum_out=least[0][:])
+        first_scores = keep.tile([NQ, PACK, P], F32, name="first_scores")
+        clamped = keep.tile([NQ, PAGE], F32, name="clamped")
+        first_value_plane = placed([P, DV], U8, "first_value_plane", HELD_KEYS[(1, 1)])
+        later_value_planes = placed([P, (PAGES - 1) * DV], U8, "later_value_planes", HELD_KEYS[(2, 1)])
+        nc.vector.tensor_scalar(first_scores[:], dealt[0], 1.0, neg_sink[:], op0=ALU.mult, op1=ALU.min, accum_out=least[0][:])
         nc.vector.tensor_reduce(least[1][:], scores[1][:], axis=AXIS.X, op=ALU.min)
-        nc.vector.tensor_scalar(copies[2][:], dealt[2], least[0][:], least[1][:], op0=ALU.min, op1=ALU.min, accum_out=least[2][:])
+        nc.vector.tensor_copy(first_value_plane[:], value_scale_pool[:].indirect(column_list[:, 0 : DV // 16]))
+        nc.vector.tensor_scalar(clamped[:], scores[2][:], least[0][:], least[1][:], op0=ALU.min, op1=ALU.min, accum_out=least[2][:])
         neg_max = least[2]
-        neg_scores = [copies[0][:], dealt[1], dealt[2]]
+        neg_scores = [first_scores[:], dealt[1], dealt[2]]
 
+        nc.vector.tensor_copy(later_value_planes[:], value_scale_pool[:].indirect(column_list[:, DV // 16 : PAGES * DV // 16]))
+        value_planes = [first_value_plane[:], later_value_planes[:, 0:DV], later_value_planes[:, DV : 2 * DV]]
         values = keep.tile([P, PAGES * DV], U32, name="values", align_bytes=64)
         nc.vector.tensor_copy(values[:], value_pool[:].bitcast(U32).indirect(column_list[:]))
 
@@ -224,7 +216,7 @@ def tile_attend_pkv4_sink_kernel(tc, qT, k_words, k_scales, v_words, v_scales, v
         sums = [psum.tile([NQ, HALF], F32, name="sums%d" % h, tag="sums%d" % h) for h in range(2)]
 
         def weigh(u):
-            w_grouped = placed([P, NQ, PACK], BF16, "w_grouped%d" % u, WEIGHTS + W_BYTES * u)
+            w_grouped = placed([P, NQ, PACK], BF16, "w_grouped%d" % u, VALUE_POOL + W_BYTES * u)
             nc.vector.tensor_tensor(
                 w_grouped[:], turned[u][:].rearrange("p t q -> p q t"),
                 slot_scales[u][:].unsqueeze(1).to_broadcast([P, NQ, PACK]), ALU.mult,
@@ -236,13 +228,12 @@ def tile_attend_pkv4_sink_kernel(tc, qT, k_words, k_scales, v_words, v_scales, v
             w_scales = keep.tile([P, NQ], U8, name="w_scales%d" % u, align_bytes=64)
             nc.vector.quantize_mx(w_codes[:].bitcast(FP8X4), w_scales[:], weights[u][:].rearrange("p q t -> p (q t)"))
             for h in range(2):
-                columns = slice(DV * u + HALF * h, DV * u + HALF * (h + 1))
                 nc.tensor.matmul_mx(
                     sums[h][:],
                     lhsT=w_codes[:].bitcast(FP8X4),
                     lhsT_scale=w_scales[:],
-                    rhs=values[:, columns].bitcast(FP8X4),
-                    rhs_scale=value_plane[:, columns],
+                    rhs=values[:, DV * u + HALF * h : DV * u + HALF * (h + 1)].bitcast(FP8X4),
+                    rhs_scale=value_planes[u][:, HALF * h : HALF * (h + 1)],
                     start=(u == 0),
                     stop=(u == PAGES - 1),
                 )
@@ -253,7 +244,7 @@ def tile_attend_pkv4_sink_kernel(tc, qT, k_words, k_scales, v_words, v_scales, v
         weigh(2)
         multiply(1)
         multiply(2)
-        inverse = placed([NQ, 1], F32, "inverse", WEIGHTS + W_BYTES)
+        inverse = placed([NQ, 1], F32, "inverse", VALUE_POOL + W_BYTES)
         nc.vector.reciprocal(inverse[:], total[:])
 
         results = [keep.tile([NQ, HALF], F32, name="result%d" % h) for h in range(2)]

@@ -24,7 +24,7 @@ POOL_PAGES = POOL // PAGE
 PASSES = D // PAGE
 HALF = DV // 2
 SCALE_ROWS = 16
-KEY_ROW0 = 32
+KEY_ROW0 = 96
 FLOPS = 2 * NQ * SLOTS * (D + DV)
 
 Q_BYTES = 4 * PACK * NQ
@@ -77,7 +77,6 @@ def tile_attend_pkv4_sink_kernel(tc, qT, k_words, k_scales, v_words, v_scales, v
         nc.vector.memset(sink_rows[0 : P - 1, :], 0.0)
         nc.vector.memset(token_scale_pool[0 : P - 1, :], 0.0)
         nc.vector.memset(key_scale_pool[0:KEY_ROW0, :].bitcast(I32), 0)
-        nc.vector.memset(key_scale_pool[KEY_ROW0 + PASSES * SCALE_ROWS : P, :].bitcast(I32), 0)
         key_scales = keep.tile([P, SLOTS], U8, name="key_scales", align_bytes=64)
         nc.vector.tensor_copy(key_scales[:], key_scale_pool[:].indirect(slot_list[:]))
         value_scale_pool = keep.tile([P, POOL_PAGES * DV], U8, name="value_scale_pool")

@@ -188,17 +188,19 @@ def tile_attend_pkv4_sink_kernel(tc, qT, k_words, k_scales, v_words, v_scales, v
         later_value_planes = placed([P, (PAGES - 1) * DV], U8, "later_value_planes", HELD_KEYS[(2, 1)])
         nc.vector.tensor_scalar(first_scores[:], dealt[0], 1.0, neg_sink[:], op0=ALU.mult, op1=ALU.min, accum_out=least[0][:])
         nc.vector.tensor_reduce(least[1][:], scores[1][:], axis=AXIS.X, op=ALU.min)
+        second_scores = keep.tile([NQ, PACK, P], F32, name="second_scores")
+        nc.scalar.activation(second_scores[:], dealt[1], ACT.Copy)
         nc.vector.tensor_copy(first_value_plane[:], value_scale_pool[:].indirect(column_list[:, 0 : DV // 16]))
         nc.vector.tensor_scalar(clamped[:], scores[2][:], least[0][:], least[1][:], op0=ALU.min, op1=ALU.min, accum_out=least[2][:])
         neg_max = least[2]
-        neg_scores = [first_scores[:], dealt[1], dealt[2]]
+        neg_scores = [first_scores[:], second_scores[:], dealt[2]]
 
         nc.vector.tensor_copy(later_value_planes[:], value_scale_pool[:].indirect(column_list[:, DV // 16 : PAGES * DV // 16]))
         value_planes = [first_value_plane[:], later_value_planes[:, 0:DV], later_value_planes[:, DV : 2 * DV]]
         values = keep.tile([P, PAGES * DV], U32, name="values", align_bytes=64)
         nc.vector.tensor_copy(values[:], value_pool[:].bitcast(U32).indirect(column_list[:]))
 
-        pieces = [(0, t, t + 1) for t in range(PACK)] + [(u, t, t + 2) for u in range(1, PAGES) for t in (0, 2)]
+        pieces = [(0, t, t + 1) for t in range(PACK)] + [(u, t0, t1) for u in range(1, PAGES) for t0, t1 in ((0, 2), (2, 3), (3, 4))]
         terms = keep.tile([NQ, SLOTS + 8], F32, name="terms")
         probs = [terms[:, PAGE * u : PAGE * (u + 1)].rearrange("q (t s) -> q t s", t=PACK) for u in range(PAGES)]
         turned = [psum.tile([P, PACK, NQ], F32, name="turned_probs%d" % u, tag="turned%d" % u) for u in range(PAGES)]

@@ -37,6 +37,7 @@ Q_SECOND = LAST_PAIRS + 4 * PAGE - 64
 SLOT_SCALES = Q_SECOND + Q_BYTES - 128
 LAST_KEYS = Q_SECOND + Q_BYTES
 VALUE_POOL = LAST_KEYS + KEYS_BYTES
+WEIGHTS = VALUE_POOL + 4 * POOL_PAGES * DV
 HELD_KEYS = {(1, 0): Q_FIRST, (0, 1): Q_FIRST + KEYS_BYTES, (1, 1): Q_SECOND + 64, (2, 1): LAST_KEYS}
 
 
@@ -217,7 +218,7 @@ def tile_attend_pkv4_sink_kernel(tc, qT, k_words, k_scales, v_words, v_scales, v
         sums = [psum.tile([NQ, HALF], F32, name="sums%d" % h, tag="sums%d" % h) for h in range(2)]
 
         def weigh(u):
-            w_grouped = placed([P, NQ, PACK], BF16, "w_grouped%d" % u, VALUE_POOL + W_BYTES * u)
+            w_grouped = placed([P, NQ, PACK], BF16, "w_grouped%d" % u, WEIGHTS + W_BYTES * u)
             nc.vector.tensor_tensor(
                 w_grouped[:], turned[u][:].rearrange("p t q -> p q t"),
                 slot_scales[u][:].unsqueeze(1).to_broadcast([P, NQ, PACK]), ALU.mult,
@@ -245,7 +246,7 @@ def tile_attend_pkv4_sink_kernel(tc, qT, k_words, k_scales, v_words, v_scales, v
         weigh(2)
         multiply(1)
         multiply(2)
-        inverse = placed([NQ, 1], F32, "inverse", VALUE_POOL + W_BYTES)
+        inverse = placed([NQ, 1], F32, "inverse", WEIGHTS + W_BYTES)
         nc.vector.reciprocal(inverse[:], total[:])
 
         results = [keep.tile([NQ, HALF], F32, name="result%d" % h) for h in range(2)]

@@ -63,8 +63,6 @@ def tile_attend_pkv4_sink_kernel(tc, qT, k_words, k_scales, v_words, v_scales, v
         )
         slot_list = lists.tile([P, SLOTS // 16], U16, name="slot_list")
         nc.sync.dma_start(slot_list[:], offs)
-        column_list = lists.tile([P, PAGES * DV // 16], U16, name="column_list")
-        nc.sync.dma_start(column_list[:], voffs)
         key_pool = keep.tile([P, POOL], I32, name="key_pool")
         nc.sync.dma_start(key_pool[:], k_words[0].rearrange("p t b -> p (t b)").bitcast(I32))
         q_rows = qT[0].rearrange("(g p j) w -> g p j w", g=PASSES, j=PACK)
@@ -90,6 +88,8 @@ def tile_attend_pkv4_sink_kernel(tc, qT, k_words, k_scales, v_words, v_scales, v
 
         early_planes = placed([P, PASSES, 2 * PAGE], U8, "early_planes", KEY_WINDOW)
         move_key_rows(early_planes[:], key_scales[:, 0 : 2 * PAGE])
+        column_list = lists.tile([P, PAGES * DV // 16], U16, name="column_list")
+        nc.sync.dma_start(column_list[:], voffs)
         value_scale_rows = v_scales.bitcast(I32).rearrange("u (s j) e -> j s u e", j=4)
         for j in range(4):
             nc.sync.dma_start(

@@ -33,12 +33,12 @@ KEYS_BYTES = 2 * PAGE
 KEY_WINDOW = 0
 Q_FIRST = KEY_WINDOW + POOL
 LAST_PAIRS = Q_FIRST + Q_BYTES
-Q_SECOND = LAST_PAIRS + 4 * PAGE - 64
+Q_SECOND = LAST_PAIRS + 4 * PAGE - 256
 SLOT_SCALES = Q_SECOND + Q_BYTES - 128
 LAST_KEYS = Q_SECOND + Q_BYTES
 VALUE_POOL = LAST_KEYS + KEYS_BYTES
 WEIGHTS = VALUE_POOL + 4 * POOL_PAGES * DV
-HELD_KEYS = {(1, 0): Q_FIRST, (0, 1): Q_FIRST + KEYS_BYTES, (1, 1): Q_SECOND + 64, (2, 1): LAST_KEYS}
+HELD_KEYS = {(1, 0): Q_FIRST, (0, 1): Q_FIRST + KEYS_BYTES, (1, 1): Q_SECOND + 256, (2, 1): LAST_KEYS}
 
 
 def tile_attend_pkv4_sink_kernel(tc, qT, k_words, k_scales, v_words, v_scales, vs, sink, offs, voffs, out):
@@ -49,10 +49,10 @@ def tile_attend_pkv4_sink_kernel(tc, qT, k_words, k_scales, v_words, v_scales, v
         shared = ctx.enter_context(tc.tile_pool(name="shared", bufs=1))
         psum = ctx.enter_context(tc.psum_pool(name="psum", bufs=1))
 
-        def placed(shape, dtype, name, offset):
-            return shared.tile(shape, dtype, name=name, offset=offset, align_bytes=64)
+        def placed(shape, dtype, name, offset, align=64):
+            return shared.tile(shape, dtype, name=name, offset=offset, align_bytes=align)
 
-        token_scale_pool = keep.tile([P, POOL], F32, name="token_scale_pool")
+        token_scale_pool = keep.tile([P, POOL], F32, name="token_scale_pool", align_bytes=256)
         nc.scalar.dma_start(token_scale_pool[P - 1 : P, :], vs[0:1, :])
         sink_rows = keep.tile([P, NQ], F32, name="sink_rows")
         nc.scalar.dma_start(sink_rows[P - 1 : P, :], sink[0].rearrange("q one -> one q"))
@@ -63,10 +63,10 @@ def tile_attend_pkv4_sink_kernel(tc, qT, k_words, k_scales, v_words, v_scales, v
         )
         slot_list = lists.tile([P, SLOTS // 16], U16, name="slot_list")
         nc.sync.dma_start(slot_list[:], offs)
-        key_pool = keep.tile([P, POOL], I32, name="key_pool")
+        key_pool = keep.tile([P, POOL], I32, name="key_pool", align_bytes=256)
         nc.sync.dma_start(key_pool[:], k_words[0].rearrange("p t b -> p (t b)").bitcast(I32))
         q_rows = qT[0].rearrange("(g p j) w -> g p j w", g=PASSES, j=PACK)
-        q_raw = [placed([P, PACK, NQ], F32, "q_raw%d" % o, (Q_FIRST, Q_SECOND)[o]) for o in range(PASSES)]
+        q_raw = [placed([P, PACK, NQ], F32, "q_raw%d" % o, (Q_FIRST, Q_SECOND)[o], 256) for o in range(PASSES)]
         for o in range(PASSES):
             nc.sync.dma_start(q_raw[o][:], q_rows[o])
 
@@ -97,7 +97,7 @@ def tile_attend_pkv4_sink_kernel(tc, qT, k_words, k_scales, v_words, v_scales, v
             )
         last_planes = placed([P, PASSES, PAGE], U8, "last_planes", KEY_WINDOW + PASSES * 2 * PAGE)
         move_key_rows(last_planes[:], key_scales[:, 2 * PAGE : SLOTS])
-        value_pool = placed([P, POOL_PAGES * DV], I32, "value_pool", VALUE_POOL)
+        value_pool = placed([P, POOL_PAGES * DV], I32, "value_pool", VALUE_POOL, 256)
         nc.sync.dma_start(
             value_pool[:].rearrange("p (u e) -> p u e", u=POOL_PAGES),
             v_words.rearrange("u p e r -> p u (e r)").bitcast(I32),
@@ -249,7 +249,7 @@ def tile_attend_pkv4_sink_kernel(tc, qT, k_words, k_scales, v_words, v_scales, v
         inverse = placed([NQ, 1], F32, "inverse", WEIGHTS + W_BYTES)
         nc.vector.reciprocal(inverse[:], total[:])
 
-        results = [keep.tile([NQ, HALF], F32, name="result%d" % h) for h in range(2)]
+        results = [keep.tile([NQ, HALF], F32, name="result%d" % h, align_bytes=256) for h in range(2)]
         nc.vector.tensor_scalar(results[0][:], sums[0][:], inverse[:], None, op0=ALU.mult)
         nc.scalar.activation(results[1][:], sums[1][:], ACT.Copy, scale=inverse[:])
         nc.sync.dma_start(out[0][:, 0:HALF], results[0][:])

@@ -24,14 +24,15 @@ POOL_PAGES = POOL // PAGE
 PASSES = D // PAGE
 HALF = DV // 2
 SCALE_ROWS = 16
-KEY_ROW0 = 96
+KEY_ROW0 = 32
 FLOPS = 2 * NQ * SLOTS * (D + DV)
 
 Q_BYTES = 4 * PACK * NQ
 W_BYTES = 2 * NQ * PACK
 KEYS_BYTES = 2 * PAGE
 KEY_WINDOW = 0
-Q_FIRST = KEY_WINDOW + POOL
+VALUE_WINDOW = KEY_WINDOW + POOL - 64
+Q_FIRST = KEY_WINDOW + POOL + POOL_PAGES * DV
 LAST_PAIRS = Q_FIRST + Q_BYTES
 Q_SECOND = LAST_PAIRS + 4 * PAGE - 256
 SLOT_SCALES = Q_SECOND + Q_BYTES - 128
@@ -76,10 +77,11 @@ def tile_attend_pkv4_sink_kernel(tc, qT, k_words, k_scales, v_words, v_scales, v
         nc.vector.memset(sink_rows[0 : P - 1, :], 0.0)
         nc.vector.memset(token_scale_pool[0 : P - 1, :], 0.0)
         nc.vector.memset(key_scale_pool[0:KEY_ROW0, :].bitcast(I32), 0)
+        nc.vector.memset(key_scale_pool[2 * KEY_ROW0 : P, :].bitcast(I32), 0)
         key_scales = keep.tile([P, SLOTS], U8, name="key_scales", align_bytes=64)
         nc.vector.tensor_copy(key_scales[:], key_scale_pool[:].indirect(slot_list[:]))
-        value_scale_pool = keep.tile([P, POOL_PAGES * DV], U8, name="value_scale_pool")
-        nc.vector.memset(value_scale_pool[:].bitcast(I32), 0)
+        value_scale_pool = placed([P, POOL_PAGES * DV], U8, "value_scale_pool", VALUE_WINDOW)
+        nc.gpsimd.memset(value_scale_pool[:].bitcast(I32), 0)
 
         def move_key_rows(planes, gathered):
             for quad in (0, 2, 1, 3):

from contextlib import ExitStack

import concourse.mybir as mybir
from concourse.masks import make_identity

F32 = mybir.dt.float32
BF16 = mybir.dt.bfloat16
I32 = mybir.dt.int32
U32 = mybir.dt.uint32
U16 = mybir.dt.uint16
U8 = mybir.dt.uint8
FP8X4 = mybir.dt.float8_e4m3fn_x4
FP4X4 = mybir.dt.float4_e2m1fn_x4
ALU = mybir.AluOpType
ACT = mybir.ActivationFunctionType
AXIS = mybir.AxisListType

P = 128
PACK = 4
PAGE = 512
SLOTS, POOL, D, DV, NQ = 1536, 4096, 1024, 256, 128
PAGES = SLOTS // PAGE
POOL_PAGES = POOL // PAGE
PASSES = D // PAGE
HALF = DV // 2
SCALE_ROWS = 16
KEY_ROW0 = 32
FLOPS = 2 * NQ * SLOTS * (D + DV)

Q_BYTES = 4 * PACK * NQ
W_BYTES = 2 * NQ * PACK
KEYS_BYTES = 2 * PAGE
KEY_WINDOW = 0
VALUE_WINDOW = KEY_WINDOW + POOL - 64
Q_FIRST = KEY_WINDOW + POOL + POOL_PAGES * DV
LAST_PAIRS = Q_FIRST + Q_BYTES
Q_SECOND = LAST_PAIRS + 4 * PAGE - 256
SLOT_SCALES = Q_SECOND + Q_BYTES - 128
LAST_KEYS = Q_SECOND + Q_BYTES
VALUE_POOL = LAST_KEYS + KEYS_BYTES
WEIGHTS = VALUE_POOL + 4 * POOL_PAGES * DV
HELD_KEYS = {(1, 0): Q_FIRST, (0, 1): Q_FIRST + KEYS_BYTES, (1, 1): Q_SECOND + 256, (2, 1): LAST_KEYS}


def tile_attend_pkv4_sink_kernel(tc, qT, k_words, k_scales, v_words, v_scales, vs, sink, offs, voffs, out):
    nc = tc.nc
    with ExitStack() as ctx:
        lists = ctx.enter_context(tc.tile_pool(name="lists", bufs=1))
        keep = ctx.enter_context(tc.tile_pool(name="keep", bufs=1))
        shared = ctx.enter_context(tc.tile_pool(name="shared", bufs=1))
        psum = ctx.enter_context(tc.psum_pool(name="psum", bufs=1))

        def placed(shape, dtype, name, offset, align=64):
            return shared.tile(shape, dtype, name=name, offset=offset, align_bytes=align)

        token_scale_pool = keep.tile([P, POOL], F32, name="token_scale_pool", align_bytes=256)
        nc.scalar.dma_start(token_scale_pool[P - 1 : P, :], vs[0:1, :])
        sink_rows = keep.tile([P, NQ], F32, name="sink_rows")
        nc.scalar.dma_start(sink_rows[P - 1 : P, :], sink[0].rearrange("q one -> one q"))
        key_scale_pool = placed([P, POOL], U8, "key_scale_pool", KEY_WINDOW)
        nc.sync.dma_start(
            key_scale_pool[KEY_ROW0 : KEY_ROW0 + PASSES * SCALE_ROWS, :].bitcast(I32),
            k_scales.bitcast(I32).rearrange("o f t -> f o t"),
        )
        slot_list = lists.tile([P, SLOTS // 16], U16, name="slot_list")
        nc.sync.dma_start(slot_list[:], offs)
        key_pool = keep.tile([P, POOL], I32, name="key_pool", align_bytes=256)
        nc.sync.dma_start(key_pool[:], k_words[0].rearrange("p t b -> p (t b)").bitcast(I32))
        q_rows = qT[0].rearrange("(g p j) w -> g p j w", g=PASSES, j=PACK)
        q_raw = [placed([P, PACK, NQ], F32, "q_raw%d" % o, (Q_FIRST, Q_SECOND)[o], 256) for o in range(PASSES)]
        for o in range(PASSES):
            nc.sync.dma_start(q_raw[o][:], q_rows[o])

        ident = keep.tile([P, P], F32, name="ident")
        nc.vector.memset(ident[:], 0.0)
        make_identity(nc, ident[:], nomemset=True)
        nc.vector.memset(sink_rows[0 : P - 1, :], 0.0)
        nc.vector.memset(token_scale_pool[0 : P - 1, :], 0.0)
        nc.vector.memset(key_scale_pool[0:KEY_ROW0, :].bitcast(I32), 0)
        nc.vector.memset(key_scale_pool[2 * KEY_ROW0 : P, :].bitcast(I32), 0)
        key_scales = keep.tile([P, SLOTS], U8, name="key_scales", align_bytes=64)
        nc.vector.tensor_copy(key_scales[:], key_scale_pool[:].indirect(slot_list[:]))
        value_scale_pool = placed([P, POOL_PAGES * DV], U8, "value_scale_pool", VALUE_WINDOW)
        nc.gpsimd.memset(value_scale_pool[:].bitcast(I32), 0)

        def move_key_rows(planes, gathered):
            for quad in (0, 2, 1, 3):
                rows = gathered[KEY_ROW0 + 8 * quad : KEY_ROW0 + 8 * (quad + 1)]
                nc.sync.dma_start(planes[32 * quad : 32 * quad + 4].rearrange("p o n -> p (o n)").bitcast(I32), rows.bitcast(I32))

        early_planes = placed([P, PASSES, 2 * PAGE], U8, "early_planes", KEY_WINDOW)
        move_key_rows(early_planes[:], key_scales[:, 0 : 2 * PAGE])
        column_list = lists.tile([P, PAGES * DV // 16], U16, name="column_list")
        nc.sync.dma_start(column_list[:], voffs)
        value_scale_rows = v_scales.bitcast(I32).rearrange("u (s j) e -> j s u e", j=4)
        for j in range(4):
            nc.sync.dma_start(
                value_scale_pool[j:P:32, :].bitcast(I32).rearrange("s (u e) -> s u e", u=POOL_PAGES), value_scale_rows[j]
            )
        last_planes = placed([P, PASSES, PAGE], U8, "last_planes", KEY_WINDOW + PASSES * 2 * PAGE)
        move_key_rows(last_planes[:], key_scales[:, 2 * PAGE : SLOTS])
        value_pool = placed([P, POOL_PAGES * DV], I32, "value_pool", VALUE_POOL, 256)
        nc.sync.dma_start(
            value_pool[:].rearrange("p (u e) -> p u e", u=POOL_PAGES),
            v_words.rearrange("u p e r -> p u (e r)").bitcast(I32),
        )

        neg_sink = keep.tile([P, 1], F32, name="neg_sink")
        turned_sink = psum.tile([NQ, P], F32, name="turned_sink", tag="sums0")
        nc.tensor.transpose(turned_sink[:], sink_rows[:], ident[:])
        nc.scalar.activation(neg_sink[:], turned_sink[:, P - 1 : P], ACT.Copy, scale=-1.0)

        turned_scales = []
        for u in range(PAGES):
            token_scales = keep.tile([P, PAGE], F32, name="token_scales%d" % u)
            nc.scalar.activation(token_scales[:], token_scale_pool[:].indirect(slot_list[:, 32 * u : 32 * (u + 1)]), ACT.Copy)
            bank = psum.tile([P, PACK, P], F32, name="turned_scales%d" % u, tag="turned%d" % u)
            for t in range(PACK):
                nc.tensor.transpose(bank[:, t, :], token_scales[:, t:PAGE:PACK], ident[:])
            turned_scales.append(bank)

        q_grouped = [keep.tile([P, NQ, PACK], BF16, name="q_grouped%d" % o, align_bytes=64) for o in range(PASSES)]
        q_codes = [keep.tile([P, NQ], U32, name="q_codes%d" % o, align_bytes=64) for o in range(PASSES)]
        q_scales = [keep.tile([P, NQ], U8, name="q_scales%d" % o, align_bytes=64) for o in range(PASSES)]
        for o in range(PASSES):
            nc.scalar.activation(
                q_grouped[o][:].rearrange("p (c i) j -> p c j i", i=4),
                q_raw[o][:].rearrange("p j (c i) -> p c j i", i=4),
                ACT.Copy,
                scale=-1.0,
            )
        slot_scales = []
        for u in range(PAGES):
            spread = shared.tile([P, PACK], F32, name="slot_scales%d" % u, offset=SLOT_SCALES + 32 * u)
            nc.scalar.activation(spread[:], turned_scales[u][:, :, P - 1], ACT.Copy)
            slot_scales.append(spread)

        key_pairs = []
        keys = {}
        scores = [psum.tile([NQ, PAGE], F32, name="scores%d" % u) for u in range(PAGES)]

        def quantize_queries(o):
            nc.vector.quantize_mx(q_codes[o][:].bitcast(FP8X4), q_scales[o][:], q_grouped[o][:].rearrange("p w j -> p (w j)"))

        def gather_keys(u):
            if u == PAGES - 1:
                pairs = placed([P, PAGE], U32, "key_pairs%d" % u, LAST_PAIRS)
            else:
                pairs = keep.tile([P, PAGE], U32, name="key_pairs%d" % u, align_bytes=64)
            nc.vector.tensor_copy(pairs[:], key_pool[:].bitcast(U32).indirect(slot_list[:, 32 * u : 32 * (u + 1)]))
            key_pairs.append(pairs)

        def part_keys(u, o):
            if (u, o) in HELD_KEYS:
                parted = placed([P, PAGE], U16, "keys%d_%d" % (u, o), HELD_KEYS[(u, o)])
            else:
                parted = keep.tile([P, PAGE], U16, name="keys%d_%d" % (u, o), align_bytes=64)
            nc.vector.tensor_copy(parted[:], key_pairs[u][:].bitcast(U16)[:, o : PASSES * PAGE : PASSES])
            keys[(u, o)] = parted[:]

        def score(u, o):
            nc.tensor.matmul_mx(
                scores[u][:],
                lhsT=q_codes[o][:].bitcast(FP8X4),
                lhsT_scale=q_scales[o][:],
                rhs=keys[(u, o)].bitcast(FP4X4),
                rhs_scale=last_planes[:, o, :] if u == PAGES - 1 else early_planes[:, o, PAGE * u : PAGE * (u + 1)],
                start=(o == 0),
                stop=(o == PASSES - 1),
            )

        gather_keys(0)
        gather_keys(1)
        part_keys(0, 0)
        quantize_queries(0)
        part_keys(1, 0)
        part_keys(0, 1)
        quantize_queries(1)
        gather_keys(2)
        part_keys(1, 1)
        part_keys(2, 0)
        part_keys(2, 1)
        for u, o in ((0, 0), (1, 0), (0, 1), (1, 1), (2, 0), (2, 1)):
            score(u, o)

        dealt = [scores[u][:].rearrange("q (s t) -> q t s", t=PACK) for u in range(PAGES)]
        least = [keep.tile([NQ, 1], F32, name="least%d" % u) for u in range(PAGES)]
        first_scores = keep.tile([NQ, PACK, P], F32, name="first_scores")
        clamped = keep.tile([NQ, PAGE], F32, name="clamped")
        first_value_plane = placed([P, DV], U8, "first_value_plane", HELD_KEYS[(1, 1)])
        later_value_planes = placed([P, (PAGES - 1) * DV], U8, "later_value_planes", HELD_KEYS[(2, 1)])
        nc.vector.tensor_scalar(first_scores[:], dealt[0], 1.0, neg_sink[:], op0=ALU.mult, op1=ALU.min, accum_out=least[0][:])
        nc.vector.tensor_reduce(least[1][:], scores[1][:], axis=AXIS.X, op=ALU.min)
        second_scores = keep.tile([NQ, PACK, P], F32, name="second_scores")
        nc.scalar.activation(second_scores[:], dealt[1], ACT.Copy)
        nc.vector.tensor_copy(first_value_plane[:], value_scale_pool[:].indirect(column_list[:, 0 : DV // 16]))
        nc.vector.tensor_scalar(clamped[:], scores[2][:], least[0][:], least[1][:], op0=ALU.min, op1=ALU.min, accum_out=least[2][:])
        neg_max = least[2]
        neg_scores = [first_scores[:], second_scores[:], dealt[2]]

        nc.vector.tensor_copy(later_value_planes[:], value_scale_pool[:].indirect(column_list[:, DV // 16 : PAGES * DV // 16]))
        value_planes = [first_value_plane[:], later_value_planes[:, 0:DV], later_value_planes[:, DV : 2 * DV]]
        values = keep.tile([P, PAGES * DV], U32, name="values", align_bytes=64)
        nc.vector.tensor_copy(values[:], value_pool[:].bitcast(U32).indirect(column_list[:]))

        pieces = [(0, t, t + 1) for t in range(PACK)] + [(u, t0, t1) for u in range(1, PAGES) for t0, t1 in ((0, 2), (2, 3), (3, 4))]
        terms = keep.tile([NQ, SLOTS + 8], F32, name="terms")
        probs = [terms[:, PAGE * u : PAGE * (u + 1)].rearrange("q (t s) -> q t s", t=PACK) for u in range(PAGES)]
        turned = [psum.tile([P, PACK, NQ], F32, name="turned_probs%d" % u, tag="turned%d" % u) for u in range(PAGES)]
        for u, t0, t1 in pieces:
            nc.scalar.activation(probs[u][:, t0:t1, :], neg_scores[u][:, t0:t1, :], ACT.Exp, bias=neg_max[:], scale=-1.0)
            for t in range(t0, t1):
                nc.tensor.transpose(turned[u][:, t, :], probs[u][:, t, :], ident[:])
        nc.scalar.activation(terms[:, SLOTS : SLOTS + 1], neg_sink[:], ACT.Exp, bias=neg_max[:], scale=-1.0)
        total = keep.tile([NQ, 1], F32, name="total")
        summed = keep.tile([NQ, SLOTS + 1], F32, name="summed")
        nc.scalar.activation(summed[:], terms[:, 0 : SLOTS + 1], ACT.Copy, accum_out=total[:])

        weights = []
        sums = [psum.tile([NQ, HALF], F32, name="sums%d" % h, tag="sums%d" % h) for h in range(2)]

        def weigh(u):
            w_grouped = placed([P, NQ, PACK], BF16, "w_grouped%d" % u, WEIGHTS + W_BYTES * u)
            nc.vector.tensor_tensor(
                w_grouped[:], turned[u][:].rearrange("p t q -> p q t"),
                slot_scales[u][:].unsqueeze(1).to_broadcast([P, NQ, PACK]), ALU.mult,
            )
            weights.append(w_grouped)

        def multiply(u):
            w_codes = keep.tile([P, NQ], U32, name="w_codes%d" % u, align_bytes=64)
            w_scales = keep.tile([P, NQ], U8, name="w_scales%d" % u, align_bytes=64)
            nc.vector.quantize_mx(w_codes[:].bitcast(FP8X4), w_scales[:], weights[u][:].rearrange("p q t -> p (q t)"))
            for h in range(2):
                nc.tensor.matmul_mx(
                    sums[h][:],
                    lhsT=w_codes[:].bitcast(FP8X4),
                    lhsT_scale=w_scales[:],
                    rhs=values[:, DV * u + HALF * h : DV * u + HALF * (h + 1)].bitcast(FP8X4),
                    rhs_scale=value_planes[u][:, HALF * h : HALF * (h + 1)],
                    start=(u == 0),
                    stop=(u == PAGES - 1),
                )

        weigh(0)
        weigh(1)
        multiply(0)
        weigh(2)
        multiply(1)
        multiply(2)
        inverse = placed([NQ, 1], F32, "inverse", WEIGHTS + W_BYTES)
        nc.vector.reciprocal(inverse[:], total[:])

        results = [keep.tile([NQ, HALF], F32, name="result%d" % h, align_bytes=256) for h in range(2)]
        nc.vector.tensor_scalar(results[0][:], sums[0][:], inverse[:], None, op0=ALU.mult)
        nc.scalar.activation(results[1][:], sums[1][:], ACT.Copy, scale=inverse[:])
        nc.sync.dma_start(out[0][:, 0:HALF], results[0][:])
        nc.scalar.dma_start(out[0][:, HALF:DV], results[1][:])
